import numpy as np, ml_dtypes
CORES = [8,136,40,168]
N = 4
BF = ml_dtypes.bfloat16
def gentries(a):
    return np.ascontiguousarray(a.reshape(8, 16, -1).transpose(0, 2, 1)).reshape(8, -1)
def gtable(e):
    e = np.asarray(e); return np.ascontiguousarray(e.reshape(8, -1, 16).transpose(0, 2, 1)).reshape(128, -1).astype(np.int32)
V, B, S, RO = 512, 128, 4, 3
E = V + (N - 1) * B
UM, QM, LAM, H, Z = 1023, 1023, 64, 9, 13
def bars(rng):
    p = np.argsort(rng.random((N, 8, 4, V)), axis=-1); inv = np.argsort(p, axis=-1)
    m = rng.random((N, 8, 4, V)) < 0.4; mi = np.take_along_axis(m, inv, -1)
    L = np.concatenate([p, inv], axis=2); M = np.concatenate([m, mi], axis=2)
    L = np.where(M, np.where(rng.random(L.shape) < 0.5, E, rng.integers(V, E, L.shape)), L)
    return np.take_along_axis(L, np.argsort(rng.random(L.shape), axis=2), 2)
def parts(rng):
    d = {}; size = rng.choice(np.array([224, 288, 352, 448]), (N, 8, 1, 1))
    for k in ("ux", "uy"): d[k] = np.rint((2 * rng.random((N, 8, 16, V)) - 1) * size).astype(np.int64)
    d["ld"] = rng.integers(-2047, 2048, (N, 8, 16, V))
    for k in ("px", "py"): d[k] = rng.integers(0, 8, (N, 8, V))
    d["wt"] = (0.5 + rng.random((N, 8, 16, V))).astype(np.float32)
    d["nb"] = bars(rng); d["bord"] = np.ascontiguousarray(np.argsort(rng.random((N, 8, V)), axis=-1)[..., :B])
    return d
def pack(d):
    out = {}
    for k in ("ux", "uy", "ld"): out[k] = np.ascontiguousarray(d[k].reshape(N, 128, V)).astype(np.int32)
    for k in ("px", "py"): out[k] = np.ascontiguousarray(d[k]).astype(np.int32)
    out["wt"] = np.ascontiguousarray(d["wt"].reshape(N, 128, V)).astype(np.float32)
    out["nb"] = np.stack([gtable(m.reshape(8, 8 * V)) for m in d["nb"]]); out["bord"] = np.stack([gtable(m) for m in d["bord"]])
    return out
def setup_inputs(rng):
    return pack(parts(rng))
def setup_inputs_spread(rng):
    d = parts(rng)
    for k in ("ux", "uy"): d[k] = np.rint((2 * rng.random((N, 8, 16, V)) - 1) * 1023 * np.exp2(-rng.integers(0, 5, (N, 8, 1, V)))).astype(np.int64)
    d["ld"] = np.rint((2 * rng.random((N, 8, 16, V)) - 1) * 2047 * np.exp2(-rng.integers(0, 6, (N, 8, 1, V)))).astype(np.int64)
    d["wt"] = (d["wt"] * np.exp2(rng.integers(-1, 2, (N, 8, 1, V)))).astype(np.float32)
    return pack(d)
def setup_inputs_ends(rng):
    d = parts(rng)
    h = rng.random(d["wt"].shape)
    d["wt"] = np.where(h < 0.4, 4.0, np.where(h < 0.8, 0.25, d["wt"])).astype(np.float32)
    for k, m in (("ux", 1023), ("uy", 1023), ("ld", 2047)):
        x = 2 * rng.integers(0, 2, (N, 8, 16, V)) - 1
        x = np.where(rng.random((N, 8, 1, V)) < 0.6, x[:, :, :1], x)
        one = (np.arange(16)[:, None] == rng.integers(0, 16, (N, 8, 1, V))) & (rng.random((N, 8, 1, V)) < 0.3)
        d[k] = m * np.where(one, -x, x)
    for k in ("px", "py"): d[k] = 7 * rng.integers(0, 2, (N, 8, V))
    h = rng.random((N, 8, 3, V)); x = rng.integers(0, V, (N, 8, 3, V))
    x = np.where(h < 0.15, V - 1, np.where(h > 0.95, E - 1, np.where(h > 0.8, rng.integers(V, E, x.shape), x)))
    L = np.concatenate([np.full((N, 8, 2, V), E), np.zeros((N, 8, 3, V), np.int64), x], axis=2)
    L = np.take_along_axis(L, np.argsort(rng.random(L.shape), axis=2), 2); d["nb"] = L
    d["bord"] = np.where(rng.random((N, 8, B)) < 0.66, (V - 1) * rng.integers(0, 2, (N, 8, B)), d["bord"])
    for r in range(N):
        for g in range(8):
            o = 1 + rng.permutation(V // S - 3)
            for s, v in ((1, V - 1), (-1, V - 1 - S)):
                i, o = o[:12], o[12:]
                c = i[:6] * S + np.arange(6) % (S - 1); n = i[6:] * S + np.arange(6) % (S - 1); far = np.concatenate([n, c])
                for k in ("px", "py"): d[k][r, g, far] = 0; d[k][r, g, v] = 7; d[k][r, g, v - 1] = 7
                for k in ("ux", "uy"):
                    w = d[k][r, g]; w[:, far] = -1023 * s; w[:, v] = 1023 * s; w[:, v - 1] = 1023 * s
                L[r, g, :2, v] = E; L[r, g, 2:, v] = n; L[r, g, :, v - 1] = far[:8]
                for j in range(6): L[r, g, 2 + j, n[j]] = c[j]
    return pack(d)
def setup_inputs_corners(rng):
    d = parts(rng); L = d["nb"]; c = rng.choice(7, (N, 8, 1, V), p=[0.4, 0.1, 0.2, 0.1, 0.1, 0.05, 0.05])
    own = rng.integers(0, V, L.shape); gh = rng.integers(V, E, L.shape); slot = np.arange(8)[:, None]
    L = np.where(c == 1, E, np.where(c == 2, own, L)); L = np.where(c == 3, np.where(slot == (own[:, :, :1] & 7), E, gh), L)
    L = np.where(c == 4, np.where(slot == 7, E, own[:, :, :1]), np.where(c == 5, np.where(slot == 7, own, E), L))
    x = rng.choice(np.array([0, V - 1, V, E - 1, -1]), L.shape)
    d["nb"] = np.where(c == 6, np.where(x < 0, np.arange(V), x), L)
    for r in range(N):
        o = rng.permutation(np.array([4, 6, 7])); lo = V + B * int(rng.integers(0, N - 1))
        d["nb"][r, int(o[0])] = rng.integers(lo, lo + B, (8, V)); d["nb"][r, int(o[1])] = rng.integers(0, V, (8, V))
    for g, m in ((0, 3), (1, 4), (2, 8), (3, 9)):
        o = rng.permutation(16); on = (1 + (o < m).astype(np.int64)) * (1 - 2 * (o & 1)); some = rng.random((N, 1, V)) < 0.8
        for k, p in (("ux", "px"), ("uy", "py")): d[k][:, g] = np.where(some, 64 * d[p][:, g][:, None, :] * on[:, None], d[k][:, g])
    d["px"][:, 5] = 3 + (d["px"][:, 5] & 1); d["py"][:, 5] = 4
    d["ux"][:, 5] = 543 * (2 * (d["px"][:, 5] - 3) - 1)[:, None, :] + rng.integers(0, 2, (N, 16, V))
    return pack(d)
def setup_inputs_crowd(rng):
    d = parts(rng)
    for r in range(N):
        for g in (0, 2, 4, 6):
            i = 1 + rng.permutation(V // S - 1)[:2]; h, c = int(i[0]) * S, int(i[1]) * S
            sc = np.full(16, 128)
            if g == 6: sc[15] = 64
            for k, p in (("ux", "px"), ("uy", "py")):
                d[p][r, g] = np.maximum(d[p][r, g], 1); d[p][r, g, c] = 0; d[k][r, g] = sc[:, None] * d[p][r, g]
            L = d["nb"][r, g]; L[L == c] = h; L[0] = h; L[5] = E
            if g == 2:
                x = L[:, :S]; x[x == E] = h
            if g == 4: L[0, :S * int(rng.integers(2, V // S - 2))] = E
            L[:, h] = c; L[:, c] = E
        i = S * np.arange(V // S); o = rng.permutation(S - 1)[:2]
        c = rng.permutation(i + int(o[0])); n = rng.permutation(i + int(o[1])); v = i + S - 1; s = rng.integers(0, 8, V // S)
        for k, p in (("ux", "px"), ("uy", "py")):
            d[p][r, 7] = np.maximum(d[p][r, 7], 1); d[p][r, 7, c] = 0; d[k][r, 7] = 128 * d[p][r, 7]
        L = d["nb"][r, 7]; L[:, v] = E; L[s, v] = n; L[s, n] = c; L[(s + 1) % 8, c] = E
        o = rng.permutation(S - 1)[:3]; a = i + int(o[0]); b = i + int(o[1]); other = i + int(o[2])
        for k, p in (("ux", "px"), ("uy", "py")):
            d[p][r, 5] = np.maximum(d[p][r, 5], 1); d[p][r, 5, b] = 0
            w = 64 * d[p][r, 5]; w[b] = -64; d[k][r, 5] = w
        n = rng.permutation(a); c = rng.permutation(b); L = d["nb"][r, 5]
        L[:, v] = rng.choice(a, (8, V // S)); L[7, v] = n
        if r % 2 == 0: L[0, v] = E
        else: L[0, v[-4:]] = E
        L[:7, a] = rng.choice(other, (7, V // S)); L[7, n] = c; L[0, b] = E
        x = rng.permutation(i); h = V // S // 2; za = x[:h]; zb = x[h:]
        n = np.concatenate([za, zb]); c = np.concatenate([rng.permutation(zb), rng.permutation(za)]); j = rng.integers(0, 8, V // S)
        act = np.concatenate([i + S - 1 - t for t in range(RO)]); sg = 1 - 2 * (rng.permutation(16) & 1)[:, None]
        for k, p, top, pa, pb, ua, ub in (("ux", "px", 3, 5, 5, 322, 321), ("uy", "py", 4, 3, 4, 189, 255)):
            at = int(rng.integers(0, top)); off = rng.integers(-300, 301, (16, 1))
            d[p][r, 3, act] = at; d[p][r, 3, za] = at + pa; d[p][r, 3, zb] = at + pb
            w = d[k][r, 3]; w[:, act] = off; w[:, za] = off + ua * sg; w[:, zb] = off + ub * sg
        w = d["ld"][r, 3]; w[:, act] = 0; w[:, za] = 0; w[:, zb] = 8 * sg
        L = d["nb"][r, 3]; L[:, i] = E; L[:, act] = E; L[j, n] = c
        for t in range(RO):
            x = rng.permutation(V // S); L[(j[x] - t) % 8, i + S - 1 - t] = n[x]
    return pack(d)
def setup_inputs_calm(rng):
    d = parts(rng)
    for g in (1, 4, 6):
        pj = rng.choice(np.array([0.0, 0.1, 0.5, 0.9]), (N, 1, V))
        for k, p in (("ux", "px"), ("uy", "py")):
            d[k][:, g] = 64 * d[p][:, g][:, None, :] + (rng.random((N, 16, V)) < pj) * rng.integers(1, 4, (N, 16, V))
        d["ld"][:, g] = rng.integers(-16, 16, (N, 16, V))
    r = int(rng.integers(0, N)); d["nb"][r, 6] = E; d["ld"][r, 6] = rng.integers(-2047, 2048, (16, V))
    d["wt"] = (d["wt"] * 0.5).astype(np.float32)
    return pack(d)
def check_ranges(d):
    bad = []
    for k, lo, hi in (("ux", -1023, 1023), ("uy", -1023, 1023), ("ld", -2047, 2047), ("px", 0, 7), ("py", 0, 7), ("nb", 0, E), ("bord", 0, V - 1)):
        if np.min(d[k]) < lo or np.max(d[k]) > hi: bad.append("range of " + k)
    w = np.asarray(d["wt"], np.float64)
    if not np.all((w >= 0.25) & (w <= 4)): bad.append("range of wt")
    return bad
def ext(s, bd):
    out = []
    for r in range(N):
        w = [s[r]]
        for d in range(1, N):
            o = (r - d) % N; w.append(np.take_along_axis(s[o], bd[o][:, None, :], 2))
        w.append(np.zeros(s[r].shape[:2] + (1,), s.dtype)); out.append(np.concatenate(w, axis=2))
    return out
def reference(ux, uy, ld, px, py, wt, nb, bord):
    take = np.take_along_axis
    x = ux.astype(np.int32).reshape(N, 8, 16, V); y = uy.astype(np.int32).reshape(N, 8, 16, V); f = ld.astype(np.int32).reshape(N, 8, 16, V)
    P = px.astype(np.int32); Q = py.astype(np.int32)
    L = np.stack([gentries(m) for m in nb]).astype(np.int64).reshape(N, 8, 8, V); bd = np.stack([gentries(m) for m in bord]).astype(np.int64)
    PX = ext(P[:, :, None], bd); PY = ext(Q[:, :, None], bd); WT = ext(wt.astype(np.float64).reshape(N, 8, 16, V), bd)
    q = np.zeros((N, 8, 8, 16, V), np.int32); w = np.zeros((N, 8, 16, V), np.float64)
    for t in range(RO):
        rho = S - 1 - t; U = np.array(L[:, :, :, rho::S])
        own = U < V; near = np.where(own, U, 0)
        c = np.stack([take(L[:, :, (k + t) % 8], near[:, :, k], 2) for k in range(8)], axis=2)
        ok = own & (c < V) & (c % S != rho)
        for j in range(8): ok = ok & (c != U[:, :, j:j + 1])
        c = np.where(ok, c, 0); sc = []
        for k in range(8):
            i = c[:, :, k]; i4 = i[:, :, None]
            dx = (take(P, i, 2) - P[:, :, rho::S])[:, :, None]; dy = (take(Q, i, 2) - Q[:, :, rho::S])[:, :, None]
            e = (take(x, i4, 3) - x[..., rho::S]) * dx + (take(y, i4, 3) - y[..., rho::S]) * dy
            sc.append(np.sum(np.abs(e) > LAM * (dx * dx + dy * dy), axis=2))
        sc = np.where(ok, np.stack(sc, axis=2), 0); best = np.argmax(sc, axis=2)
        named = take(c, best[:, :, None], 2)[:, :, 0]; does = (np.max(sc, axis=2) >= H) & np.any(U == E, axis=2)
        for r in range(N):
            for g in range(8):
                i = np.flatnonzero(does[r, g])
                if i.size == 0: continue
                M = L[r, g]; u, j = np.unique(named[r, g, i], return_index=True); v = rho + S * i[j]
                m = np.any(M[:, u] == E, axis=0); u, v = u[m], v[m]
                if u.size == 0: continue
                su = np.argmax(M[:, u] == E, axis=0); sv = np.argmax(M[:, v] == E, axis=0)
                M[su, u] = v; M[sv, v] = u
        X = ext(x, bd); Y = ext(y, bd); nx = []; ny = []
        for r in range(N):
            sx = np.zeros((8, 16, V), np.int32); sy = np.zeros((8, 16, V), np.int32)
            for k in range(8):
                ix = np.array(L[r, :, k]); i3 = ix[:, None, :]; full = i3 < E
                dx = np.where(full, take(PX[r], i3, 2) - P[r][:, None], 0); dy = np.where(full, take(PY[r], i3, 2) - Q[r][:, None], 0)
                e = (take(X[r], i3, 2) - x[r]) * dx + (take(Y[r], i3, 2) - y[r]) * dy
                T = LAM * (dx * dx + dy * dy); z = q[r, :, k] + e
                z = np.clip(z - np.clip(z, -T, T), -QM, QM)
                stay = np.sum(z == 0, axis=1) < Z
                z = np.where(stay[:, None], z, 0); L[r, :, k] = np.where(stay, ix, E); q[r, :, k] = z
                sx = sx + z * dx; sy = sy + z * dy; w[r] = w[r] + np.abs(z) * take(WT[r], i3, 2)
            nx.append(np.clip(x[r] + ((sx + 16) >> 5), -UM, UM)); ny.append(np.clip(y[r] + ((sy + f[r] + 16) >> 5), -UM, UM))
        x = np.stack(nx); y = np.stack(ny)
    return {"yx": x.reshape(N, 128, V).astype(np.float32), "yy": y.reshape(N, 128, V).astype(np.float32), "yw": w.reshape(N, 128, V).astype(np.float32)}

def check_inputs(d):
    bad = list(check_ranges(d))
    if not bad:
        for name, y in reference(**d).items():
            for q in range(N):
                v = np.abs(np.asarray(y[q], np.float64)); s = np.sqrt(np.mean(v * v))
                if v.max() > 12 * s or s < 2.0 ** 5: bad.append('%s of rank %d is uneven or too small' % (name, q))
    return bad

@@ -1,0 +1,819 @@
+import numpy as np
+from concourse.bass import DstId, RemoteDMATransfer
+from concourse.mybir import AluOpType as A, ActivationFunctionType as F
+
+f32, f16, b16, i32, u16 = "float32", "float16", "bfloat16", "int32", "uint16"
+ZWID = 776
+ZC = 648
+BIG = 65536.0
+_B = {
+    "XW": (904, f32), "YW": (904, f32), "PW": (904, f32), "WW": (904, f32), "x16": (512, f16), "y16": (512, f16),
+    "ld16": (512, f16), "PV": (512, b16), "DX": (4096, b16), "DY": (4096, b16), "MQ": (8192, f16), "Q16": (4096, f16),
+    "gx": (1024, f16), "gy": (1024, f16), "bb": (1024, f32), "ab": (1024, f32), "xacc": (1024, f32),
+    "pw": (1536, f32), "ppx": (1536, f32), "ppy": (1536, f32), "sg": (2048, b16), "r16": (1536, f16), "nz": (1024, b16),
+    "AS": (2048, b16), "FF": (1536, b16), "LT": (ZWID, f32),
+    "ZZ": (9 * ZC, f32), "UXI": (512, i32), "UYI": (512, i32), "PI": (512, i32), "NBI": (256, i32),
+    "BDI": (8, i32), "Lo": (256, u16), "bo": (8, u16), "wacc": (1024, f32), "yacc": (1024, f32),
+    "SXY": (768, f16), "LXY": (2304, f16), "SP": (128, f32), "SW": (128, f32),
+    "ef": (512, b16), "FEW": (1024, b16), "HEW": (512, b16), "U16": (128, f16), "Um": (1024, f16), "O1": (64, u16),
+    "O2": (64, u16), "EQ": (1280, b16), "Gp1": (1024, b16), "cgx": (512, f16), "cgy": (512, f16),
+    "CDX": (1024, b16), "CDY": (1024, b16), "sqs": (512, b16), "cb": (512, f32), "cab": (512, f32), "csg": (1024, b16),
+    "K0": (512, f32), "K2": (256, f32), "best": (128, f32), "BI": (128, i32), "c16": (128, f16),
+    "dd": (128, f32), "t1": (128, f32), "t2": (128, f32), "t3": (256, f32), "t4": (128, f32), "C16": (128, f16),
+    "Cn": (128, f16), "OC": (24, u16), "O4": (48, u16), "o4f": (16, f32), "FEc": (256, b16),
+    "NCOL": (256, f32), "Z4": (128, f16), "R2": (256, f16), "AL": (384, b16), "DD": (384, b16), "EP": (128, b16),
+    "ED": (768, f32), "EN": (768, f32), "ES": (768, b16), "EWC": (384, f32), "EQq": (384, f32), "EM": (256, f32), "eg": (256, f16),
+    "EA": (256, f32), "EZ": (128, f32), "esg": (128, b16), "eab": (128, f32), "em": (128, f32), "enz": (128, b16),
+    "ci": (4, i32), "cj": (4, i32), "col": (16, f32), "RM": (17, f32), "RC": (40, f32),
+    "MD": (1280, b16), "KC": (1024, b16),
+    "PG": (1024, b16), "IDS": (128 * 8, b16), "I32": (128, f32), "GSB": (144, b16), "BO": (128 * 3, b16),
+    "TS": (1024, b16), "SEL": (128 * 7, b16), "SB": (2048, f16), "EE": (2048, b16), "TRI": (128, b16), "B2": (136, b16),
+    "nPV": (128, b16), "TRc": (128, b16), "CM": (240, b16), "SH": (320, b16), "MM": (128, b16), "VJ": (384, f32),
+    "ZV": (384, f16), "DJ": (128, f32), "K16": (16, f32),
+}
+ALIAS = {"wout": ("K0", 0, 512), "Zp": ("Um", 0, 512), "Zt": ("Um", 512, 512), "LDI": ("UXI", 0, 512), "G1": ("Um", 0, 1024),
+         "K1": ("cab", 0, 512), "tb": ("EQ", 0, 1280), "eq2": ("EQ", 0, 1024), "IX": ("cb", 0, 256),
+         "IG": ("cb", 256, 128), "PR": ("cb", 384, 128), "H8": ("K0", 0, 128), "tq": ("csg", 0, 256)}
+PLACE = {}
+SCRATCH = {}
+for _k, (_w, _d) in _B.items():
+    if _w > 400:
+        PLACE[_k] = (_k, 0)
+        SCRATCH[_k] = ("sbuf", [128, _w], _d)
+    else:
+        _o = SCRATCH.get("pool_" + _d, (0, [128, 0]))[1][1]
+        PLACE[_k] = ("pool_" + _d, _o)
+        SCRATCH["pool_" + _d] = ("sbuf", [128, _o + (_w + 15) // 16 * 16], _d)
+for _i in range(8):
+    SCRATCH["P%d" % _i] = ("psum", [128, 512], f32)
+NDMA = 90
+SEMAPHORES = ["qt", "qv", "qa", "qg", "ls", "aP", "aW", "a0", "a1", "a2"] + ["d%d" % _i for _i in range(NDMA)]
+SZ = {f32: 4, f16: 2, b16: 2, i32: 4, u16: 2}
+CY = 0.83e-3 * 1.15
+HOP = 0.12
+TUNE = {'s1': (-10, 1.1), 'per': 1.31, 'cs': 0.1, 'ex': 10.0, 'exn': 15.5, 'cv': (4, 5, 6, 9, 10, 13, 16, 17, 19, 21, 23, 26, 29, 30, 33, 35, 37, 44, 45, 50, 51, 52, 53, 59, 64, 69, 70, 74, 76, 77, 78, 82, 84, 86, 89, 93, 101, 102, 117, 118, 120, 123, 126, 128, 132, 134, 135, 139, 145, 151, 156), 'dsum': (6, 7), 'mq': 22.1, 'win': 0, 'um': (0, 8, 4), 'mina': (4, 6, 7, 8, 9, 12, 14), 'nzv': (0, 15, 16, 17, 18, 19), 'tries': 200}
+DLAT = 2.6
+
+
+def S(name, a=0, b=None, step=1, p=None):
+    if name in ALIAS:
+        real, o, w = ALIAS[name]
+        return ("ap", real, o + a, o + (w if b is None else b), step, p)
+    if b is None:
+        b = _B[name][0] if name in _B else 512
+    return ("ap", name, a, b, step, p)
+
+
+def IND(win, off):
+    return ("ind", win, off)
+
+
+def is_ap(x):
+    return isinstance(x, tuple) and x[0] in ("ap", "ind")
+
+
+def width(x):
+    if x[0] == "ind":
+        return 16 * (x[2][3] - x[2][2])
+    return len(range(x[2], x[3], x[4]))
+
+
+def psum(x):
+    return x[0] == "ap" and x[1][0] == "@"
+
+
+def size(x):
+    return 4 if psum(x) else SZ[_B[x[1]][1]]
+
+
+def build():
+    ops = []
+    nb = [2]
+    nd = [0]
+    nc = [0]
+    grp = [(0.0, 1.0)]
+
+    def bank():
+        nb[0] += 1
+        return "@%d" % nb[0]
+
+    def add(eng, kind, args, rd, wr, cost, lat=0.0, after=(), kw=None):
+        r, w = [], []
+        for x in rd:
+            if x[0] == "ind":
+                r += [x[1], x[2]]
+            else:
+                r.append(x)
+        for x in wr:
+            if x[0] == "ind":
+                w.append(x[1])
+                r.append(x[2])
+            else:
+                w.append(x)
+        ops.append(dict(grp=grp[0], eng=eng, kind=kind, args=args, rd=r, wr=w, cost=cost, lat=lat, after=list(after), kw=kw or {}))
+        return len(ops) - 1
+
+    def vcost(out, ins, two):
+        n = width(ins[0]) if ins else width(out)
+        if out[0] == "ind":
+            return 0.05 + 3.8 * n * CY
+        if ins and ins[0][0] == "ind":
+            return 0.05 + 1.56 * n * CY
+        if two:
+            c = 1 if any(psum(x) for x in ins) else 2
+        else:
+            c = 0.5 if all(size(x) == 2 for x in [out] + ins) else 1
+        return 0.05 + max(64, n * c) * CY
+
+    def tt(out, a, b, op):
+        return add("v", "tensor_tensor", (out, a, b, op), [a, b], [out], vcost(out, [a, b], True))
+
+    def ts(out, a, s1, op0, s2=None, op1=None):
+        args = (out, a, s1, s2, op0) if op1 is None else (out, a, s1, s2, op0, op1)
+        return add("v", "tensor_scalar", args, [a] + [s for s in (s1, s2) if is_ap(s)], [out], vcost(out, [a], False))
+
+    def cp(out, a):
+        return add("v", "tensor_copy", (out, a), [a], [out], vcost(out, [a], False))
+
+    def ms(out, c):
+        return add("v", "memset", (out, c), [], [out], vcost(out, [], False))
+
+    def act(out, a, fn, bias=None, scale=None):
+        kw = {}
+        if fn == F.Copy and scale is None:
+            nc[0] += 1
+            if nc[0] in TUNE["cv"]:
+                return cp(out, a)
+        if bias is not None:
+            kw["bias"] = bias
+        if scale is not None:
+            kw["scale"] = scale
+        c = 0.07 + max(64, width(a) * (1.56 if a[0] == "ind" else 1)) * CY
+        return add("a", "activation", (out, a, fn), [a] + ([scale] if is_ap(scale) else []), [out], c, kw=kw)
+
+    def iota(out, pat, base, cm=0):
+        kw = {} if _B[out[1]][1] == i32 else {"allow_small_or_imprecise_dtypes": True}
+        return add("g", "iota", (out, pat, base, cm), [], [out], 0.13 + 2 * width(out) * CY, kw=kw)
+
+    def mm(groups, after=(), start=True, stop=True):
+        rd, wr, c = [], [], 0.03
+        for out, terms in groups:
+            wr.append(out)
+            for l, r in terms:
+                rd += [l, r]
+                c += max(64, width(r)) * (4 if size(r) == 4 else 1) * CY / 2
+        return add("t", "mm", (groups, start, stop), rd, wr, c, after=after)
+
+    def dma(eng, out, a, acc=False, lat=2.2):
+        rd = [x for x in (a,) if is_ap(x)] + ([out] if acc else [])
+        nd[0] += 1
+        return add(eng, "dma", (out, a, acc, "d%d" % (nd[0] - 1)), rd, [x for x in (out,) if is_ap(x)],
+                   1.0 if eng == "g" else 0.1, lat=lat)
+
+    def send(parts):
+        i = add("g", "send", (parts,), [p[0] for p in parts], [], 1.0)
+        for src, nm, a, w, sem in parts:
+            add("r", "recv", (sem, len(parts)), [], [S(nm, a, a + 3 * w)], 0.0, lat=4.5, after=[i])
+
+    def blk(name, k, w=128):
+        return S(name, k * w, (k + 1) * w)
+
+    def c1(name, k):
+        return S(name, k, k + 1)
+
+    dma("s", S("BDI"), "bord")
+    ms(S("PI"), 0)
+    dma("s", S("PI", p=(0, 128, 16)), "px")
+    dma("a", S("PI", p=(8, 128, 16)), "py")
+    dma("s", S("UXI"), "ux")
+    dma("a", S("UYI"), "uy")
+    dma("s", S("NBI"), "nb")
+    dma("a", S("WW", 0, 512), "wt")
+    iota(S("ci"), [[0, 4]], 0, 1)
+    iota(S("IX"), [[1, 256]], 0)
+    iota(S("tb", 0, 512), [[0, 128], [1, 4]], 0)
+    ts(c1("cj", 0), c1("ci", 0), 15, A.bitwise_and)
+    ts(c1("cj", 1), c1("ci", 0), 112, A.bitwise_and)
+    ts(c1("cj", 2), c1("ci", 0), 16, A.bitwise_and)
+    ts(c1("cj", 3), c1("ci", 0), 127, A.bitwise_and)
+    cp(S("col", 0, 4), S("cj"))
+    rcol, gcol, bcol, pcol = (c1("col", k) for k in range(4))
+    ts(c1("col", 4), rcol, -1.0, A.mult, 4.0, A.add)
+    ts(S("tb", 512, 1024), S("tb", 0, 512), c1("col", 4), A.is_equal)
+    tt(S("PW", 0, 512), S("tb", 512, 1024), S("PI"), A.add)
+    cp(S("bo"), S("BDI"))
+    cp(S("SP"), IND(S("PW", 0, 512), S("bo")))
+    send([(S("SP"), "PW", 512, 128, "aP")])
+    cp(S("XW", 0, 512), S("UXI"))
+    cp(S("YW", 0, 512), S("UYI"))
+    act(S("SW"), IND(S("WW", 0, 512), S("bo")), F.Copy)
+
+    def border(t, extra):
+        act(S("SXY", 256 * t, 256 * t + 128), IND(S("XW", 0, 512), S("bo")), F.Copy)
+        cp(S("SXY", 256 * t + 128, 256 * t + 256), IND(S("YW", 0, 512), S("bo")))
+        send([(blk("SXY", t, 256), "LXY", 768 * t, 256, "a%d" % t)] + extra)
+        for d in range(3):
+            o = 768 * t + 256 * d
+            act(S("XW", 512 + 128 * d, 640 + 128 * d), S("LXY", o, o + 128), F.Copy)
+            act(S("YW", 512 + 128 * d, 640 + 128 * d), S("LXY", o + 128, o + 256), F.Copy)
+    border(0, [(S("SW"), "WW", 512, 128, "aW")])
+    act(S("x16"), S("XW", 0, 512), F.Copy)
+    act(S("y16"), S("YW", 0, 512), F.Copy)
+    act(S("PV"), S("PW", 0, 512), F.Copy)
+    dma("s", S("LDI"), "ld")
+    cp(S("ld16"), S("LDI"))
+    cp(S("Lo"), S("NBI"))
+    for nm in ("XW", "YW", "PW", "WW"):
+        ms(S(nm, 896, 904), 0.0)
+    iota(S("IG"), [[16, 8], [0, 16]], 0)
+    iota(S("PR"), [[0, 8], [1, 16]], 0)
+    iota(S("H8"), [[8, 16], [0, 8]], 0)
+    IX = S("IX", 0, 128)
+    ts(S("RM", 0, 16), S("IX", 0, 16), rcol, A.is_equal)
+    ts(c1("RM", 16), rcol, 0.0, A.is_equal)
+    tt(S("RC", 0, 8), S("RM", 0, 8), S("RM", 8, 16), A.add)
+    tt(S("RC", 8, 24), S("RM", 0, 16), S("RM", 1, 17), A.subtract)
+    tt(S("RC", 24, 40), S("RM", 0, 16), S("RM", 1, 17), A.add)
+    ts(c1("col", 5), rcol, 8.0, A.is_ge)
+    ts(c1("col", 6), rcol, 8.0, A.is_lt, 8.0, A.mult)
+    tt(c1("col", 7), c1("col", 6), pcol, A.add)
+    ts(c1("col", 8), gcol, 15.0, A.add)
+    ts(c1("col", 9), pcol, 7.0, A.add)
+    ts(c1("col", 10), pcol, 16.0, A.add)
+    ts(c1("col", 11), c1("RM", 8), -999488.0, A.mult, 1000000.0, A.add)
+    ts(c1("col", 12), c1("col", 5), -5000.0, A.mult)
+    ts(c1("col", 13), c1("RM", 8), 5512.0, A.mult, c1("col", 12), A.add)
+    ts(c1("col", 14), bcol, 0.0, A.is_equal)
+    ts(c1("col", 15), bcol, 16.0, A.is_equal)
+    I, NI, I32x, IBn, I896, N896, IH, I2 = (blk("IDS", k) for k in range(8))
+    for m, c in ((I, 1.0), (NI, -1.0), (I32x, 32.0), (IBn, -BIG), (I896, 896.0), (N896, -896.0), (IH, c1("col", 5)),
+                 (I2, c1("col", 6))):
+        ts(m, IX, pcol, A.is_equal, c, A.mult)
+    I32 = S("I32")
+    ts(I32, IX, pcol, A.is_equal)
+    ts(S("GSB"), S("IX", 0, 144), c1("col", 8), A.is_equal)
+    GS = [S("GSB", 15 - r, 143 - r) for r in range(16)]
+    BO, BO4, BOn = (blk("BO", k) for k in range(3))
+    for m, c in ((BO, 1.0), (BO4, 4096.0), (BOn, -BIG)):
+        ts(m, S("IG"), gcol, A.is_equal, c, A.mult)
+    TS = [blk("TS", k) for k in range(8)]
+    SEL = [blk("SEL", k) for k in range(7)]
+    for k, (r, c) in enumerate(((0, 1.0), (0, -1.0), (8, 1.0), (8, -1.0), (1, -BIG), (2, -BIG), (3, -BIG))):
+        ts(SEL[k], BO, c1("RM", r), A.mult, c, A.mult)
+    ts(S("RC", 8, 24), S("RC", 8, 24), 511.5, A.mult)
+    ts(S("RC", 24, 40), S("RC", 24, 40), -0.5, A.mult)
+    for k in range(8):
+        act(TS[k], BOn, F.Copy, scale=c1("RC", k))
+    for r in range(16):
+        act(blk("SB", r), BO, F.Copy, scale=c1("RC", 8 + r))
+        act(blk("EE", r), GS[r % 8], F.Copy, scale=c1("RC", 24 + r))
+    ts(blk("tq", 0), S("PR"), rcol, A.is_ge, 4.0, A.mult)
+    ts(blk("tq", 1), S("PR"), 8.0, A.is_lt)
+    tt(blk("tq", 0), blk("tq", 0), BO, A.mult)
+    tt(blk("tq", 0), blk("tq", 0), blk("tq", 1), A.mult)
+    tt(S("TRI"), I2, blk("tq", 0), A.subtract)
+    ts(S("B2"), S("IX", 0, 136), c1("col", 9), A.is_equal, c1("RC", 0), A.mult)
+    B2 = [S("B2", 7 - k, 135 - k) for k in range(8)]
+    ts(S("nPV"), S("H8"), pcol, A.is_equal, -1.0, A.mult)
+    ts(S("TRc"), IX, pcol, A.is_le, 4096.0, A.mult)
+    ms(S("CM"), 0.0)
+    ms(S("CM", 112, 128), -1.0)
+    for b in range(2):
+        ts(blk("SH", b, 160), S("IX", 0, 160), c1("col", 10), A.is_equal, c1("col", 14 + b), A.mult)
+    ts(S("MM"), IX, c1("col", 7), A.is_equal)
+    for t in range(3):
+        ts(blk("VJ", t), IX, 4.0, A.mult, 3.0 - t - 896.0, A.add)
+        ts(blk("ZV", t), IX, 3.0, A.mult, 3.0 - t - 648.0, A.add)
+    ts(S("DJ"), IX, 520.0, A.add)
+    ts(S("o4f"), S("IX", 0, 16), 16.0, A.mult, rcol, A.add)
+    ts(S("K16", 0, 8), S("o4f", 0, 8), 648.0, A.add, 16.0, A.mult)
+    ts(S("K16", 8, 16), S("o4f", 0, 8), 520.0, A.add, 16.0, A.mult)
+    iota(S("tb", 0, 1024), [[1, 8], [0, 128]], 0)
+    iota(S("tb", 1024, 1280), [[1, 2], [0, 128]], 0)
+    ts(S("MD"), S("tb"), rcol, A.is_equal)
+    iota(S("KC"), [[-512, 8], [0, 128]], 3584 - 8192)
+    iota(S("tb", 0, 1024), [[16, 8], [0, 128]], 0)
+    ts(S("PG"), S("tb", 0, 1024), pcol, A.is_equal)
+    ms(S("Zp"), 0.0)
+    ms(S("LT", 512, ZWID), 896.0)
+    for k in range(8):
+        cp(S("Zp", k, 512, 16), blk("NBI", k, 32))
+    add("v", "transpose", (S("Zt"), S("Zp")), [S("Zp")], [S("Zt")], 0.05 + 256 * CY)
+    bk = bank()
+    mm([(S(bk, 32 * j + 16 * b, 32 * j + 16 * b + 16),
+         [(S("SH", 160 * b + 16 - 16 * (gp - b), 160 * b + 144 - 16 * (gp - b)), S("Zt", 32 * j + 16 * gp, 32 * j + 16 * gp + 16))
+          for gp in range(2)]) for j in range(16) for b in range(2)])
+    act(S("LT", 0, 512), S(bk), F.Copy)
+    for k in range(8):
+        o = blk("Lo", k, 32)
+        act(blk("Q16", k, 512), IND(S("PW"), o), F.Copy)
+    bk = bank()
+    mm([(S(bk), [(B2[k], blk("Q16", k, 512)) for k in range(8)] + [(S("nPV"), S("PV"))])])
+    act(S("sqs"), S(bk), F.Square, scale=1.0 / 32)
+    ts(S("ef"), S("LT", 0, 512), 896.0, A.is_equal)
+    bk = bank()
+    mm([(S(bk), [(I, S("ef")), (S("MM"), S("sqs"))])])
+    act(blk("FF", 0, 512), S(bk), F.Copy)
+
+    wn = [0]
+    last_w = []
+
+    def wsum(src, direct):
+        if direct:
+            last_w.append(src)
+        else:
+            dma("g", blk("wacc", wn[0] % 2, 512), src, acc=True, lat=DLAT)
+            wn[0] += 1
+
+    def compact(dst_w, src, n):
+        bk = bank()
+        mm([(S(bk, 0, dst_w), [(GS[r], S(src, r, n, 16)) for r in range(16)])])
+        return S(bk, 0, dst_w)
+
+    def step1(t):
+        rho = 3 - t
+        if t:
+            act(S("ef"), S("LT", 0, 512), F.Relu, bias=-895.0)
+        act_ = lambda nm, o=0: S(nm, o + rho, o + 512, 4)
+        fo = 512 * (t % 2)
+        if t < 2:
+            bk = bank()
+            mm([(S(bk), [(S("TRI"), S("ef"))])])
+            act(S("FEW", fo, fo + 512), S(bk), F.Relu, scale=0.25)
+        bk = bank()
+        mm([(S(bk), [(BO, S("ef"))])])
+        act(S("HEW"), S(bk), F.Identity, bias=-1.0)
+        ts(S("U16"), act_("LT"), 512.0, A.min)
+        for k in range(8):
+            if k < TUNE["um"][t]:
+                act(blk("Um", k), S("U16"), F.Copy, scale=c1("RM", k))
+            else:
+                ts(blk("Um", k), S("U16"), c1("RM", k), A.mult)
+        cp(S("O1"), compact(64, "Um", 1024))
+        tt(S("G1"), IND(S("LT", 0, 520), S("O1")), S("MD", 128 * t, 128 * t + 1024), A.mult)
+        ts(S("O2"), compact(64, "G1", 1024), 511.0, A.min)
+        act(S("Gp1"), IND(S("PW", 0, 512), S("O2")), F.Copy)
+        bk = bank()
+        mm([(S(bk, 0, 128), [(B2[k], blk("Gp1", k)) for k in range(8)] + [(S("nPV"), act_("PV"))])])
+        act(S("sqs", 0, 128), S(bk, 0, 128), F.Square, scale=1.0 / 32)
+        reg = lambda bk, k: S(bk, 128 * (k % 4), 128 * (k % 4) + 128)
+        prev = []
+        for h in range(2):
+            ks = range(4 * h, 4 * h + 4)
+            H = lambda nm: blk(nm, h, 512)
+            bk = bank()
+            mm([(reg(bk, k), [(BO, blk("G1", k)), (NI, S("U16"))]) for k in ks])
+            ts(H("EQ"), S(bk), c1("col", 11), A.min, c1("col", 13), A.is_equal)
+            for nm, s in (("CDY", 2), ("CDX", 0)):
+                bk = bank()
+                mm([(reg(bk, k), [(SEL[s], blk("Gp1", k)), (SEL[s + 1], act_("PV"))]) for k in ks])
+                act(H(nm), S(bk), F.Copy)
+            act(S("cgy"), IND(S("YW", 0, 512), blk("O2", h, 32)), F.Copy)
+            act(S("cgx"), IND(S("XW", 0, 512), blk("O2", h, 32)), F.Copy)
+            bk = bank()
+            iy = mm([(reg(bk, k), [(I, blk("cgy", k % 4)), (NI, act_("y16"))]) for k in ks])
+            tt(S("cb"), S(bk), H("CDY"), A.mult)
+            bk = bank()
+            mm([(reg(bk, k), [(I, blk("cgx", k % 4)), (NI, act_("x16"))]) for k in ks], after=[iy])
+            tt(S(bk), S(bk), H("CDX"), A.mult)
+            tt(S(bk), S(bk), S("cb"), A.add)
+            act(S("cab"), S(bk), F.Abs)
+            bk = bank()
+            mm([(reg(bk, k), [(I32, blk("cab", k % 4)), (TS[k], S("sqs", 0, 128))]) for k in ks])
+            act(H("csg"), S(bk), F.Sign, bias=-0.5)
+            bk = bank()
+            ik = mm([(reg(bk, k), [(BO4, blk("csg", k)), (BO, blk("G1", k)), (I, blk("KC", k)), (BOn, blk("EQ", k)),
+                                   (SEL[4 + t], blk("Gp1", k))]) for k in ks], after=prev)
+            prev = [ik]
+            if h == 0:
+                act(S("K0"), S(bk), F.Copy)
+            else:
+                tt(S("K1"), S(bk), S("K0"), A.max)
+        tt(S("K2"), blk("K1", 0, 256), blk("K1", 1, 256), A.max)
+        tt(S("best"), blk("K2", 0), blk("K2", 1), A.max)
+        cp(S("BI"), S("best"))
+        ts(S("BI"), S("BI"), 511, A.bitwise_and)
+        cp(S("c16"), S("BI"))
+        O3 = blk("OC", t, 8)
+        ts(O3, compact(8, "c16", 128), 1.0 / 16, A.mult)
+        tt(S("dd"), S("best"), act_("HEW"), A.min)
+        ts(S("t1"), S("dd"), 0.0, A.is_lt, 1024.0, A.mult)
+        tt(S("C16"), S("c16"), S("t1"), A.add)
+        act(S("Cn"), S("C16"), F.Copy, scale=-1.0)
+        for h in range(2):
+            bk = bank()
+            mm([(reg(bk, k), [(S("C16"), blk("PG", k)), (blk("PG", k), S("Cn")), (I, S("TRc"))]) for k in range(4 * h, 4 * h + 4)])
+            ts(blk("eq2", h, 512), S(bk), 0.0, A.is_equal)
+        tt(S("t2"), IND(S("HEW"), O3), S("dd"), A.min)
+        bk = bank()
+        mm([(S(bk, 0, 128), [(S("CM", 112 - 16 * k, 240 - 16 * k), blk("eq2", k)) for k in range(8)])])
+        tt(S("t2"), S(bk, 0, 128), S("t2"), A.min)
+        ts(blk("AL", t), S("t2"), 0.0, A.is_ge)
+        if t < 2:
+            ts(blk("DD", t), S("t2"), 0.0, A.is_lt)
+        tt(S("Z4"), S("c16"), S("DJ"), A.subtract)
+        tt(blk("R2", 0), blk("ZV", t), blk("AL", t), A.mult)
+        tt(blk("R2", 1), S("Z4"), blk("AL", t), A.mult)
+        tt(S("o4f"), compact(16, "R2", 256), S("K16"), A.add)
+        ts(blk("O4", t, 16), S("o4f"), 1.0 / 16, A.mult)
+        if t < 2:
+            ts(S("t1"), S("c16"), -896.0, A.add)
+            tt(S("t1"), S("t1"), act_("FEW", fo), A.mult)
+            tt(blk("NCOL", 0), S("t1"), act_("LT"), A.add)
+            act(blk("FEc", t), IND(S("FEW", fo, fo + 512), O3), F.Copy)
+            tt(S("t4"), blk("FEc", t), blk("VJ", t), A.mult)
+            tt(blk("NCOL", 1), IND(S("LT", 0, 512), O3), S("t4"), A.add)
+            cp(IND(S("LT"), blk("O4", t, 16)), S("NCOL"))
+        act(S("EP"), IND(S("PW", 0, 512), O3), F.Copy)
+        act(blk("EWC", t), IND(S("WW", 0, 512), O3), F.Copy)
+        bk = bank()
+        mm([(reg(bk, j), [(SEL[2 * j], S("EP")), (SEL[2 * j + 1], act_("PV"))]) for j in range(2)])
+        act(blk("ED", t, 256), S(bk, 0, 256), F.Copy)
+        act(blk("EN", t, 256), S(bk, 0, 256), F.Copy, scale=-1.0)
+        act(blk("ES", t, 256), S(bk, 0, 256), F.Square, scale=1.0 / 32)
+
+    def extra(s, t):
+        rho = 3 - s
+        O3 = blk("OC", s, 8)
+        act(blk("eg", 0), IND(S("XW", 0, 512), O3), F.Copy)
+        act(blk("eg", 1), IND(S("YW", 0, 512), O3), F.Copy)
+        bk = bank()
+        mm([(S(bk, 128 * j, 128 * j + 128), [(I, blk("eg", j)), (NI, S(nm, rho, 512, 4))]) for j, nm in enumerate(("x16", "y16"))])
+        tt(S("EA"), S(bk, 0, 256), blk("ED", s, 256), A.mult)
+        tt(S("EZ"), blk("EA", 0), blk("EA", 1), A.add)
+        if s < t:
+            tt(S("EZ"), S("EZ"), blk("EQq", s), A.add)
+        act(S("esg"), S("EZ"), F.Sign)
+        act(S("eab"), S("EZ"), F.Abs)
+        bk = bank()
+        mm([(S(bk, 0, 128), [(I32, S("eab")), (IBn, blk("ES", 2 * s)), (IBn, blk("ES", 2 * s + 1))]
+             + ([(IBn, blk("DD", s))] if s < t else []))])
+        ts(S("em"), S(bk, 0, 128), 0.0, A.max, 1023.0, A.min)
+        if s < t:
+            act(S("enz"), S("em"), F.Sign)
+            bk = bank()
+            mm([(S(bk, 0, 128), [(BO, S("enz"))])])
+            ts(blk("AL", s), S(bk, 0, 128), 4.0, A.is_ge)
+            if t < 2:
+                ts(blk("DD", s), S(bk, 0, 128), 4.0, A.is_lt)
+        tt(S("em"), S("em"), blk("AL", s), A.mult)
+        tt(blk("EQq", s), S("em"), S("esg"), A.mult)
+        oc = S("O4", 16 * s + 8, 16 * s + 16)
+        zs = []
+        if s == t:
+            macc = S("em") if t == 2 else blk("EM", s)
+            if t < 2:
+                act(macc, blk("EQq", s), F.Abs)
+        else:
+            macc = blk("EM", s)
+            tt(macc, macc, S("em"), A.add)
+        for j, (src, cv, cc) in enumerate(((blk("EQq", s), blk("ED", 2 * s), blk("EN", 2 * s)),
+                                           (blk("EQq", s), blk("ED", 2 * s + 1), blk("EN", 2 * s + 1)),
+                                           (macc, blk("EWC", s), S("WW", rho, 512, 4)))[:3 if t == 2 else 2]):
+            o = ZC * (3 * s + j)
+            if s == t or j == 2:
+                iota(S("ZZ", o, o + ZC), [[0, ZC]], 0)
+            tt(S("ZZ", o + rho, o + 512, 4), src, cv, A.mult)
+            tt(IND(S("ZZ", o, o + ZC), oc), src, cc, A.mult)
+            zs.append(S("ZZ", o, o + 512))
+        for j, acc in enumerate(("xacc", "yacc")):
+            if s < t and TUNE["dsum"][j]:
+                dma("g", blk(acc, s, 512), zs[j], acc=True, lat=DLAT)
+            else:
+                mm([(S("@%d" % j), [(I32, zs[j])])], start=False, stop=s == t)
+        if t == 2:
+            wsum(zs[2], s == 2)
+        if s == 0 and t == 1:
+            ts(S("t1"), blk("DD", 0), 896.0, A.mult)
+            tt(blk("t3", 0), S("t1"), S("FEW", 3, 512, 4), A.mult)
+            tt(blk("t3", 1), S("t1"), blk("FEc", 0), A.mult)
+            tt(S("NCOL"), IND(S("LT"), blk("O4", 0, 16)), S("t3"), A.max)
+            cp(IND(S("LT"), blk("O4", 0, 16)), S("NCOL"))
+
+    def chunk(t, k):
+        n = 8 * t + k
+        R = lambda nm: blk(nm, n % (_B[nm][0] // 512), 512)
+        C = lambda nm: blk(nm, k, 512)
+        sg = R("sg")
+        o = blk("Lo", k, 32)
+        if t == 0:
+            for nm, s in (("DY", 2), ("DX", 0)):
+                bk = bank()
+                mm([(S(bk), [(SEL[s], C("Q16")), (SEL[s + 1], S("PV"))])])
+                act(C(nm), S(bk), F.Copy)
+        act(R("gy"), IND(S("YW"), o), F.Copy)
+        act(R("gx"), IND(S("XW"), o), F.Copy)
+        bk = S(bank())
+        iy = mm([(bk, [(I, R("gy")), (NI, S("y16"))])])
+        tt(R("bb"), bk, C("DY"), A.mult)
+        bk = S(bank())
+        mm([(bk, [(I, R("gx")), (NI, S("x16"))])], after=[iy])
+        tt(bk, bk, C("DX"), A.mult)
+        tt(bk, bk, R("bb"), A.add)
+        if t:
+            tt(bk, bk, C("Q16"), A.add)
+        act(R("ab"), bk, F.Abs)
+        act(sg, bk, F.Sign)
+        bk = S(bank())
+        mm([(bk, [(I32, R("ab")), (TS[k], blk("FF", t, 512))])])
+        act(R("r16"), bk, F.Relu)
+        if n not in TUNE["nzv"]:
+            act(R("nz"), R("r16"), F.Sign)
+        else:
+            ts(R("nz"), R("r16"), 0.0, A.is_gt)
+        bn = bank()
+        z0 = R("nz")[2]
+        mm([(S(bn, 0, 256), [(GS[k], S("nz", z0, z0 + 256)), (GS[8 + k], S("nz", z0 + 256, z0 + 512))])])
+        z0 = R("r16")[2]
+        act(blk("AS", k, 256), S(bn, 0, 256), F.Sign, bias=-3.5)
+        bn = bank()
+        bk = S(bn)
+        if t == 2 or n in TUNE["mina"]:
+            def less(bn, more):
+                mm([(S(bn, 256 * h, 256 * h + 256), [(blk("SB", 8 * h + k), blk("AS", k, 256)),
+                                                     (NI, S("r16", z0 + 256 * h, z0 + 256 * h + 256))]
+                     + [(I, blk("MQ", 16 * u + 2 * k + h, 256)) for u in more]) for h in range(2)])
+            less(bn, ())
+            act(R("r16"), bk, F.Relu)
+            if t == 2:
+                act(R("pw"), IND(S("WW"), o), F.Copy)
+                bn = bank()
+                less(bn, (0, 1))
+                dst = blk("wacc", k, 512) if k < 2 else R("pw")
+                tt(dst, S(bn), R("pw"), A.mult)
+                if k >= 2:
+                    wsum(dst, k >= 6)
+            bn = bank()
+            bk = S(bn)
+            less(bn, ())
+        else:
+            mm([(S(bn, 256 * h, 256 * h + 256), [(blk("SB", 8 * h + k), blk("AS", k, 256))]) for h in range(2)])
+            tt(bk, bk, R("r16"), A.min)
+        if t < 2:
+            tt(C("Q16"), bk, sg, A.mult)
+            keep = grp[0]
+            grp[0] = (100.0 * (t + 1) + TUNE["mq"], 1.0)
+            act(blk("MQ", 8 * t + k, 512), C("Q16"), F.Abs)
+            grp[0] = keep
+            bk = S(bank())
+            mm([(bk, [(I, C("Q16"))])])
+        else:
+            tt(bk, bk, sg, A.mult)
+        for j, (pp, d, acc) in enumerate((("ppx", "DX", "xacc"), ("ppy", "DY", "yacc"))):
+            last = TUNE["dsum"][j]
+            if k < 2 and last:
+                tt(blk(acc, k, 512), bk, C(d), A.mult)
+            else:
+                tt(R(pp), bk, C(d), A.mult)
+                if k < last:
+                    dma("g", blk(acc, k % 2, 512), R(pp), acc=True, lat=DLAT)
+                else:
+                    mm([(S("@%d" % j), [(I32, R(pp))])], start=False, stop=False)
+            if k == 7 and last:
+                for h in range(2):
+                    mm([(S("@%d" % j), [(I32, blk(acc, h, 512))])], start=False, stop=False)
+
+    for t in range(3):
+        mm([(S("@0"), [(I32x, S("x16"))])], stop=False)
+        mm([(S("@1"), [(I32x, S("y16")), (I, S("ld16"))])], stop=False)
+        t0 = 100.0 * (t + 1)
+        grp[0] = (t0 + TUNE["s1"][0], TUNE["s1"][1])
+        step1(t)
+        for k in range(8):
+            grp[0] = (t0 + TUNE["per"] * k, TUNE["cs"])
+            chunk(t, k)
+            if 2 <= k < 2 + t:
+                grp[0] = (t0 + TUNE["ex"] * (k - 2) - 1.0, TUNE["cs"])
+                extra(k - 2, t)
+        grp[0] = (t0 + TUNE["exn"], 1.0)
+        extra(t, t)
+        grp[0] = (t0 + 50.0, 0.01)
+        if t < 2:
+            bn = bank()
+            mm([(S(bn, 256 * h, 256 * h + 256), [(blk("EE", 8 * h + k), blk("AS", k, 256)) for k in range(8)]
+                 + [(IH, S("FF", 512 * t + 256 * h, 512 * t + 256 * h + 256))]) for h in range(2)])
+            act(blk("FF", t + 1, 512), S(bn), F.Copy)
+            bn = bank()
+            mm([(S(bn), [(I896, blk("FF", t + 1, 512)), (N896, blk("FF", t, 512))])])
+            tt(S("LT", 0, 512), S(bn), S("LT", 0, 512), A.max)
+        for bn, ti, wi, h in (("@0", "UXI", "XW", "x16"), ("@1", "UYI", "YW", "y16")):
+            ts(S(ti), S(bn), 0.5, A.add, 1.0 / 32, A.mult)
+            ts(S(wi, 0, 512), S(ti), -1023.0, A.max, 1023.0, A.min)
+            if t < 2:
+                act(S(h), S(wi, 0, 512), F.Copy)
+        if t < 2:
+            border(t + 1, [])
+    dma("s", "yx", S("XW", 0, 512))
+    dma("s", "yy", S("YW", 0, 512))
+    bk = S(bank())
+    terms = [blk("wacc", 0, 512), blk("wacc", 1, 512), last_w[2], last_w[0], last_w[1]]
+    for m, x in enumerate(terms):
+        mm([(bk, [(I32, x)])], start=m == 0, stop=m == 4)
+    act(S("wout"), bk, F.Copy)
+    dma("s", "yw", S("wout"))
+    return ops
+
+
+def schedule(ops):
+    n = len(ops)
+    summand = lambda o: o["kind"] == "mm" and not o["args"][1] and not o["args"][2]
+    hist = {}
+    deps = []
+    users = {}
+    for i, o in enumerate(ops):
+        d = dict((j, True) for j in o["after"])
+        acc = [(x, False) for x in o["rd"]] + [(x, True) for x in o["wr"]]
+        for x, w in acc:
+            nm = x[1]
+            ps = nm[0] == "@"
+            lo, hi = (0, 512) if ps else (x[2], x[3])
+            for (j, a, b, wj) in hist.get(nm, ()):
+                if j == i or b <= lo or hi <= a:
+                    continue
+                if ps and summand(o) and summand(ops[j]):
+                    continue
+                if x[5] is not None and ops[j]["wr"] and ops[j]["wr"][0][5] not in (None, x[5]):
+                    continue
+                same = ops[j]["eng"] == o["eng"] and ops[j]["kind"] != "dma" and o["kind"] != "dma"
+                if wj and not w:
+                    d[j] = True
+                elif wj or w:
+                    d[j] = d.get(j, False) or not (same and ps and o["eng"] == "t")
+                elif ps and not same:
+                    d[j] = True
+            if ps:
+                users.setdefault(nm, set()).add(i)
+        for x, w in acc:
+            nm = x[1]
+            lo, hi = (0, 512) if nm[0] == "@" else (x[2], x[3])
+            h = hist.setdefault(nm, [])
+            if w and x[4] == 1 and x[5] is None and nm[0] != "@":
+                h[:] = [e for e in h if not (lo <= e[1] and e[2] <= hi)]
+            h.append((i, lo, hi, w))
+        deps.append(d)
+    succ = [[] for _ in range(n)]
+    for i in range(n):
+        for j in deps[i]:
+            succ[j].append(i)
+    pr = [0.0] * n
+    for i in range(n - 1, -1, -1):
+        pr[i] = ops[i]["cost"] + ops[i]["lat"] + max([pr[j] + HOP for j in succ[i]] + [0.0])
+    head = [0.0] * n
+    for i in range(n):
+        base, stretch = ops[i]["grp"]
+        head[i] = max([head[j] + ops[j]["cost"] + ops[j]["lat"] + HOP for j in deps[i] if ops[j]["grp"] == ops[i]["grp"]] + [0.0])
+        if base:
+            pr[i] = -(base + stretch * head[i])
+    rng = np.random.default_rng(1)
+    best = place(ops, deps, succ, users, pr)
+    for _ in range(TUNE["tries"]):
+        q = list(pr)
+        for _r in range(3):
+            a = int(rng.integers(0, n))
+            d = float(rng.normal()) * 4.0
+            for i in range(a, min(n, a + int(rng.integers(1, 40)))):
+                q[i] += d
+        new = place(ops, deps, succ, users, q)
+        if max(new[3]) <= max(best[3]):
+            best, pr = new, q
+    return best
+
+
+def place(ops, deps, succ, users, pr):
+    n = len(ops)
+    deps = [dict(d) for d in deps]
+    first = dict((min(u), nm) for nm, u in users.items() if nm not in ("@0", "@1"))
+    left = dict((nm, len(u)) for nm, u in users.items())
+    waiting = sorted(first)
+    phys = {"@0": 0, "@1": 1}
+    free = dict((b, (0.0, [])) for b in range(2, 8))
+    fin = [None] * n
+    cnt = [len(deps[i]) for i in range(n)]
+    ready = [i for i in range(n) if cnt[i] == 0]
+    est = dict((i, 0.0) for i in ready)
+    efree = dict((e, 0.0) for e in "tvagsr")
+    order = []
+    while ready:
+        cand = []
+        for i in ready:
+            s = max(est[i], efree[ops[i]["eng"]])
+            if i in first:
+                if len(free) < (1 if i == waiting[0] else 2):
+                    continue
+                s = max(s, min(v[0] for v in free.values()))
+            cand.append((s, i))
+        s0, i0 = min(cand)
+        e = ops[i0]["eng"]
+        s, i = max(((s, i) for s, i in cand if ops[i]["eng"] == e and s <= s0 + TUNE["win"]), key=lambda c: pr[c[1]])
+        if i in first:
+            b = min(free, key=lambda k: free[k][0])
+            for j in free.pop(b)[1]:
+                deps[i][j] = True
+            phys[first[i]] = b
+            waiting.remove(i)
+        efree[e] = s + ops[i]["cost"]
+        fin[i] = efree[e] + ops[i]["lat"]
+        order.append(i)
+        ready.remove(i)
+        for nm in set(x[1] for x in ops[i]["rd"] + ops[i]["wr"] if x[1][0] == "@"):
+            left[nm] -= 1
+            if left[nm] == 0 and nm not in ("@0", "@1"):
+                free[phys[nm]] = (max(fin[j] for j in users[nm]) + HOP, list(users[nm]))
+        for j in succ[i]:
+            cnt[j] -= 1
+            if cnt[j] == 0:
+                est[j] = max(fin[k] + (HOP if deps[j][k] else 0.0) for k in deps[j])
+                ready.append(j)
+    return order, deps, phys, fin
+
+
+PLAN = []
+
+
+def rank_program(g, core, T, topo):
+    rank = T.rank_of(core)
+    if rank is None:
+        return
+    if not PLAN:
+        ops = build()
+        PLAN.append((ops,) + schedule(ops))
+    ops, order, deps, phys, fin = PLAN[0]
+    N = len(T.cores)
+    peers = [T.cores[(rank + d) % N] for d in range(1, N)]
+    eng = [e for e in topo.engines(core, peers[0]) if all(e in topo.engines(core, p) for p in peers)]
+    queue = {"t": g.tensor, "v": g.vector, "a": g.scalar, "g": g, "s": g.sync}
+
+    def ap(x):
+        if not is_ap(x):
+            return x
+        if x[0] == "ind":
+            return ap(x[1]).indirect(ap(x[2]))
+        nm, o = ("P%d" % phys[x[1]], 0) if x[1][0] == "@" else PLACE[x[1]]
+        p = slice(None) if x[5] is None else slice(*x[5])
+        return T[nm][p, o + x[2]:o + x[3]] if x[4] == 1 else T[nm][p, o + x[2]:o + x[3]:x[4]]
+
+    mark = {}
+    clock = {}
+    known = dict((e, {}) for e in queue)
+    count = dict((e, 0) for e in "tvag")
+    total = {}
+    sent = 0
+    for i in order:
+        o = ops[i]
+        e = o["eng"]
+        if e == "r":
+            mark[i] = (o["args"][0], (N - 1) * (len(eng) // o["args"][1]))
+            clock[i] = {mark[i][0]: mark[i][1]}
+            total[mark[i][0]] = mark[i][1]
+            continue
+        q, kn = queue[e], known[e]
+        need = sorted((j for j in deps[i] if deps[i][j] and j in mark), key=lambda j: -fin[j])
+        for j in need:
+            sem, val = mark[j]
+            if kn.get(sem, 0) < val:
+                val = max(mark[k][1] for k in need if mark[k][0] == sem)
+                q.wait_ge(T.sem[sem], val)
+                kn[sem] = val
+            for s, v in clock[j].items():
+                kn[s] = max(kn.get(s, 0), v)
+        a = o["args"]
+        if o["kind"] == "send":
+            parts = a[0]
+            per = len(eng) // len(parts)
+            trs = []
+            for m, (src, nm, c0, w, sem) in enumerate(parts):
+                ids, dsts = [], []
+                for d, p in enumerate(peers):
+                    rid, pid = topo.addr(p, core)
+                    ids.append(DstId(rid=rid, pnc=pid))
+                    dsts.append(T[nm][:, c0 + d * w:c0 + (d + 1) * w])
+                trs.append(RemoteDMATransfer(dst_ids=ids, dma_engine_mask=sum(1 << x for x in eng[m * per:(m + 1) * per]),
+                                             remote_sem=T.sem[sem], src=ap(src), dsts=dsts))
+            g.remote_dma_fused(trs, local_sem=T.sem.ls)
+            sent += per * len(parts)
+            continue
+        if o["kind"] == "dma":
+            kw = {"accum_op": A.add} if a[2] else {}
+            q.dma_start(*[ap(x) if is_ap(x) else T[x][:] for x in a[:2]], **kw).then_inc(T.sem[a[3]], 16)
+            mark[i] = (a[3], 16)
+            total[a[3]] = 16
+        else:
+            if o["kind"] == "mm":
+                for out, terms in a[0]:
+                    for m, (l, r) in enumerate(terms):
+                        ins = q.matmul(ap(out), ap(l), ap(r), a[1] and m == 0, a[2] and m == len(terms) - 1)
+            else:
+                fn = {"tensor_tensor": g.vector.tensor_tensor, "tensor_scalar": g.vector.tensor_scalar,
+                      "tensor_copy": g.vector.tensor_copy, "memset": g.vector.memset, "transpose": g.vector.transpose,
+                      "activation": g.scalar.activation, "iota": g.iota}[o["kind"]]
+                ins = fn(*[ap(x) for x in a], **dict((k, ap(v)) for k, v in o["kw"].items()))
+            count[e] += 1
+            ins.then_inc(T.sem["q" + e], 1)
+            mark[i] = ("q" + e, count[e])
+            total["q" + e] = count[e]
+        clock[i] = dict(kn)
+        clock[i][mark[i][0]] = mark[i][1]
+    g.wait_ge(T.sem.ls, sent)
+    for sem, val in total.items():
+        if known["s"].get(sem, 0) < val:
+            g.sync.wait_ge(T.sem[sem], val)

@@ -3,37 +3,36 @@ from concourse.bass import DstId, RemoteDMATransfer
 from concourse.mybir import AluOpType as A, ActivationFunctionType as F
 
 f32, f16, b16, i32, u16 = "float32", "float16", "bfloat16", "int32", "uint16"
-ZWID = 776
 ZC = 648
-BIG = 65536.0
 _B = {
-    "XW": (904, f32), "YW": (904, f32), "PW": (904, f32), "WW": (904, f32), "x16": (512, f16), "y16": (512, f16),
-    "ld16": (512, f16), "PV": (512, b16), "DX": (4096, b16), "DY": (4096, b16), "MQ": (8192, f16), "Q16": (4096, f16),
-    "gx": (1024, f16), "gy": (1024, f16), "bb": (1024, f32), "ab": (1024, f32), "xacc": (1024, f32),
-    "pw": (1536, f32), "ppx": (1536, f32), "ppy": (1536, f32), "sg": (2048, b16), "r16": (1536, f16), "nz": (1024, b16),
-    "AS": (2048, b16), "FF": (1536, b16), "LT": (ZWID, f32),
-    "ZZ": (9 * ZC, f32), "UXI": (512, i32), "UYI": (512, i32), "PI": (512, i32), "NBI": (256, i32),
-    "BDI": (8, i32), "Lo": (256, u16), "bo": (8, u16), "wacc": (1024, f32), "yacc": (1024, f32),
-    "SXY": (768, f16), "LXY": (2304, f16), "SP": (128, f32), "SW": (128, f32),
-    "ef": (512, b16), "FEW": (1024, b16), "HEW": (512, b16), "U16": (128, f16), "Um": (1024, f16), "O1": (64, u16),
-    "O2": (64, u16), "EQ": (1280, b16), "Gp1": (1024, b16), "cgx": (512, f16), "cgy": (512, f16),
-    "CDX": (1024, b16), "CDY": (1024, b16), "sqs": (512, b16), "cb": (512, f32), "cab": (512, f32), "csg": (1024, b16),
-    "K0": (512, f32), "K2": (256, f32), "best": (128, f32), "BI": (128, i32), "c16": (128, f16),
-    "dd": (128, f32), "t1": (128, f32), "t2": (128, f32), "t3": (256, f32), "t4": (128, f32), "C16": (128, f16),
-    "Cn": (128, f16), "OC": (24, u16), "O4": (48, u16), "o4f": (16, f32), "FEc": (256, b16),
-    "NCOL": (256, f32), "Z4": (128, f16), "R2": (256, f16), "AL": (384, b16), "DD": (384, b16), "EP": (128, b16),
-    "ED": (768, f32), "EN": (768, f32), "ES": (768, b16), "EWC": (384, f32), "EQq": (384, f32), "EM": (256, f32), "eg": (256, f16),
-    "EA": (256, f32), "EZ": (128, f32), "esg": (128, b16), "eab": (128, f32), "em": (128, f32), "enz": (128, b16),
-    "ci": (4, i32), "cj": (4, i32), "col": (16, f32), "RM": (17, f32), "RC": (40, f32),
-    "MD": (1280, b16), "KC": (1024, b16),
-    "PG": (1024, b16), "IDS": (128 * 8, b16), "I32": (128, f32), "GSB": (144, b16), "BO": (128 * 3, b16),
-    "TS": (1024, b16), "SEL": (128 * 7, b16), "SB": (2048, f16), "EE": (2048, b16), "TRI": (128, b16), "B2": (136, b16),
-    "nPV": (128, b16), "TRc": (128, b16), "CM": (240, b16), "SH": (320, b16), "MM": (128, b16), "VJ": (384, f32),
-    "ZV": (384, f16), "DJ": (128, f32), "K16": (16, f32),
+    "XW": (904, f32), "YW": (904, f32), "WW": (904, f32), "PW": (912, b16), "UT": (1024, f16), "LD2": (1024, f16),
+    "DXT": (4096, b16), "DYT": (4096, b16), "NT": (4096, b16), "DD": (8192, b16), "Q16": (4096, f16), "RR": (8192, f16),
+    "R2": (2048, f16), "gx": (2048, f16), "gy": (2048, f16), "PB": (2048, f32), "ZB": (2048, f32),
+    "R0": (2048, f16), "NZ": (2048, b16), "PP": (1024, f32), "UI": (1024, i32), "PI": (512, i32), "NBI": (256, i32),
+    "BDI": (8, i32), "Lo": (256, u16), "bo": (8, u16), "SX": (384, f16), "SY": (384, f16), "LX": (1152, f16),
+    "LY": (1152, f16), "SP": (128, b16), "SW": (128, f32), "LT": (ZC, f32), "Z2": (6 * ZC, f32), "ZW": (3 * ZC, f32),
+    "SS": (768, b16), "tc": (256, b16), "AI": (256, b16), "ND": (512, b16),
+    "cgx": (1024, f16), "cgy": (1024, f16), "CDX": (1024, b16), "CDY": (1024, b16), "cb": (1024, f32),
+    "EQ": (512, b16), "xa": (256, f16),
+    "O1": (64, u16), "O2": (64, u16), "UL": (64, f16), "CI": (64, i32), "ia": (128, i32), "ib": (64, i32), "ic": (64, i32),
+    "CL": (64, f16), "FB": (128, b16), "dL": (128, b16), "sqL": (128, b16), "KY": (256, f32), "PVL": (384, f32),
+    "ef": (256, b16), "hn": (128, b16), "BI": (128, i32), "BJ": (128, i32), "t1": (128, f16), "c16": (128, f16),
+    "C16": (128, f16), "Cn": (128, f16), "O3": (24, u16), "Oc": (24, u16), "Ox": (24, u16), "Oy": (24, u16),
+    "cf": (40, f32), "dum": (8, f32), "LTc": (128, f32), "AL": (384, b16), "DN": (128, b16), "FE": (512, b16),
+    "NV": (128, f32), "NC": (256, f32), "VJ": (384, f32), "vio": (384, f16), "EP": (128, b16), "ED": (768, f32),
+    "nq": (384, f32), "ES": (768, b16), "EWC": (384, f32), "EQq": (384, f32), "EM": (1152, f16), "eg": (512, f16),
+    "EA": (512, f32), "em": (256, f16), "enz": (256, b16), "EMs": (384, f32),
+    "ci": (16, i32), "cj": (24, i32), "col": (40, f32), "RM": (16, f32), "MK": (16, f32), "e8": (8, f32),
+    "IX": (256, b16), "IG": (128, b16), "IH": (128, b16), "MD": (1040, b16), "one": (1024, b16),
+    "IDS": (128 * 7, b16), "I1023": (128, f16), "F32": (128 * 9, f32), "GSB": (144 * 5, b16), "BO": (256, b16),
+    "BR": (2048, b16), "NB": (128 * 4, b16), "OX": (1024, b16), "WV": (1136, b16), "NXR": (896, b16), "PGm": (1024, b16),
+    "RB": (128 * 5, b16), "HB": (256, b16), "TRI": (256, b16), "TRc": (128, b16), "CM": (240, b16), "SH": (320, b16),
+    "nf": (8, b16),
 }
-ALIAS = {"wout": ("K0", 0, 512), "Zp": ("Um", 0, 512), "Zt": ("Um", 512, 512), "LDI": ("UXI", 0, 512), "G1": ("Um", 0, 1024),
-         "K1": ("cab", 0, 512), "tb": ("EQ", 0, 1280), "eq2": ("EQ", 0, 1024), "IX": ("cb", 0, 256),
-         "IG": ("cb", 256, 128), "PR": ("cb", 384, 128), "H8": ("K0", 0, 128), "tq": ("csg", 0, 256)}
+ALIAS = {"XY16": ("Q16", 0, 1024), "PI2": ("NZ", 0, 1024), "PT": ("DD", 0, 1024), "Zp": ("cgx", 0, 512), "Zt": ("cgx", 512, 512),
+         "G1": ("cgx", 0, 1024), "csg": ("CDX", 0, 1024), "eq2": ("CDY", 0, 1024), "PG": ("RR", 4096, 4096), "eab": ("EA", 0, 256),
+         "dc": ("ND", 0, 512), "sq": ("SS", 256, 512),
+         "tb": ("CDX", 0, 1024), "WX": ("cb", 0, 512), "wout": ("cb", 512, 512), "LDI": ("PI", 0, 512)}
 PLACE = {}
 SCRATCH = {}
 for _k, (_w, _d) in _B.items():
@@ -46,13 +45,18 @@ for _k, (_w, _d) in _B.items():
         SCRATCH["pool_" + _d] = ("sbuf", [128, _o + (_w + 15) // 16 * 16], _d)
 for _i in range(8):
     SCRATCH["P%d" % _i] = ("psum", [128, 512], f32)
-NDMA = 90
-SEMAPHORES = ["qt", "qv", "qa", "qg", "ls", "aP", "aW", "a0", "a1", "a2"] + ["d%d" % _i for _i in range(NDMA)]
+NDMA = 100
+SEMAPHORES = ["qt", "qv", "qa", "qg", "ls", "aP", "aW"] + ["a%s%d" % (_c, _i) for _c in "xy" for _i in range(3)] \
+    + ["d%d" % _i for _i in range(NDMA)]
 SZ = {f32: 4, f16: 2, b16: 2, i32: 4, u16: 2}
-CY = 0.83e-3 * 1.15
+CY = 0.83e-3 * 1.1
+GA = 1.56
 HOP = 0.12
-TUNE = {'s1': (-10, 1.1), 'per': 1.31, 'cs': 0.1, 'ex': 10.0, 'exn': 15.5, 'cv': (4, 5, 6, 9, 10, 13, 16, 17, 19, 21, 23, 26, 29, 30, 33, 35, 37, 44, 45, 50, 51, 52, 53, 59, 64, 69, 70, 74, 76, 77, 78, 82, 84, 86, 89, 93, 101, 102, 117, 118, 120, 123, 126, 128, 132, 134, 135, 139, 145, 151, 156), 'dsum': (6, 7), 'mq': 22.1, 'win': 0, 'um': (0, 8, 4), 'mina': (4, 6, 7, 8, 9, 12, 14), 'nzv': (0, 15, 16, 17, 18, 19), 'tries': 200}
 DLAT = 2.6
+BIG = 65536.0
+GROUPS = [((0, 1), 1, 1), ((2, 3), 1, 1), ((4, 5), 1, 1), ((6,), 1, 1), ((7,), 0, 0)]
+TRIES = 1500
+MARGIN = 0.5
 
 
 def S(name, a=0, b=None, step=1, p=None):
@@ -69,7 +73,7 @@ def IND(win, off):
 
 
 def is_ap(x):
-    return isinstance(x, tuple) and x[0] in ("ap", "ind")
+    return isinstance(x, tuple) and len(x) > 0 and x[0] in ("ap", "ind")
 
 
 def width(x):
@@ -86,31 +90,31 @@ def size(x):
     return 4 if psum(x) else SZ[_B[x[1]][1]]
 
 
+def sub(x, a, b, step=1, p=None):
+    return ("ap", x[1], x[2] + a, x[2] + b, step, p)
+
+
 def build():
     ops = []
-    nb = [2]
+    nb = [0]
     nd = [0]
-    nc = [0]
-    grp = [(0.0, 1.0)]
+    tag = ["setup"]
 
     def bank():
         nb[0] += 1
         return "@%d" % nb[0]
 
-    def add(eng, kind, args, rd, wr, cost, lat=0.0, after=(), kw=None):
+    def add(alts, rd, wr, lat=0.0, after=()):
         r, w = [], []
         for x in rd:
-            if x[0] == "ind":
-                r += [x[1], x[2]]
-            else:
-                r.append(x)
+            r += [x[1], x[2]] if x[0] == "ind" else [x]
         for x in wr:
             if x[0] == "ind":
                 w.append(x[1])
                 r.append(x[2])
             else:
                 w.append(x)
-        ops.append(dict(grp=grp[0], eng=eng, kind=kind, args=args, rd=r, wr=w, cost=cost, lat=lat, after=list(after), kw=kw or {}))
+        ops.append(dict(alts=alts, rd=r, wr=w, lat=lat, after=list(after), tag=tag[0]))
         return len(ops) - 1
 
     def vcost(out, ins, two):
@@ -118,42 +122,70 @@ def build():
         if out[0] == "ind":
             return 0.05 + 3.8 * n * CY
         if ins and ins[0][0] == "ind":
-            return 0.05 + 1.56 * n * CY
+            return 0.05 + GA * n * CY
         if two:
             c = 1 if any(psum(x) for x in ins) else 2
         else:
             c = 0.5 if all(size(x) == 2 for x in [out] + ins) else 1
         return 0.05 + max(64, n * c) * CY
 
-    def tt(out, a, b, op):
-        return add("v", "tensor_tensor", (out, a, b, op), [a, b], [out], vcost(out, [a, b], True))
-
-    def ts(out, a, s1, op0, s2=None, op1=None):
+    def v_ts(out, a, s1, op0, s2=None, op1=None):
         args = (out, a, s1, s2, op0) if op1 is None else (out, a, s1, s2, op0, op1)
-        return add("v", "tensor_scalar", args, [a] + [s for s in (s1, s2) if is_ap(s)], [out], vcost(out, [a], False))
+        return ("v", "tensor_scalar", args, {}, vcost(out, [a], False))
 
-    def cp(out, a):
-        return add("v", "tensor_copy", (out, a), [a], [out], vcost(out, [a], False))
+    def v_cp(out, a):
+        return ("v", "tensor_copy", (out, a), {}, vcost(out, [a], False))
 
-    def ms(out, c):
-        return add("v", "memset", (out, c), [], [out], vcost(out, [], False))
-
-    def act(out, a, fn, bias=None, scale=None):
+    def a_act(out, a, fn, bias=None, scale=None):
         kw = {}
-        if fn == F.Copy and scale is None:
-            nc[0] += 1
-            if nc[0] in TUNE["cv"]:
-                return cp(out, a)
         if bias is not None:
             kw["bias"] = bias
         if scale is not None:
             kw["scale"] = scale
-        c = 0.07 + max(64, width(a) * (1.56 if a[0] == "ind" else 1)) * CY
-        return add("a", "activation", (out, a, fn), [a] + ([scale] if is_ap(scale) else []), [out], c, kw=kw)
+        return ("a", "activation", (out, a, fn), kw, 0.07 + max(64, width(a) * (GA if a[0] == "ind" else 1)) * CY)
+
+    def aps(*xs):
+        return [x for x in xs if is_ap(x)]
+
+    def tt(out, a, b, op):
+        return add([("v", "tensor_tensor", (out, a, b, op), {}, vcost(out, [a, b], True))], [a, b], [out])
+
+    def ts(out, a, s1, op0, s2=None, op1=None):
+        return add([v_ts(out, a, s1, op0, s2, op1)], aps(a, s1, s2), [out])
+
+    def cp(out, a):
+        return add([v_cp(out, a)], [a], [out])
+
+    def ms(out, c):
+        return add([("v", "memset", (out, c), {}, vcost(out, [], False))], [], [out])
+
+    def act(out, a, fn, bias=None, scale=None):
+        return add([a_act(out, a, fn, bias, scale)], aps(a, bias, scale), [out])
+
+    def mv(out, a, scale=None, bias=None):
+        if scale is None and bias is None:
+            alts = [a_act(out, a, F.Copy), v_cp(out, a)]
+        elif bias is None:
+            alts = [a_act(out, a, F.Copy, scale=scale), v_ts(out, a, scale, A.mult)]
+        else:
+            alts = [a_act(out, a, F.Identity, bias=bias), v_ts(out, a, bias, A.add)]
+        return add(alts, aps(a, scale, bias), [out])
+
+    def gather(out, a):
+        return act(out, a, F.Copy)
+
+    def relu(out, a):
+        return add([a_act(out, a, F.Relu), v_ts(out, a, 0.0, A.max)], [a], [out])
+
+    def nonzero(out, a):
+        return add([v_ts(out, a, 0.0, A.is_gt), a_act(out, a, F.Sign)], [a], [out])
 
     def iota(out, pat, base, cm=0):
         kw = {} if _B[out[1]][1] == i32 else {"allow_small_or_imprecise_dtypes": True}
-        return add("g", "iota", (out, pat, base, cm), [], [out], 0.13 + 2 * width(out) * CY, kw=kw)
+        return add([("g", "iota", (out, pat, base, cm), kw, 0.13 + 2 * width(out) * CY)], [], [out])
+
+    def asel(out, a, pat, base, op=A.is_equal):
+        return add([("g", "affine_select", (out, a, pat, op, 0.0, base, 1), {}, 0.17 + 2 * width(out) * CY)], [a], [out])
 
     def mm(groups, after=(), start=True, stop=True):
         rd, wr, c = [], [], 0.03
@@ -161,19 +193,18 @@ def build():
             wr.append(out)
             for l, r in terms:
                 rd += [l, r]
-                c += max(64, width(r)) * (4 if size(r) == 4 else 1) * CY / 2
-        return add("t", "mm", (groups, start, stop), rd, wr, c, after=after)
+                c += max(min(64, width(l)), width(r)) * (4 if size(r) == 4 else 1) * CY / 2
+        return add([("t", "mm", (groups, start, stop), {}, c)], rd, wr, after=after)
 
     def dma(eng, out, a, acc=False, lat=2.2):
-        rd = [x for x in (a,) if is_ap(x)] + ([out] if acc else [])
         nd[0] += 1
-        return add(eng, "dma", (out, a, acc, "d%d" % (nd[0] - 1)), rd, [x for x in (out,) if is_ap(x)],
-                   1.0 if eng == "g" else 0.1, lat=lat)
+        return add([(eng, "dma", (out, a, acc, "d%d" % (nd[0] - 1)), {}, 1.0 if eng == "g" else 0.1)],
+                   aps(a) + ([out] if acc else []), aps(out), lat=lat)
 
     def send(parts):
-        i = add("g", "send", (parts,), [p[0] for p in parts], [], 1.0)
-        for src, nm, a, w, sem in parts:
-            add("r", "recv", (sem, len(parts)), [], [S(nm, a, a + 3 * w)], 0.0, lat=4.5, after=[i])
+        i = add([("g", "send", (parts,), {}, 1.0)], [p[0] for p in parts], [])
+        for src, nm, a, w, sem, ne in parts:
+            add([("r", "recv", (sem, ne), {}, 0.0)], [], [S(nm, a, a + 3 * w)], lat=4.5, after=[i])
 
     def blk(name, k, w=128):
         return S(name, k * w, (k + 1) * w)
@@ -185,488 +216,503 @@ def build():
     ms(S("PI"), 0)
     dma("s", S("PI", p=(0, 128, 16)), "px")
     dma("a", S("PI", p=(8, 128, 16)), "py")
-    dma("s", S("UXI"), "ux")
-    dma("a", S("UYI"), "uy")
+    dma("s", S("UI", 0, 512), "ux")
+    dma("a", S("UI", 512, 1024), "uy")
     dma("s", S("NBI"), "nb")
     dma("a", S("WW", 0, 512), "wt")
-    iota(S("ci"), [[0, 4]], 0, 1)
+    iota(S("ci", 0, 8), [[0, 8]], 0, 1)
+    iota(S("ci", 8, 16), [[1, 8]], 0, 1)
     iota(S("IX"), [[1, 256]], 0)
-    iota(S("tb", 0, 512), [[0, 128], [1, 4]], 0)
-    ts(c1("cj", 0), c1("ci", 0), 15, A.bitwise_and)
-    ts(c1("cj", 1), c1("ci", 0), 112, A.bitwise_and)
-    ts(c1("cj", 2), c1("ci", 0), 16, A.bitwise_and)
-    ts(c1("cj", 3), c1("ci", 0), 127, A.bitwise_and)
-    cp(S("col", 0, 4), S("cj"))
-    rcol, gcol, bcol, pcol = (c1("col", k) for k in range(4))
-    ts(c1("col", 4), rcol, -1.0, A.mult, 4.0, A.add)
-    ts(S("tb", 512, 1024), S("tb", 0, 512), c1("col", 4), A.is_equal)
-    tt(S("PW", 0, 512), S("tb", 512, 1024), S("PI"), A.add)
-    cp(S("bo"), S("BDI"))
-    cp(S("SP"), IND(S("PW", 0, 512), S("bo")))
-    send([(S("SP"), "PW", 512, 128, "aP")])
-    cp(S("XW", 0, 512), S("UXI"))
-    cp(S("YW", 0, 512), S("UYI"))
-    act(S("SW"), IND(S("WW", 0, 512), S("bo")), F.Copy)
-
-    def border(t, extra):
-        act(S("SXY", 256 * t, 256 * t + 128), IND(S("XW", 0, 512), S("bo")), F.Copy)
-        cp(S("SXY", 256 * t + 128, 256 * t + 256), IND(S("YW", 0, 512), S("bo")))
-        send([(blk("SXY", t, 256), "LXY", 768 * t, 256, "a%d" % t)] + extra)
-        for d in range(3):
-            o = 768 * t + 256 * d
-            act(S("XW", 512 + 128 * d, 640 + 128 * d), S("LXY", o, o + 128), F.Copy)
-            act(S("YW", 512 + 128 * d, 640 + 128 * d), S("LXY", o + 128, o + 256), F.Copy)
-    border(0, [(S("SW"), "WW", 512, 128, "aW")])
-    act(S("x16"), S("XW", 0, 512), F.Copy)
-    act(S("y16"), S("YW", 0, 512), F.Copy)
-    act(S("PV"), S("PW", 0, 512), F.Copy)
-    dma("s", S("LDI"), "ld")
-    cp(S("ld16"), S("LDI"))
-    cp(S("Lo"), S("NBI"))
-    for nm in ("XW", "YW", "PW", "WW"):
-        ms(S(nm, 896, 904), 0.0)
-    iota(S("IG"), [[16, 8], [0, 16]], 0)
-    iota(S("PR"), [[0, 8], [1, 16]], 0)
-    iota(S("H8"), [[8, 16], [0, 8]], 0)
+    for k, m in enumerate((15, 112, 127, 7, 16, 120)):
+        ts(c1("cj", k), c1("ci", 0), m, A.bitwise_and)
+    ts(c1("cj", 6), c1("ci", 0), 3, A.arith_shift_right)
+    ts(S("cj", 8, 16), S("ci", 8, 16), 7, A.bitwise_and)
+    cp(S("col", 0, 7), S("cj", 0, 7))
+    rcol, gcol, pcol, kcol, bcol, ocol, hcol = (c1("col", k) for k in range(7))
     IX = S("IX", 0, 128)
-    ts(S("RM", 0, 16), S("IX", 0, 16), rcol, A.is_equal)
-    ts(c1("RM", 16), rcol, 0.0, A.is_equal)
-    tt(S("RC", 0, 8), S("RM", 0, 8), S("RM", 8, 16), A.add)
-    tt(S("RC", 8, 24), S("RM", 0, 16), S("RM", 1, 17), A.subtract)
-    tt(S("RC", 24, 40), S("RM", 0, 16), S("RM", 1, 17), A.add)
-    ts(c1("col", 5), rcol, 8.0, A.is_ge)
-    ts(c1("col", 6), rcol, 8.0, A.is_lt, 8.0, A.mult)
-    tt(c1("col", 7), c1("col", 6), pcol, A.add)
-    ts(c1("col", 8), gcol, 15.0, A.add)
-    ts(c1("col", 9), pcol, 7.0, A.add)
-    ts(c1("col", 10), pcol, 16.0, A.add)
-    ts(c1("col", 11), c1("RM", 8), -999488.0, A.mult, 1000000.0, A.add)
-    ts(c1("col", 12), c1("col", 5), -5000.0, A.mult)
-    ts(c1("col", 13), c1("RM", 8), 5512.0, A.mult, c1("col", 12), A.add)
+    ts(S("RM"), S("IX", 0, 16), rcol, A.is_equal)
+    ts(S("col", 16, 24), S("cj", 8, 16), ocol, A.add)
+    lo8, wcol, ccol, keyc = (c1("col", k) for k in range(7, 11))
+    ts(lo8, rcol, 8.0, A.is_lt)
+    ts(wcol, lo8, -1023.0, A.mult, 1024.0, A.add)
+    ts(c1("col", 11), c1("RM", 8), 8.0, A.mult, c1("RM", 0), A.add)
+    tt(ccol, c1("col", 11), c1("RM", 4), A.add)
+    ts(keyc, kcol, -512.0, A.mult, 3584.0 - 8192.0, A.add)
+    ts(c1("col", 12), gcol, 15.0, A.add)
+    ts(c1("col", 13), pcol, 16.0, A.add)
     ts(c1("col", 14), bcol, 0.0, A.is_equal)
     ts(c1("col", 15), bcol, 16.0, A.is_equal)
-    I, NI, I32x, IBn, I896, N896, IH, I2 = (blk("IDS", k) for k in range(8))
-    for m, c in ((I, 1.0), (NI, -1.0), (I32x, 32.0), (IBn, -BIG), (I896, 896.0), (N896, -896.0), (IH, c1("col", 5)),
-                 (I2, c1("col", 6))):
+    ts(S("PW", 0, 512), S("PI"), c1("RM", 5), A.add)
+    ts(S("PW", 896, 912), S("RM"), 0.0, A.mult, c1("RM", 4), A.add)
+    ts(S("PW", 896, 912), S("PW", 896, 912), 896.0, A.mult)
+    cp(S("bo"), S("BDI"))
+    mv(S("SP"), IND(S("PW", 0, 512), S("bo")))
+    cp(S("XW", 0, 512), S("UI", 0, 512))
+    cp(S("YW", 0, 512), S("UI", 512, 1024))
+
+    def border(t, more):
+        mv(blk("SX", t), IND(S("XW", 0, 512), S("bo")))
+        mv(blk("SY", t), IND(S("YW", 0, 512), S("bo")))
+        ne = 2 if more else 4
+        send(more + [(blk("SX", t), "LX", 384 * t, 128, "ax%d" % t, ne), (blk("SY", t), "LY", 384 * t, 128, "ay%d" % t, ne)])
+        mv(S("XW", 512, 896), blk("LX", t, 384))
+        mv(S("YW", 512, 896), blk("LY", t, 384))
+    border(0, [(S("SP"), "PW", 512, 128, "aP", 4)])
+    mv(S("SW"), IND(S("WW", 0, 512), S("bo")))
+    send([(S("SW"), "WW", 512, 128, "aW", 8)])
+    for nm in ("XW", "YW", "WW"):
+        ms(S(nm, 896, 904), 0.0)
+    ms(S("one"), 1.0)
+    iota(S("IG"), [[16, 8], [0, 16]], 0)
+    iota(S("IH"), [[1, 16], [0, 8]], 0)
+    I, NI, I32x, IBn, I896, N896, ILO = (blk("IDS", k) for k in range(7))
+    for m, c in ((I, 1.0), (NI, -1.0), (I32x, 32.0), (IBn, -BIG), (I896, 896.0), (N896, -896.0), (ILO, lo8),
+                 (S("I1023"), 1023.0)):
         ts(m, IX, pcol, A.is_equal, c, A.mult)
-    I32 = S("I32")
-    ts(I32, IX, pcol, A.is_equal)
-    ts(S("GSB"), S("IX", 0, 144), c1("col", 8), A.is_equal)
-    GS = [S("GSB", 15 - r, 143 - r) for r in range(16)]
-    BO, BO4, BOn = (blk("BO", k) for k in range(3))
-    for m, c in ((BO, 1.0), (BO4, 4096.0), (BOn, -BIG)):
-        ts(m, S("IG"), gcol, A.is_equal, c, A.mult)
-    TS = [blk("TS", k) for k in range(8)]
-    SEL = [blk("SEL", k) for k in range(7)]
-    for k, (r, c) in enumerate(((0, 1.0), (0, -1.0), (8, 1.0), (8, -1.0), (1, -BIG), (2, -BIG), (3, -BIG))):
-        ts(SEL[k], BO, c1("RM", r), A.mult, c, A.mult)
-    ts(S("RC", 8, 24), S("RC", 8, 24), 511.5, A.mult)
-    ts(S("RC", 24, 40), S("RC", 24, 40), -0.5, A.mult)
-    for k in range(8):
-        act(TS[k], BOn, F.Copy, scale=c1("RC", k))
-    for r in range(16):
-        act(blk("SB", r), BO, F.Copy, scale=c1("RC", 8 + r))
-        act(blk("EE", r), GS[r % 8], F.Copy, scale=c1("RC", 24 + r))
-    ts(blk("tq", 0), S("PR"), rcol, A.is_ge, 4.0, A.mult)
-    ts(blk("tq", 1), S("PR"), 8.0, A.is_lt)
-    tt(blk("tq", 0), blk("tq", 0), BO, A.mult)
-    tt(blk("tq", 0), blk("tq", 0), blk("tq", 1), A.mult)
-    tt(S("TRI"), I2, blk("tq", 0), A.subtract)
-    ts(S("B2"), S("IX", 0, 136), c1("col", 9), A.is_equal, c1("RC", 0), A.mult)
-    B2 = [S("B2", 7 - k, 135 - k) for k in range(8)]
-    ts(S("nPV"), S("H8"), pcol, A.is_equal, -1.0, A.mult)
+    I32, NI32, RT1, RT2, RT4, SH0, SH1, BF0, BF8 = (blk("F32", k) for k in range(9))
+    mv(I32, I)
+    mv(NI32, NI)
+    for m, k in ((RT1, 1), (RT2, 2), (RT4, 4)):
+        ts(m, IX, c1("col", 16 + k), A.is_equal)
+    for k in range(1, 8):
+        ts(blk("NXR", k - 1), IX, c1("col", 16 + k), A.is_equal, -1.0, A.mult)
+    NXR = [NI] + [blk("NXR", k) for k in range(7)]
+    for h, m in enumerate((SH0, SH1)):
+        asel(m, S("one", 0, 128), [[-16, 8], [1000, 2], [-1, 8]], -1000 * h)
+    GSk = []
+    for k, c in enumerate((1.0, wcol, -4096.0, 1.0 / 16, ccol)):
+        ts(blk("GSB", k, 144), S("IX", 0, 144), c1("col", 12), A.is_equal, c, A.mult)
+        GSk.append([S("GSB", 144 * k + 15 - r, 144 * k + 143 - r) for r in range(16)])
+    GS, GSW, GSK, GS16, GSC = GSk
+    BO, BO8 = blk("BO", 0), blk("BO", 1)
+    ts(BO, S("IG"), gcol, A.is_equal)
+    ts(BO8, S("IG"), gcol, A.is_equal, lo8, A.mult)
+    for h in range(2):
+        asel(blk("BR", h, 1024), S("one"), [[-1, 8], [-16, 8], [0, 16]], -8 * h)
+    BR = [blk("BR", r) for r in range(16)]
+    NB0, NB8, NB5, NB4 = (blk("NB", k) for k in range(4))
+    for m, r, c in ((NB0, 0, -1.0), (NB8, 8, -1.0), (NB5, 5, -896.0), (NB4, 4, -1.0)):
+        ts(m, BO, c1("RM", r), A.mult, c, A.mult)
+    mv(BF0, BO, scale=c1("RM", 0))
+    mv(BF8, BO, scale=c1("RM", 8))
+    for xy in range(2):
+        asel(blk("OX", xy, 512), S("one", 0, 512), [[-32, 4], [-2, 16], [0, 8]], -xy)
+    OX = [[blk("OX", 4 * xy + j) for j in range(4)] for xy in range(2)]
+    RB = {}
+    for m, (r, h) in enumerate(((0, 0), (0, 1), (8, 0), (8, 1))):
+        RB[r, h] = blk("RB", m)
+        asel(RB[r, h], S("one", 0, 128), [[-16, 8], [1000, 2], [0, 8]], -r - 1000 * h)
+    RB8 = blk("RB", 4)
+    mv(RB8, RB[8, 1], scale=8.0)
+    for h in range(2):
+        asel(blk("HB", h), S("one", 0, 128), [[-16, 8], [0, 2], [-1, 8]], -8 * h)
+    asel(S("PGm"), S("one"), [[-16, 8], [0, 128]], 0)
+    ts(blk("TRI", 0), S("IH"), hcol, A.is_equal, -1.0, A.mult)
+    asel(blk("TRI", 1), blk("TRI", 0), [[-1, 128]], 0, A.is_ge)
+    tt(blk("TRI", 1), blk("TRI", 0), blk("TRI", 1), A.subtract)
+    TRI = blk("TRI", 1)
     ts(S("TRc"), IX, pcol, A.is_le, 4096.0, A.mult)
     ms(S("CM"), 0.0)
-    ms(S("CM", 112, 128), -1.0)
+    ms(S("CM", 112, 128), -16.0)
     for b in range(2):
-        ts(blk("SH", b, 160), S("IX", 0, 160), c1("col", 10), A.is_equal, c1("col", 14 + b), A.mult)
-    ts(S("MM"), IX, c1("col", 7), A.is_equal)
-    for t in range(3):
-        ts(blk("VJ", t), IX, 4.0, A.mult, 3.0 - t - 896.0, A.add)
-        ts(blk("ZV", t), IX, 3.0, A.mult, 3.0 - t - 648.0, A.add)
-    ts(S("DJ"), IX, 520.0, A.add)
-    ts(S("o4f"), S("IX", 0, 16), 16.0, A.mult, rcol, A.add)
-    ts(S("K16", 0, 8), S("o4f", 0, 8), 648.0, A.add, 16.0, A.mult)
-    ts(S("K16", 8, 16), S("o4f", 0, 8), 520.0, A.add, 16.0, A.mult)
-    iota(S("tb", 0, 1024), [[1, 8], [0, 128]], 0)
-    iota(S("tb", 1024, 1280), [[1, 2], [0, 128]], 0)
-    ts(S("MD"), S("tb"), rcol, A.is_equal)
-    iota(S("KC"), [[-512, 8], [0, 128]], 3584 - 8192)
-    iota(S("tb", 0, 1024), [[16, 8], [0, 128]], 0)
-    ts(S("PG"), S("tb", 0, 1024), pcol, A.is_equal)
+        ts(blk("SH", b, 160), S("IX", 0, 160), c1("col", 13), A.is_equal, c1("col", 14 + b), A.mult)
+    ts(S("MK"), S("IX", 0, 16), hcol, A.is_equal, -1.0, A.mult)
+    ts(S("dum"), S("IX", 0, 8), 16.0, A.mult, rcol, A.add)
+    ts(S("dum"), S("dum"), 520.0, A.add)
+    iota(S("tb"), [[0, 128], [1, 8]], 0)
+    ts(S("MD", 0, 1024), S("tb"), kcol, A.is_equal)
+    ts(S("MD", 1024, 1040), S("tb", 0, 16), kcol, A.is_equal)
+    iota(S("vio"), [[-1, 3], [4, 128]], 3)
+    ms(S("WV"), 0.0)
+    for u in range(8):
+        mv(S("WV", 128 * u + 112, 128 * u + 128), sub(I896, 16 * u, 16 * u + 16))
+    iota(S("Z2", 0, 2 * ZC), [[0, 2 * ZC]], 0)
+    for s in (1, 2):
+        dma("s", blk("Z2", s, 2 * ZC), S("Z2", 0, 2 * ZC))
+    dma("s", S("ZW", 0, 2 * ZC), S("Z2", 0, 2 * ZC))
+    dma("s", S("ZW", 2 * ZC, 3 * ZC), S("Z2", 0, ZC))
     ms(S("Zp"), 0.0)
-    ms(S("LT", 512, ZWID), 896.0)
+    ms(S("LT", 512, ZC), 896.0)
     for k in range(8):
         cp(S("Zp", k, 512, 16), blk("NBI", k, 32))
-    add("v", "transpose", (S("Zt"), S("Zp")), [S("Zp")], [S("Zt")], 0.05 + 256 * CY)
+    add([("v", "transpose", (S("Zt"), S("Zp")), {}, 0.05 + 256 * CY)], [S("Zp")], [S("Zt")])
     bk = bank()
     mm([(S(bk, 32 * j + 16 * b, 32 * j + 16 * b + 16),
          [(S("SH", 160 * b + 16 - 16 * (gp - b), 160 * b + 144 - 16 * (gp - b)), S("Zt", 32 * j + 16 * gp, 32 * j + 16 * gp + 16))
           for gp in range(2)]) for j in range(16) for b in range(2)])
-    act(S("LT", 0, 512), S(bk), F.Copy)
-    for k in range(8):
-        o = blk("Lo", k, 32)
-        act(blk("Q16", k, 512), IND(S("PW"), o), F.Copy)
+    mv(S("LT", 0, 512), S(bk))
     bk = bank()
-    mm([(S(bk), [(B2[k], blk("Q16", k, 512)) for k in range(8)] + [(S("nPV"), S("PV"))])])
-    act(S("sqs"), S(bk), F.Square, scale=1.0 / 32)
-    ts(S("ef"), S("LT", 0, 512), 896.0, A.is_equal)
+    mm([(S(bk, 0, 256), [(SH0, S("LT", 0, 512, 2)), (SH1, S("LT", 1, 512, 2))])])
+    cp(S("Lo"), S(bk, 0, 256))
+    ts(S("AI"), S(bk, 0, 256), 896.0, A.not_equal, 896.0, A.mult)
+    for xy in range(2):
+        cp(S("XY16", xy, 1024, 2), blk("UI", xy, 512))
+        mv(S("PI2", xy, 1024, 2), S("PW", 0, 512), scale=c1("RM", 8 * xy))
+    for src, dst, m in (("XY16", "UT", I), ("PI2", "PT", BO)):
+        for h in range(2):
+            bk = bank()
+            mm([(S(bk, 128 * u, 128 * u + 128), [(blk(src, 4 * h + u), m)]) for u in range(4)])
+            mv(blk(dst, h, 512), S(bk))
+    dma("s", S("LDI"), "ld")
+    ms(S("LD2", 0, 1024, 2), 0.0)
+    cp(S("LD2", 1, 1024, 2), S("LDI"))
+    ms(S("one", 512, 1024), 1.0 / 64)
     bk = bank()
-    mm([(S(bk), [(I, S("ef")), (S("MM"), S("sqs"))])])
-    act(blk("FF", 0, 512), S(bk), F.Copy)
+    mm([(S(bk, 128 * t + 64 * xy, 128 * t + 64 * xy + 64),
+         [(RB[8 * xy, h], S("PW", 256 * h + 3 - t, 256 * h + 256, 4)) for h in range(2)]) for t in range(3) for xy in range(2)])
+    mv(S("PVL"), S(bk, 0, 384))
+    bk = bank()
+    mm([(S(bk, 128 * t, 128 * t + 128), [(ILO, blk("vio", t))] + [(m, S("PW", 3 - t, 512, 4)) for m in (RB[0, 1], RB8, NB5)])
+        for t in range(2)])
+    mv(S("VJ", 0, 256), S(bk, 0, 256))
+    tag[0] = "pos"
+    for chunks, _, _ in GROUPS:
+        a, b = chunks[0], chunks[-1] + 1
+        gather(S("PG", 512 * a, 512 * b), IND(S("PW"), S("Lo", 32 * a, 32 * b)))
+    bk = bank()
+    mm([(S(bk), [(GSC[8 + k], S("PG", k, 4096, 8)) for k in range(8)])])
+    tt(S("LT", 0, 512), S(bk), S("LT", 0, 512), A.add)
+    for chunks, _, _ in GROUPS:
+        a, b = chunks[0], chunks[-1] + 1
+        for B in chunks:
+            for xy, nm, m in ((1, "DYT", NB8), (0, "DXT", NB0)):
+                bk = bank()
+                mm([(S(bk, 128 * j, 128 * j + 128), [(OX[xy][j], blk("PT", B)), (blk("PG", 4 * B + j), m)]) for j in range(4)])
+                mv(blk(nm, B, 512), S(bk))
+        for xy, nm in enumerate(("DXT", "DYT")):
+            act(S("sq", 256 * xy + 32 * a, 256 * xy + 32 * b), S(nm, 512 * a, 512 * b, 16), F.Square, scale=8.0)
+        tt(S("tc", 32 * a, 32 * b), S("sq", 32 * a, 32 * b), S("sq", 256 + 32 * a, 256 + 32 * b), A.add)
+        for B in chunks:
+            bk = bank()
+            mm([(S(bk, i, 512, 16), [(NI, blk("tc", B, 32))]) for i in range(16)])
+            mv(blk("NT", B, 512), S(bk))
+    for xy, nm in enumerate(("DXT", "DYT")):
+        mv(blk("dc", xy, 256), S(nm, 0, 4096, 16))
+    for u in range(16):
+        mv(blk("DD", u, 512), S("dc"), scale=c1("MK", u))
 
-    wn = [0]
-    last_w = []
-
-    def wsum(src, direct):
-        if direct:
-            last_w.append(src)
-        else:
-            dma("g", blk("wacc", wn[0] % 2, 512), src, acc=True, lat=DLAT)
-            wn[0] += 1
-
-    def compact(dst_w, src, n):
-        bk = bank()
-        mm([(S(bk, 0, dst_w), [(GS[r], S(src, r, n, 16)) for r in range(16)])])
-        return S(bk, 0, dst_w)
+    def reg(bk, k, w=128):
+        return S(bk, w * k, w * k + w)
 
     def step1(t):
         rho = 3 - t
-        if t:
-            act(S("ef"), S("LT", 0, 512), F.Relu, bias=-895.0)
-        act_ = lambda nm, o=0: S(nm, o + rho, o + 512, 4)
-        fo = 512 * (t % 2)
-        if t < 2:
-            bk = bank()
-            mm([(S(bk), [(S("TRI"), S("ef"))])])
-            act(S("FEW", fo, fo + 512), S(bk), F.Relu, scale=0.25)
+        half = lambda nm, h: S(nm, 256 * h + rho, 256 * h + 256, 4)
+        act_ = lambda nm: S(nm, rho, 512, 4)
+        for xy, nm in enumerate(("XW", "YW")):
+            mv(blk("xa", xy), act_(nm))
+        ts(blk("ef", 0), act_("LT"), 896.0, A.is_equal)
         bk = bank()
-        mm([(S(bk), [(BO, S("ef"))])])
-        act(S("HEW"), S(bk), F.Identity, bias=-1.0)
-        ts(S("U16"), act_("LT"), 512.0, A.min)
-        for k in range(8):
-            if k < TUNE["um"][t]:
-                act(blk("Um", k), S("U16"), F.Copy, scale=c1("RM", k))
-            else:
-                ts(blk("Um", k), S("U16"), c1("RM", k), A.mult)
-        cp(S("O1"), compact(64, "Um", 1024))
-        tt(S("G1"), IND(S("LT", 0, 520), S("O1")), S("MD", 128 * t, 128 * t + 1024), A.mult)
-        ts(S("O2"), compact(64, "G1", 1024), 511.0, A.min)
-        act(S("Gp1"), IND(S("PW", 0, 512), S("O2")), F.Copy)
+        mm([(reg(bk, 0), [(BO8, blk("ef", 0))])])
+        ts(S("hn"), reg(bk, 0), 0.0, A.is_equal)
         bk = bank()
-        mm([(S(bk, 0, 128), [(B2[k], blk("Gp1", k)) for k in range(8)] + [(S("nPV"), act_("PV"))])])
-        act(S("sqs", 0, 128), S(bk, 0, 128), F.Square, scale=1.0 / 32)
-        reg = lambda bk, k: S(bk, 128 * (k % 4), 128 * (k % 4) + 128)
-        prev = []
+        mm([(S(bk, 0, 64), [(SH0, half("LT", 0)), (SH1, half("LT", 1))])])
+        ts(S("O1"), S(bk, 0, 64), 512.0, A.min)
+        mv(S("UL"), S(bk, 0, 64))
+        tt(S("G1"), IND(S("LT", 0, 520), S("O1")), S("MD", t, t + 1024), A.mult)
+        bk = bank()
+        mm([(S(bk, 0, 64), [(GSW[r], S("G1", r, 1024, 16)) for r in range(16)])])
+        cp(S("CI"), S(bk, 0, 64))
+        ts(S("ib"), S("CI"), 1023, A.bitwise_and)
+        ts(S("O2"), S("ib"), 511.0, A.min)
+        cp(S("CL"), S("ib"))
+        for xy in range(2):
+            ts(blk("ia", xy, 64), S("CI"), 10 + 3 * xy, A.arith_shift_right, 7, A.bitwise_and)
+        tt(S("dL"), S("ia"), blk("PVL", t), A.subtract)
+        act(S("sqL"), S("dL"), F.Square, scale=8.0)
+        ts(S("ic"), S("CI"), 3, A.bitwise_and)
+        ts(blk("FB", 0, 64), S("ic"), float(rho), A.is_equal)
+        ts(blk("FB", 1, 64), S("CL"), 512.0, A.is_ge)
+        bk = bank()
+        mm([(reg(bk, m, 64), [(I, S("CL")), (NXR[m], S("UL"))]) for m in range(8)])
+        ts(S("EQ"), S(bk), 0.0, A.is_equal)
+        gather(S("cgy"), IND(S("YW", 0, 512), S("O2")))
+        gather(S("cgx"), IND(S("XW", 0, 512), S("O2")))
         for h in range(2):
-            ks = range(4 * h, 4 * h + 4)
             H = lambda nm: blk(nm, h, 512)
-            bk = bank()
-            mm([(reg(bk, k), [(BO, blk("G1", k)), (NI, S("U16"))]) for k in ks])
-            ts(H("EQ"), S(bk), c1("col", 11), A.min, c1("col", 13), A.is_equal)
-            for nm, s in (("CDY", 2), ("CDX", 0)):
+            for xy, nm in ((1, "CDY"), (0, "CDX")):
                 bk = bank()
-                mm([(reg(bk, k), [(SEL[s], blk("Gp1", k)), (SEL[s + 1], act_("PV"))]) for k in ks])
-                act(H(nm), S(bk), F.Copy)
-            act(S("cgy"), IND(S("YW", 0, 512), blk("O2", h, 32)), F.Copy)
-            act(S("cgx"), IND(S("XW", 0, 512), blk("O2", h, 32)), F.Copy)
+                mm([(reg(bk, k, 64), [(BR[8 * h + k], blk("dL", xy, 64))]) for k in range(8)])
+                mv(H(nm), S(bk))
+            bks = []
+            for xy, nm in ((1, "cgy"), (0, "cgx")):
+                bks.append(bank())
+                mm([(reg(bks[-1], k, 64), [(I, S(nm, 8 * h + k, 1024, 16)), (NI, blk("xa", 2 * xy + h, 64))]) for k in range(8)])
+            tt(H("cb"), S(bks[0]), H("CDY"), A.mult)
+            tt(S(bks[1]), S(bks[1]), H("CDX"), A.mult)
+            tt(S(bks[1]), S(bks[1]), H("cb"), A.add)
+            act(H("cb"), S(bks[1]), F.Abs)
             bk = bank()
-            iy = mm([(reg(bk, k), [(I, blk("cgy", k % 4)), (NI, act_("y16"))]) for k in ks])
-            tt(S("cb"), S(bk), H("CDY"), A.mult)
+            mm([(reg(bk, k, 64), [(NI32, blk("cb", 8 * h + k, 64)), (BR[8 * h + k], blk("sqL", 0, 64)),
+                                  (BR[8 * h + k], blk("sqL", 1, 64))]) for k in range(8)])
+            act(H("csg"), S(bk), F.Sign, bias=0.5)
+        bk = bank()
+        mm([(S(bk, 0, 64), [(I, S("CL"))] + [(IBn, blk("EQ", m, 64)) for m in range(8)] + [(IBn, blk("FB", m, 64)) for m in range(2)]
+             + [(GSK[r], blk("csg", r, 64)) for r in range(16)])])
+        mv(blk("KY", 0, 64), S(bk, 0, 64), bias=keyc)
+        for n, m in enumerate((RT1, RT2, RT4)):
             bk = bank()
-            mm([(reg(bk, k), [(I, blk("cgx", k % 4)), (NI, act_("x16"))]) for k in ks], after=[iy])
-            tt(S(bk), S(bk), H("CDX"), A.mult)
-            tt(S(bk), S(bk), S("cb"), A.add)
-            act(S("cab"), S(bk), F.Abs)
-            bk = bank()
-            mm([(reg(bk, k), [(I32, blk("cab", k % 4)), (TS[k], S("sqs", 0, 128))]) for k in ks])
-            act(H("csg"), S(bk), F.Sign, bias=-0.5)
-            bk = bank()
-            ik = mm([(reg(bk, k), [(BO4, blk("csg", k)), (BO, blk("G1", k)), (I, blk("KC", k)), (BOn, blk("EQ", k)),
-                                   (SEL[4 + t], blk("Gp1", k))]) for k in ks], after=prev)
-            prev = [ik]
-            if h == 0:
-                act(S("K0"), S(bk), F.Copy)
-            else:
-                tt(S("K1"), S(bk), S("K0"), A.max)
-        tt(S("K2"), blk("K1", 0, 256), blk("K1", 1, 256), A.max)
-        tt(S("best"), blk("K2", 0), blk("K2", 1), A.max)
-        cp(S("BI"), S("best"))
-        ts(S("BI"), S("BI"), 511, A.bitwise_and)
-        cp(S("c16"), S("BI"))
-        O3 = blk("OC", t, 8)
-        ts(O3, compact(8, "c16", 128), 1.0 / 16, A.mult)
-        tt(S("dd"), S("best"), act_("HEW"), A.min)
-        ts(S("t1"), S("dd"), 0.0, A.is_lt, 1024.0, A.mult)
+            mm([(S(bk, 0, 64), [(m, blk("KY", n, 64))])])
+            tt(blk("KY", n + 1, 64), S(bk, 0, 64), blk("KY", n, 64), A.max)
+        bk = bank()
+        mm([(reg(bk, h, 64), [((BF0, BF8)[h], blk("KY", 3, 64)), (IBn, blk("hn", h, 64))]) for h in range(2)])
+        cp(S("BI"), reg(bk, 0))
+        ts(S("t1"), reg(bk, 0), 0.0, A.is_lt, 1024.0, A.mult)
+        ts(S("BJ"), S("BI"), 511, A.bitwise_and)
+        cp(S("c16"), S("BJ"))
+        bk = bank()
+        mm([(S(bk, 0, 8), [(GS16[r], S("c16", r, 128, 16)) for r in range(16)])])
+        O3 = blk("O3", t, 8)
+        cp(O3, S(bk, 0, 8))
+        mv(blk("cf", 0, 8), S(bk, 0, 8))
+        tt(blk("cf", 1, 8), S("dum"), blk("cf", 0, 8), A.subtract)
         tt(S("C16"), S("c16"), S("t1"), A.add)
-        act(S("Cn"), S("C16"), F.Copy, scale=-1.0)
+        mv(S("Cn"), S("C16"), scale=-1.0)
         for h in range(2):
             bk = bank()
-            mm([(reg(bk, k), [(S("C16"), blk("PG", k)), (blk("PG", k), S("Cn")), (I, S("TRc"))]) for k in range(4 * h, 4 * h + 4)])
+            mm([(reg(bk, k % 4), [(S("C16"), blk("PGm", k)), (blk("PGm", k), S("Cn")), (I, S("TRc"))]) for k in range(4 * h, 4 * h + 4)])
             ts(blk("eq2", h, 512), S(bk), 0.0, A.is_equal)
-        tt(S("t2"), IND(S("HEW"), O3), S("dd"), A.min)
+        mv(S("LTc"), IND(S("LT", 0, 512), O3))
+        ts(blk("ef", 1), S("LTc"), 896.0, A.is_equal)
         bk = bank()
-        mm([(S(bk, 0, 128), [(S("CM", 112 - 16 * k, 240 - 16 * k), blk("eq2", k)) for k in range(8)])])
-        tt(S("t2"), S(bk, 0, 128), S("t2"), A.min)
-        ts(blk("AL", t), S("t2"), 0.0, A.is_ge)
+        mm([(reg(bk, 0), [(BO8, blk("ef", 1)), (NI, S("t1"))] + [(S("CM", 112 - 16 * k, 240 - 16 * k), blk("eq2", k)) for k in range(8)])])
+        ts(S("DN"), reg(bk, 0), 0.5, A.is_lt)
         if t < 2:
-            ts(blk("DD", t), S("t2"), 0.0, A.is_lt)
-        tt(S("Z4"), S("c16"), S("DJ"), A.subtract)
-        tt(blk("R2", 0), blk("ZV", t), blk("AL", t), A.mult)
-        tt(blk("R2", 1), S("Z4"), blk("AL", t), A.mult)
-        tt(S("o4f"), compact(16, "R2", 256), S("K16"), A.add)
-        ts(blk("O4", t, 16), S("o4f"), 1.0 / 16, A.mult)
+            ts(blk("AL", t), reg(bk, 0), 0.5, A.is_ge)
+        bk = bank()
+        mm([(S(bk, 0, 8), [(GS16[r], S("DN", r, 128, 16)) for r in range(16)])])
+        tt(blk("cf", 2, 8), S(bk, 0, 8), blk("cf", 1, 8), A.mult)
+        tt(blk("cf", 3, 8), blk("cf", 2, 8), blk("cf", 0, 8), A.add)
+        cp(blk("Oc", t, 8), blk("cf", 3, 8))
+        ts(blk("Ox", t, 8), blk("cf", 3, 8), 2.0, A.mult)
+        ts(blk("Oy", t, 8), blk("cf", 3, 8), 2.0, A.mult, 1.0, A.add)
+        mv(S("EP"), IND(S("PW", 0, 512), O3))
+        mv(blk("EWC", t), IND(S("WW", 0, 512), O3))
+        bk = bank()
+        mm([(reg(bk, xy), [(BR[8 * xy], S("EP")), ((NB0, NB8)[xy], act_("PW"))]) for xy in range(2)])
+        mv(blk("ED", t, 256), S(bk, 0, 256))
+        act(blk("ES", t, 256), S(bk, 0, 256), F.Square, scale=8.0)
         if t < 2:
-            ts(S("t1"), S("c16"), -896.0, A.add)
-            tt(S("t1"), S("t1"), act_("FEW", fo), A.mult)
-            tt(blk("NCOL", 0), S("t1"), act_("LT"), A.add)
-            act(blk("FEc", t), IND(S("FEW", fo, fo + 512), O3), F.Copy)
-            tt(S("t4"), blk("FEc", t), blk("VJ", t), A.mult)
-            tt(blk("NCOL", 1), IND(S("LT", 0, 512), O3), S("t4"), A.add)
-            cp(IND(S("LT"), blk("O4", t, 16)), S("NCOL"))
-        act(S("EP"), IND(S("PW", 0, 512), O3), F.Copy)
-        act(blk("EWC", t), IND(S("WW", 0, 512), O3), F.Copy)
-        bk = bank()
-        mm([(reg(bk, j), [(SEL[2 * j], S("EP")), (SEL[2 * j + 1], act_("PV"))]) for j in range(2)])
-        act(blk("ED", t, 256), S(bk, 0, 256), F.Copy)
-        act(blk("EN", t, 256), S(bk, 0, 256), F.Copy, scale=-1.0)
-        act(blk("ES", t, 256), S(bk, 0, 256), F.Square, scale=1.0 / 32)
-
-    def extra(s, t):
-        rho = 3 - s
-        O3 = blk("OC", s, 8)
-        act(blk("eg", 0), IND(S("XW", 0, 512), O3), F.Copy)
-        act(blk("eg", 1), IND(S("YW", 0, 512), O3), F.Copy)
-        bk = bank()
-        mm([(S(bk, 128 * j, 128 * j + 128), [(I, blk("eg", j)), (NI, S(nm, rho, 512, 4))]) for j, nm in enumerate(("x16", "y16"))])
-        tt(S("EA"), S(bk, 0, 256), blk("ED", s, 256), A.mult)
-        tt(S("EZ"), blk("EA", 0), blk("EA", 1), A.add)
-        if s < t:
-            tt(S("EZ"), S("EZ"), blk("EQq", s), A.add)
-        act(S("esg"), S("EZ"), F.Sign)
-        act(S("eab"), S("EZ"), F.Abs)
-        bk = bank()
-        mm([(S(bk, 0, 128), [(I32, S("eab")), (IBn, blk("ES", 2 * s)), (IBn, blk("ES", 2 * s + 1))]
-             + ([(IBn, blk("DD", s))] if s < t else []))])
-        ts(S("em"), S(bk, 0, 128), 0.0, A.max, 1023.0, A.min)
-        if s < t:
-            act(S("enz"), S("em"), F.Sign)
             bk = bank()
-            mm([(S(bk, 0, 128), [(BO, S("enz"))])])
-            ts(blk("AL", s), S(bk, 0, 128), 4.0, A.is_ge)
-            if t < 2:
-                ts(blk("DD", s), S(bk, 0, 128), 4.0, A.is_lt)
-        tt(S("em"), S("em"), blk("AL", s), A.mult)
-        tt(blk("EQq", s), S("em"), S("esg"), A.mult)
-        oc = S("O4", 16 * s + 8, 16 * s + 16)
-        zs = []
-        if s == t:
-            macc = S("em") if t == 2 else blk("EM", s)
-            if t < 2:
-                act(macc, blk("EQq", s), F.Abs)
-        else:
-            macc = blk("EM", s)
-            tt(macc, macc, S("em"), A.add)
-        for j, (src, cv, cc) in enumerate(((blk("EQq", s), blk("ED", 2 * s), blk("EN", 2 * s)),
-                                           (blk("EQq", s), blk("ED", 2 * s + 1), blk("EN", 2 * s + 1)),
-                                           (macc, blk("EWC", s), S("WW", rho, 512, 4)))[:3 if t == 2 else 2]):
-            o = ZC * (3 * s + j)
-            if s == t or j == 2:
-                iota(S("ZZ", o, o + ZC), [[0, ZC]], 0)
-            tt(S("ZZ", o + rho, o + 512, 4), src, cv, A.mult)
-            tt(IND(S("ZZ", o, o + ZC), oc), src, cc, A.mult)
-            zs.append(S("ZZ", o, o + 512))
-        for j, acc in enumerate(("xacc", "yacc")):
-            if s < t and TUNE["dsum"][j]:
-                dma("g", blk(acc, s, 512), zs[j], acc=True, lat=DLAT)
-            else:
-                mm([(S("@%d" % j), [(I32, zs[j])])], start=False, stop=s == t)
-        if t == 2:
-            wsum(zs[2], s == 2)
-        if s == 0 and t == 1:
-            ts(S("t1"), blk("DD", 0), 896.0, A.mult)
-            tt(blk("t3", 0), S("t1"), S("FEW", 3, 512, 4), A.mult)
-            tt(blk("t3", 1), S("t1"), blk("FEc", 0), A.mult)
-            tt(S("NCOL"), IND(S("LT"), blk("O4", 0, 16)), S("t3"), A.max)
-            cp(IND(S("LT"), blk("O4", 0, 16)), S("NCOL"))
+            mm([(reg(bk, u), [(I, blk("ef", u)), (TRI, blk("ef", u)), (IBn, S("DN"))]) for u in range(2)])
+            relu(blk("FE", t, 256), S(bk, 0, 256))
+            bk = bank()
+            mm([(reg(bk, 0), [(ILO, S("c16"))] + [(m, S("EP")) for m in (RB[0, 1], RB8, NB5)])])
+            tt(S("NV"), reg(bk, 0), blk("FE", 2 * t), A.mult)
+            tt(blk("NC", 0), blk("FE", 2 * t + 1), blk("VJ", t), A.mult)
+            tt(blk("NC", 1), blk("NC", 0), S("LTc"), A.add)
+            cp(IND(S("LT"), blk("Oc", t, 8)), blk("NC", 1))
+            tt(act_("LT"), act_("LT"), S("NV"), A.add)
 
-    def chunk(t, k):
-        n = 8 * t + k
-        R = lambda nm: blk(nm, n % (_B[nm][0] // 512), 512)
-        C = lambda nm: blk(nm, k, 512)
-        sg = R("sg")
-        o = blk("Lo", k, 32)
+    def extra(s0, s1, t):
+        ss = range(s0, s1)
+        n = 128 * len(ss)
+        for xy, nm in enumerate(("XW", "YW")):
+            mv(S("eg", 256 * xy, 256 * xy + n), IND(S(nm, 0, 512), S("O3", 8 * s0, 8 * s1)))
+        bk = bank()
+        mm([(reg(bk, 2 * u + xy), [(I, blk("eg", 2 * xy + u)), (NI32, S(nm, 3 - s, 512, 4))])
+            for u, s in enumerate(ss) for xy, nm in enumerate(("XW", "YW"))])
+        tt(S("EA", 0, 2 * n), S(bk, 0, 2 * n), S("ED", 256 * s0, 256 * s1), A.mult)
+        bz = bank()
+        mm([(reg(bz, u), [(I32, blk("EA", 2 * u)), (I32, blk("EA", 2 * u + 1))] + ([(I32, blk("EQq", s))] if s < t else []))
+            for u, s in enumerate(ss)])
+        act(S("eab", 0, n), S(bz, 0, n), F.Abs)
+        act(S(bz, 0, n), S(bz, 0, n), F.Sign)
+        bk = bank()
+        mm([(reg(bk, u), [(I32, blk("eab", u)), (NI, blk("ES", 2 * s)), (NI, blk("ES", 2 * s + 1))]
+             + ([(IBn, S("DN"))] if s == t else [])) for u, s in enumerate(ss)])
+        em = S("EM", 384 * t + 128 * s0, 384 * t + 128 * s1)
+        al = S("AL", 128 * s0, 128 * s1)
+        if s0 == t:
+            ts(em, S(bk, 0, n), 0.0, A.max, 1023.0, A.min)
+        else:
+            ts(S("em", 0, n), S(bk, 0, n), 0.0, A.max, 1023.0, A.min)
+            nonzero(S("enz", 0, n), S("em", 0, n))
+            bk = bank()
+            mm([(S(bk, 0, n), [(BO, S("enz", 0, n)), (I32x, al)])])
+            ts(al, S(bk, 0, n), 35.5, A.is_ge)
+            tt(em, S("em", 0, n), al, A.mult)
+        tt(S("EQq", 128 * s0, 128 * s1), S(bz, 0, n), em, A.mult)
+        mv(S("nq", 128 * s0, 128 * s1), S("EQq", 128 * s0, 128 * s1), scale=-1.0)
+        for s in ss:
+            o = 2 * ZC * s
+            for xy, off in enumerate(("Ox", "Oy")):
+                tt(S("Z2", o + 2 * (3 - s) + xy, o + 1024, 8), blk("EQq", s), blk("ED", 2 * s + xy), A.mult)
+                tt(IND(S("Z2", o, o + 2 * ZC), blk(off, s, 8)), blk("nq", s), blk("ED", 2 * s + xy), A.mult)
+        if t == 2:
+            bk = bank()
+            mm([(reg(bk, u), [(I, blk("EM", 3 * r + s)) for r in range(s, 3)]) for u, s in enumerate(ss)])
+            mv(S("EMs", 128 * s0, 128 * s1), S(bk, 0, n))
+            for s in ss:
+                o = ZC * s
+                tt(S("ZW", o + 3 - s, o + 512, 4), blk("EMs", s), blk("EWC", s), A.mult)
+                tt(IND(S("ZW", o, o + ZC), blk("Oc", s, 8)), blk("EMs", s), S("WW", 3 - s, 512, 4), A.mult)
+        if s0 == 0 and t == 1:
+            bk = bank()
+            mm([(reg(bk, u), [(I896, blk("FE", u)), (N896, blk("AL", 0))]) for u in range(2)])
+            tt(S("LT", 3, 512, 4), reg(bk, 0), S("LT", 3, 512, 4), A.max)
+            mv(blk("NC", 0), IND(S("LT"), blk("Oc", 0, 8)))
+            tt(blk("NC", 1), reg(bk, 1), blk("NC", 0), A.max)
+            cp(IND(S("LT"), blk("Oc", 0, 8)), blk("NC", 1))
+
+    def group(t, chunks, dma1, dma2, acc, wb):
+        a, b = chunks[0], chunks[-1] + 1
+        def R(nm, lo=a, hi=b):
+            o = (8 * t + lo) % (_B[nm][0] // 512)
+            return S(nm, 512 * o, 512 * (o + hi - lo))
+        C = lambda nm, B: blk(nm, B, 512)
+        gather(R("gy"), IND(S("YW"), S("Lo", 32 * a, 32 * b)))
+        gather(R("gx"), IND(S("XW"), S("Lo", 32 * a, 32 * b)))
+        for B in chunks:
+            bks = []
+            for xy, nm in ((1, "gy"), (0, "gx")):
+                bks.append(S(bank()))
+                g_ = R(nm, B, B + 1)
+                mm([(reg(bks[-1][1], j), [(OX[xy][j], blk("UT", B)), (sub(g_, 128 * j, 128 * j + 128), NI)]) for j in range(4)])
+            tt(R("PB", B, B + 1), bks[0], C("DYT", B), A.mult)
+            more = ([] if dma1 else [R("PB", B, B + 1)]) + ([C("Q16", B)] if t else [])
+            tt(bks[1] if more else R("ZB", B, B + 1), bks[1], C("DXT", B), A.mult)
+            for m, x in enumerate(more):
+                tt(bks[1] if m + 1 < len(more) else R("ZB", B, B + 1), bks[1], x, A.add)
+        if dma1:
+            dma("g", R("ZB"), R("PB"), acc=True, lat=DLAT)
+        act(R("PB"), R("ZB"), F.Abs)
+        if dma2:
+            dma("g", R("PB"), S("NT", 512 * a, 512 * b), acc=True, lat=DLAT)
+            relu(R("R0"), R("PB"))
+        else:
+            for B in chunks:
+                bk = S(bank())
+                mm([(bk, [(I32, R("PB", B, B + 1)), (I, C("NT", B))])])
+                relu(R("R0", B, B + 1), bk)
+        nonzero(R("NZ"), R("R0"))
+        n = 32 * len(chunks)
+        bk = bank()
+        nz = R("NZ")
+        mm([(S(bk, 0, n), [(I, sub(nz, i, 16 * n, 16)) for i in range(16)]
+             + ([(I32x, S("SS", 256 * t - 256 + 32 * a, 256 * t - 256 + 32 * b))] if t else []))], stop=t > 0)
         if t == 0:
-            for nm, s in (("DY", 2), ("DX", 0)):
-                bk = bank()
-                mm([(S(bk), [(SEL[s], C("Q16")), (SEL[s + 1], S("PV"))])])
-                act(C(nm), S(bk), F.Copy)
-        act(R("gy"), IND(S("YW"), o), F.Copy)
-        act(R("gx"), IND(S("XW"), o), F.Copy)
-        bk = S(bank())
-        iy = mm([(bk, [(I, R("gy")), (NI, S("y16"))])])
-        tt(R("bb"), bk, C("DY"), A.mult)
-        bk = S(bank())
-        mm([(bk, [(I, R("gx")), (NI, S("x16"))])], after=[iy])
-        tt(bk, bk, C("DX"), A.mult)
-        tt(bk, bk, R("bb"), A.add)
-        if t:
-            tt(bk, bk, C("Q16"), A.add)
-        act(R("ab"), bk, F.Abs)
-        act(sg, bk, F.Sign)
-        bk = S(bank())
-        mm([(bk, [(I32, R("ab")), (TS[k], blk("FF", t, 512))])])
-        act(R("r16"), bk, F.Relu)
-        if n not in TUNE["nzv"]:
-            act(R("nz"), R("r16"), F.Sign)
-        else:
-            ts(R("nz"), R("r16"), 0.0, A.is_gt)
-        bn = bank()
-        z0 = R("nz")[2]
-        mm([(S(bn, 0, 256), [(GS[k], S("nz", z0, z0 + 256)), (GS[8 + k], S("nz", z0 + 256, z0 + 512))])])
-        z0 = R("r16")[2]
-        act(blk("AS", k, 256), S(bn, 0, 256), F.Sign, bias=-3.5)
-        bn = bank()
-        bk = S(bn)
-        if t == 2 or n in TUNE["mina"]:
-            def less(bn, more):
-                mm([(S(bn, 256 * h, 256 * h + 256), [(blk("SB", 8 * h + k), blk("AS", k, 256)),
-                                                     (NI, S("r16", z0 + 256 * h, z0 + 256 * h + 256))]
-                     + [(I, blk("MQ", 16 * u + 2 * k + h, 256)) for u in more]) for h in range(2)])
-            less(bn, ())
-            act(R("r16"), bk, F.Relu)
+            mm([(S(bk, 8 * u, 8 * u + 8), [(blk("PG", 4 * a + u), sub(NB4, 0, 128, 16))]) for u in range(n // 8)], start=False, stop=False)
+            mm([(S(bk, 0, n), [(I32x, S("one", 512, 512 + n))])], start=False)
+        stay = ts(S("SS", 256 * t + 32 * a, 256 * t + 32 * b), S(bk, 0, n), 35.5 if t else 4.0, A.is_ge)
+        for B in chunks:
+            bk = bank()
+            mm([(S(bk, i, 512, 16), [(S("I1023"), blk("SS", 8 * t + B, 32))]) for i in range(16)])
+            r = C("RR", 8 * t + B) if t < 2 else R("R2", B, B + 1)
+            tt(r, S(bk), R("R0", B, B + 1), A.min)
+            bk = bank()
+            add([a_act(S(bk), R("ZB", B, B + 1), F.Sign)], [R("ZB", B, B + 1)], [S(bk)], after=[stay])
+            tt(C("Q16", B), S(bk), r, A.mult)
+            if B % 4 == 0:
+                h = B // 4
+                acc.append(bank())
+                mm([(S(acc[h]), [(I32x, blk("UT", h, 512))])], stop=False)
+                mm([(reg(acc[h], u), [(blk("LD2", 4 * h + u), I)]) for u in range(4)], start=False, stop=False)
+            o = 128 * (B % 4)
+            mm([(S(acc[B // 4], o + 16 * g, o + 16 * g + 16, 1, (32 * j, 32 * j + 32, 1)),
+                 [(S("DD", 32 * B + 8 * j + g, 8192, 256), blk("Q16", 32 * B + 8 * j + g, 16))])
+                for j in range(4) for g in range(8)], start=False, stop=False)
             if t == 2:
-                act(R("pw"), IND(S("WW"), o), F.Copy)
-                bn = bank()
-                less(bn, (0, 1))
-                dst = blk("wacc", k, 512) if k < 2 else R("pw")
-                tt(dst, S(bn), R("pw"), A.mult)
-                if k >= 2:
-                    wsum(dst, k >= 6)
-            bn = bank()
-            bk = S(bn)
-            less(bn, ())
-        else:
-            mm([(S(bn, 256 * h, 256 * h + 256), [(blk("SB", 8 * h + k), blk("AS", k, 256))]) for h in range(2)])
-            tt(bk, bk, R("r16"), A.min)
-        if t < 2:
-            tt(C("Q16"), bk, sg, A.mult)
-            keep = grp[0]
-            grp[0] = (100.0 * (t + 1) + TUNE["mq"], 1.0)
-            act(blk("MQ", 8 * t + k, 512), C("Q16"), F.Abs)
-            grp[0] = keep
-            bk = S(bank())
-            mm([(bk, [(I, C("Q16"))])])
-        else:
-            tt(bk, bk, sg, A.mult)
-        for j, (pp, d, acc) in enumerate((("ppx", "DX", "xacc"), ("ppy", "DY", "yacc"))):
-            last = TUNE["dsum"][j]
-            if k < 2 and last:
-                tt(blk(acc, k, 512), bk, C(d), A.mult)
-            else:
-                tt(R(pp), bk, C(d), A.mult)
-                if k < last:
-                    dma("g", blk(acc, k % 2, 512), R(pp), acc=True, lat=DLAT)
-                else:
-                    mm([(S("@%d" % j), [(I32, R(pp))])], start=False, stop=False)
-            if k == 7 and last:
-                for h in range(2):
-                    mm([(S("@%d" % j), [(I32, blk(acc, h, 512))])], start=False, stop=False)
+                bk = bank()
+                mm([(reg(bk, j), [(blk("RR", 32 * u + 4 * B + j), I) for u in range(2)]
+                     + [(sub(r, 128 * j, 128 * j + 128), I)]) for j in range(4)])
+                pp = blk("PP", B % 2, 512)
+                gather(pp, IND(S("WW"), blk("Lo", B, 32)))
+                tt(pp, S(bk), pp, A.mult)
+                if B % 4 == 0:
+                    wb.append(bank())
+                mm([(reg(wb[-1], B % 4, 64), [(I32, sub(pp, k, 512, 8)) for k in range(8)])])
+
+    def update(t, h, acc):
+        for s in range(t + 1):
+            o = 2 * ZC * s + 512 * h
+            mm([(reg(acc[h], u), [(S("Z2", o + 128 * u, o + 128 * u + 128), I32)]) for u in range(4)], start=False, stop=False)
+        mm([(S(acc[h]), [(I32x, S("one", 512, 1024))])], start=False)
+        ts(blk("UI", h, 512), S(acc[h]), 1.0 / 32, A.mult)
+        ts(blk("UT", h, 512), blk("UI", h, 512), -1023.0, A.max, 1023.0, A.min)
+        for xy, nm in enumerate(("XW", "YW")):
+            bk = bank()
+            mm([(reg(bk, u, 64), [(blk("UT", 4 * h + u), sub(I, xy, 128, 2))]) for u in range(4)])
+            mv(blk(nm, h, 256), S(bk, 0, 256))
+            if t == 2:
+                dma("sa"[xy], ("y" + "xy"[xy], 256 * h, 256 * h + 256), blk(nm, h, 256))
 
     for t in range(3):
-        mm([(S("@0"), [(I32x, S("x16"))])], stop=False)
-        mm([(S("@1"), [(I32x, S("y16")), (I, S("ld16"))])], stop=False)
-        t0 = 100.0 * (t + 1)
-        grp[0] = (t0 + TUNE["s1"][0], TUNE["s1"][1])
+        tag[0] = "s1_%d" % t
         step1(t)
-        for k in range(8):
-            grp[0] = (t0 + TUNE["per"] * k, TUNE["cs"])
-            chunk(t, k)
-            if 2 <= k < 2 + t:
-                grp[0] = (t0 + TUNE["ex"] * (k - 2) - 1.0, TUNE["cs"])
-                extra(k - 2, t)
-        grp[0] = (t0 + TUNE["exn"], 1.0)
-        extra(t, t)
-        grp[0] = (t0 + 50.0, 0.01)
-        if t < 2:
-            bn = bank()
-            mm([(S(bn, 256 * h, 256 * h + 256), [(blk("EE", 8 * h + k), blk("AS", k, 256)) for k in range(8)]
-                 + [(IH, S("FF", 512 * t + 256 * h, 512 * t + 256 * h + 256))]) for h in range(2)])
-            act(blk("FF", t + 1, 512), S(bn), F.Copy)
-            bn = bank()
-            mm([(S(bn), [(I896, blk("FF", t + 1, 512)), (N896, blk("FF", t, 512))])])
-            tt(S("LT", 0, 512), S(bn), S("LT", 0, 512), A.max)
-        for bn, ti, wi, h in (("@0", "UXI", "XW", "x16"), ("@1", "UYI", "YW", "y16")):
-            ts(S(ti), S(bn), 0.5, A.add, 1.0 / 32, A.mult)
-            ts(S(wi, 0, 512), S(ti), -1023.0, A.max, 1023.0, A.min)
-            if t < 2:
-                act(S(h), S(wi, 0, 512), F.Copy)
+        tag[0] = "ex_%d" % t
+        if t:
+            extra(0, t, t)
+        extra(t, t + 1, t)
+        if t == 2:
+            bk = bank()
+            mm([(S(bk), [(I32, S("ZW", ZC * s, ZC * s + 512)) for s in range(3)])])
+            mv(S("WX"), S(bk))
+        acc, wb = [], []
+        for chunks, dma1, dma2 in GROUPS:
+            tag[0] = "m%d_%d" % (t, chunks[0])
+            group(t, chunks, dma1, dma2, acc, wb)
+        tag[0] = "up_%d" % t
+        for h in range(2):
+            update(t, h, acc)
         if t < 2:
             border(t + 1, [])
-    dma("s", "yx", S("XW", 0, 512))
-    dma("s", "yy", S("YW", 0, 512))
-    bk = S(bank())
-    terms = [blk("wacc", 0, 512), blk("wacc", 1, 512), last_w[2], last_w[0], last_w[1]]
-    for m, x in enumerate(terms):
-        mm([(bk, [(I32, x)])], start=m == 0, stop=m == 4)
-    act(S("wout"), bk, F.Copy)
-    dma("s", "yw", S("wout"))
+            bk = bank()
+            mm([(S(bk, u, 256, 8), [(S("WV", 128 * u + 112 - 16 * g, 128 * u + 240 - 16 * g), S("SS", 256 * t + g, 256 * t + 256, 8))
+                                    for g in range(8)]) for u in range(8)])
+            tt(blk("ND", t, 256), S("AI"), S(bk, 0, 256), A.subtract)
+            if t == 0:
+                tt(S("AI"), S("AI"), blk("ND", 0, 256), A.subtract)
+            bk = bank()
+            mm([(S(bk, h, 512, 2), [(blk("HB", h), blk("ND", t, 256))]) for h in range(2)])
+            tt(S("LT", 0, 512), S(bk), S("LT", 0, 512), A.max)
+    for h in range(2):
+        tt(blk("wout", h, 256), S(wb[h], 0, 256), blk("WX", h, 256), A.add)
+        dma("s", ("yw", 256 * h, 256 * h + 256), blk("wout", h, 256))
     return ops
 
 
-def schedule(ops):
-    n = len(ops)
-    summand = lambda o: o["kind"] == "mm" and not o["args"][1] and not o["args"][2]
-    hist = {}
-    deps = []
-    users = {}
+def depend(ops):
+    is_mm = lambda o: o["alts"][0][1] == "mm"
+    summand = lambda o: is_mm(o) and not o["alts"][0][2][1] and not o["alts"][0][2][2]
+    hist, deps, users = {}, [], {}
     for i, o in enumerate(ops):
         d = dict((j, True) for j in o["after"])
         acc = [(x, False) for x in o["rd"]] + [(x, True) for x in o["wr"]]
         for x, w in acc:
             nm = x[1]
             ps = nm[0] == "@"
-            lo, hi = (0, 512) if ps else (x[2], x[3])
-            for (j, a, b, wj) in hist.get(nm, ()):
-                if j == i or b <= lo or hi <= a:
+            for (j, a, b, wj, pj) in hist.get(nm, ()):
+                if j == i:
                     continue
-                if ps and summand(o) and summand(ops[j]):
-                    continue
-                if x[5] is not None and ops[j]["wr"] and ops[j]["wr"][0][5] not in (None, x[5]):
-                    continue
-                same = ops[j]["eng"] == o["eng"] and ops[j]["kind"] != "dma" and o["kind"] != "dma"
-                if wj and not w:
-                    d[j] = True
-                elif wj or w:
-                    d[j] = d.get(j, False) or not (same and ps and o["eng"] == "t")
-                elif ps and not same:
+                if ps:
+                    if not (summand(o) and summand(ops[j])):
+                        d[j] = d.get(j, False) or not (is_mm(o) and is_mm(ops[j]))
+                elif b > x[2] and x[3] > a and (w or wj) and (pj is None or x[5] is None or pj == x[5]):
                     d[j] = True
             if ps:
                 users.setdefault(nm, set()).add(i)
         for x, w in acc:
-            nm = x[1]
-            lo, hi = (0, 512) if nm[0] == "@" else (x[2], x[3])
-            h = hist.setdefault(nm, [])
-            if w and x[4] == 1 and x[5] is None and nm[0] != "@":
-                h[:] = [e for e in h if not (lo <= e[1] and e[2] <= hi)]
-            h.append((i, lo, hi, w))
+            h = hist.setdefault(x[1], [])
+            if w and x[4] == 1 and x[5] is None and x[1][0] != "@":
+                h[:] = [e for e in h if not (x[2] <= e[1] and e[2] <= x[3])]
+            h.append((i, x[2], x[3], w, x[5]))
         deps.append(d)
+    return deps, users
+
+
+def schedule(ops, tries):
+    n = len(ops)
+    deps, users = depend(ops)
     succ = [[] for _ in range(n)]
     for i in range(n):
         for j in deps[i]:
             succ[j].append(i)
     pr = [0.0] * n
     for i in range(n - 1, -1, -1):
-        pr[i] = ops[i]["cost"] + ops[i]["lat"] + max([pr[j] + HOP for j in succ[i]] + [0.0])
-    head = [0.0] * n
-    for i in range(n):
-        base, stretch = ops[i]["grp"]
-        head[i] = max([head[j] + ops[j]["cost"] + ops[j]["lat"] + HOP for j in deps[i] if ops[j]["grp"] == ops[i]["grp"]] + [0.0])
-        if base:
-            pr[i] = -(base + stretch * head[i])
+        pr[i] = ops[i]["alts"][0][4] + ops[i]["lat"] + max([pr[j] + HOP for j in succ[i]] + [0.0])
     rng = np.random.default_rng(1)
     best = place(ops, deps, succ, users, pr)
-    for _ in range(TUNE["tries"]):
+    for _ in range(tries):
         q = list(pr)
         for _r in range(3):
             a = int(rng.integers(0, n))
@@ -674,7 +720,7 @@ def schedule(ops):
             for i in range(a, min(n, a + int(rng.integers(1, 40)))):
                 q[i] += d
         new = place(ops, deps, succ, users, q)
-        if max(new[3]) <= max(best[3]):
+        if new is not None and (best is None or max(new[3]) <= max(best[3])):
             best, pr = new, q
     return best
 
@@ -682,12 +728,14 @@ def schedule(ops):
 def place(ops, deps, succ, users, pr):
     n = len(ops)
     deps = [dict(d) for d in deps]
-    first = dict((min(u), nm) for nm, u in users.items() if nm not in ("@0", "@1"))
+    first = dict((min(u), nm) for nm, u in users.items())
     left = dict((nm, len(u)) for nm, u in users.items())
+    banks = [set(x[1] for x in o["rd"] + o["wr"] if x[1][0] == "@") for o in ops]
     waiting = sorted(first)
-    phys = {"@0": 0, "@1": 1}
-    free = dict((b, (0.0, [])) for b in range(2, 8))
+    phys = {}
+    free = dict((b, (0.0, [])) for b in range(8))
     fin = [None] * n
+    way = [None] * n
     cnt = [len(deps[i]) for i in range(n)]
     ready = [i for i in range(n) if cnt[i] == 0]
     est = dict((i, 0.0) for i in ready)
@@ -695,36 +743,46 @@ def place(ops, deps, succ, users, pr):
     order = []
     while ready:
         cand = []
+        fb = min(v[0] for v in free.values()) if free else 0.0
         for i in ready:
-            s = max(est[i], efree[ops[i]["eng"]])
+            s = est[i]
             if i in first:
-                if len(free) < (1 if i == waiting[0] else 2):
+                if len(free) < (1 if i == waiting[0] else 3):
                     continue
-                s = max(s, min(v[0] for v in free.values()))
-            cand.append((s, i))
-        s0, i0 = min(cand)
-        e = ops[i0]["eng"]
-        s, i = max(((s, i) for s, i in cand if ops[i]["eng"] == e and s <= s0 + TUNE["win"]), key=lambda c: pr[c[1]])
+                s = max(s, fb)
+            alts = ops[i]["alts"]
+            own = max(s, efree[alts[0][0]])
+            cand.append((own, i, alts[0]))
+            for alt in alts[1:]:
+                if max(s, efree[alt[0]]) + alt[4] + MARGIN < own + alts[0][4]:
+                    cand.append((max(s, efree[alt[0]]), i, alt))
+        if not cand:
+            return None
+        s0, _, alt0 = min(cand, key=lambda c: c[0])
+        e = alt0[0]
+        s, i, alt = max((c for c in cand if c[2][0] == e and c[0] <= s0 + 0.05),
+                        key=lambda c: pr[c[1]] - (0.0 if c[2] is ops[c[1]]["alts"][0] else 3.0))
         if i in first:
             b = min(free, key=lambda k: free[k][0])
             for j in free.pop(b)[1]:
                 deps[i][j] = True
             phys[first[i]] = b
             waiting.remove(i)
-        efree[e] = s + ops[i]["cost"]
+        efree[e] = s + alt[4]
         fin[i] = efree[e] + ops[i]["lat"]
+        way[i] = alt
         order.append(i)
         ready.remove(i)
-        for nm in set(x[1] for x in ops[i]["rd"] + ops[i]["wr"] if x[1][0] == "@"):
+        for nm in banks[i]:
             left[nm] -= 1
-            if left[nm] == 0 and nm not in ("@0", "@1"):
+            if left[nm] == 0:
                 free[phys[nm]] = (max(fin[j] for j in users[nm]) + HOP, list(users[nm]))
         for j in succ[i]:
             cnt[j] -= 1
             if cnt[j] == 0:
                 est[j] = max(fin[k] + (HOP if deps[j][k] else 0.0) for k in deps[j])
                 ready.append(j)
-    return order, deps, phys, fin
+    return order, deps, phys, fin, way
 
 
 PLAN = []
@@ -736,12 +794,15 @@ def rank_program(g, core, T, topo):
         return
     if not PLAN:
         ops = build()
-        PLAN.append((ops,) + schedule(ops))
-    ops, order, deps, phys, fin = PLAN[0]
+        PLAN.append((ops,) + schedule(ops, TRIES))
+    ops, order, deps, phys, fin, way = PLAN[0]
     N = len(T.cores)
     peers = [T.cores[(rank + d) % N] for d in range(1, N)]
     eng = [e for e in topo.engines(core, peers[0]) if all(e in topo.engines(core, p) for p in peers)]
     queue = {"t": g.tensor, "v": g.vector, "a": g.scalar, "g": g, "s": g.sync}
+    call = {"tensor_tensor": g.vector.tensor_tensor, "tensor_scalar": g.vector.tensor_scalar,
+            "tensor_copy": g.vector.tensor_copy, "memset": g.vector.memset, "transpose": g.vector.transpose,
+            "activation": g.scalar.activation, "iota": g.iota, "affine_select": g.affine_select}
 
     def ap(x):
         if not is_ap(x):
@@ -752,6 +813,11 @@ def rank_program(g, core, T, topo):
         p = slice(None) if x[5] is None else slice(*x[5])
         return T[nm][p, o + x[2]:o + x[3]] if x[4] == 1 else T[nm][p, o + x[2]:o + x[3]:x[4]]
 
+    def side(x):
+        if is_ap(x):
+            return ap(x)
+        return T[x[0]][:, x[1]:x[2]] if isinstance(x, tuple) else T[x][:]
+
     mark = {}
     clock = {}
     known = dict((e, {}) for e in queue)
@@ -759,10 +825,9 @@ def rank_program(g, core, T, topo):
     total = {}
     sent = 0
     for i in order:
-        o = ops[i]
-        e = o["eng"]
+        e, kind, a, kw, _ = way[i]
         if e == "r":
-            mark[i] = (o["args"][0], (N - 1) * (len(eng) // o["args"][1]))
+            mark[i] = (a[0], (N - 1) * a[1])
             clock[i] = {mark[i][0]: mark[i][1]}
             total[mark[i][0]] = mark[i][1]
             continue
@@ -776,37 +841,32 @@ def rank_program(g, core, T, topo):
                 kn[sem] = val
             for s, v in clock[j].items():
                 kn[s] = max(kn.get(s, 0), v)
-        a = o["args"]
-        if o["kind"] == "send":
-            parts = a[0]
-            per = len(eng) // len(parts)
+        if kind == "send":
             trs = []
-            for m, (src, nm, c0, w, sem) in enumerate(parts):
+            used = 0
+            for src, nm, c0, w, sem, ne in a[0]:
                 ids, dsts = [], []
                 for d, p in enumerate(peers):
                     rid, pid = topo.addr(p, core)
                     ids.append(DstId(rid=rid, pnc=pid))
-                    dsts.append(T[nm][:, c0 + d * w:c0 + (d + 1) * w])
-                trs.append(RemoteDMATransfer(dst_ids=ids, dma_engine_mask=sum(1 << x for x in eng[m * per:(m + 1) * per]),
+                    dsts.append(ap(S(nm, c0 + d * w, c0 + (d + 1) * w)))
+                trs.append(RemoteDMATransfer(dst_ids=ids, dma_engine_mask=sum(1 << x for x in eng[used:used + ne]),
                                              remote_sem=T.sem[sem], src=ap(src), dsts=dsts))
+                used += ne
             g.remote_dma_fused(trs, local_sem=T.sem.ls)
-            sent += per * len(parts)
+            sent += used
             continue
-        if o["kind"] == "dma":
-            kw = {"accum_op": A.add} if a[2] else {}
-            q.dma_start(*[ap(x) if is_ap(x) else T[x][:] for x in a[:2]], **kw).then_inc(T.sem[a[3]], 16)
+        if kind == "dma":
+            q.dma_start(side(a[0]), side(a[1]), **({"accum_op": A.add} if a[2] else {})).then_inc(T.sem[a[3]], 16)
             mark[i] = (a[3], 16)
             total[a[3]] = 16
         else:
-            if o["kind"] == "mm":
+            if kind == "mm":
                 for out, terms in a[0]:
                     for m, (l, r) in enumerate(terms):
                         ins = q.matmul(ap(out), ap(l), ap(r), a[1] and m == 0, a[2] and m == len(terms) - 1)
             else:
-                fn = {"tensor_tensor": g.vector.tensor_tensor, "tensor_scalar": g.vector.tensor_scalar,
-                      "tensor_copy": g.vector.tensor_copy, "memset": g.vector.memset, "transpose": g.vector.transpose,
-                      "activation": g.scalar.activation, "iota": g.iota}[o["kind"]]
-                ins = fn(*[ap(x) for x in a], **dict((k, ap(v)) for k, v in o["kw"].items()))
+                ins = call[kind](*[ap(x) for x in a], **dict((k, ap(v)) for k, v in kw.items()))
             count[e] += 1
             ins.then_inc(T.sem["q" + e], 1)
             mark[i] = ("q" + e, count[e])

@@ -6,33 +6,34 @@ f32, f16, b16, i32, u16 = "float32", "float16", "bfloat16", "int32", "uint16"
 ZC = 648
 _B = {
     "XW": (904, f32), "YW": (904, f32), "WW": (904, f32), "PW": (912, b16), "UT": (1024, f16), "LD2": (1024, f16),
-    "DXT": (4096, b16), "DYT": (4096, b16), "NT": (4096, b16), "DD": (8192, b16), "Q16": (4096, f16), "RR": (8192, f16),
-    "R2": (2048, f16), "gx": (2048, f16), "gy": (2048, f16), "PB": (2048, f32), "ZB": (2048, f32),
-    "R0": (2048, f16), "NZ": (2048, b16), "PP": (1024, f32), "UI": (1024, i32), "PI": (512, i32), "NBI": (256, i32),
-    "BDI": (8, i32), "Lo": (256, u16), "bo": (8, u16), "SX": (384, f16), "SY": (384, f16), "LX": (1152, f16),
-    "LY": (1152, f16), "SP": (128, b16), "SW": (128, f32), "LT": (ZC, f32), "Z2": (6 * ZC, f32), "ZW": (3 * ZC, f32),
-    "SS": (768, b16), "tc": (256, b16), "AI": (256, b16), "ND": (512, b16),
+    "DXT": (4096, b16), "DYT": (4096, b16), "NT": (4096, b16), "DD": (8192, b16), "Q16": (2048, f16), "RR": (4096, f16),
+    "gx": (2048, f16), "gy": (2048, f16), "PB": (2048, f32), "AB": (2048, f32), "ZB": (4096, f32),
+    "R0": (2048, f16), "NZ": (2048, b16), "UI": (1024, i32), "PI": (512, i32), "NBI": (256, i32),
+    "BDI": (8, i32), "Lo": (256, u16), "bo": (8, u16), "SX": (384, f16), "SY": (384, f16), "LX": (768, f16),
+    "LY": (768, f16), "SP": (128, b16), "SW": (128, f32), "PX": (2048, f32), "LT": (ZC, f32), "Z2": (6 * ZC, f32), "ZW": (3 * ZC, f32),
+    "SS": (1024, b16), "AI": (256, b16), "ND": (512, b16),
     "cgx": (1024, f16), "cgy": (1024, f16), "CDX": (1024, b16), "CDY": (1024, b16), "cb": (1024, f32),
     "EQ": (512, b16), "xa": (256, f16),
-    "O1": (64, u16), "O2": (64, u16), "UL": (64, f16), "CI": (64, i32), "ia": (128, i32), "ib": (64, i32), "ic": (64, i32),
-    "CL": (64, f16), "FB": (128, b16), "dL": (128, b16), "sqL": (128, b16), "KY": (256, f32), "PVL": (384, f32),
-    "ef": (256, b16), "hn": (128, b16), "BI": (128, i32), "BJ": (128, i32), "t1": (128, f16), "c16": (128, f16),
-    "C16": (128, f16), "Cn": (128, f16), "O3": (24, u16), "Oc": (24, u16), "Ox": (24, u16), "Oy": (24, u16),
+    "O1": (64, u16), "O2": (64, u16), "UL": (64, f16),
+    "CL": (64, f16), "FB": (128, b16), "dL": (128, b16), "sqL": (128, b16), "tL": (64, b16), "KY": (256, f32), "PVL": (384, f32),
+    "ef": (256, b16), "hn": (128, b16), "t1": (128, f16), "c16": (128, f16),
+    "C16": (128, f16), "Cn": (128, f16), "O3": (24, u16), "Oc": (24, u16), "Oxy": (48, u16),
     "cf": (40, f32), "dum": (8, f32), "LTc": (128, f32), "AL": (384, b16), "DN": (128, b16), "FE": (512, b16),
-    "NV": (128, f32), "NC": (256, f32), "VJ": (384, f32), "vio": (384, f16), "EP": (128, b16), "ED": (768, f32),
+    "NV": (128, f32), "NC": (256, f32), "VJ": (256, f32), "EP": (128, b16), "ED": (768, f32),
     "nq": (384, f32), "ES": (768, b16), "EWC": (384, f32), "EQq": (384, f32), "EM": (1152, f16), "eg": (512, f16),
-    "EA": (512, f32), "em": (256, f16), "enz": (256, b16), "EMs": (384, f32),
-    "ci": (16, i32), "cj": (24, i32), "col": (40, f32), "RM": (16, f32), "MK": (16, f32), "e8": (8, f32),
-    "IX": (256, b16), "IG": (128, b16), "IH": (128, b16), "MD": (1040, b16), "one": (1024, b16),
-    "IDS": (128 * 7, b16), "I1023": (128, f16), "F32": (128 * 9, f32), "GSB": (144 * 5, b16), "BO": (256, b16),
+    "EA": (512, f32), "em": (256, f16), "enz": (256, b16), "G8": (144 * 8, b16),
+    "ci": (16, i32), "cj": (24, i32), "col": (40, f32), "RM": (16, f32), "e8": (8, f32),
+    "IX": (256, b16), "IG": (128, b16), "IH": (128, b16),
+    "IDS": (128 * 10, b16), "ST": (256, f16), "EB": (1024, b16), "F32": (128 * 10, f32), "GSB": (144 * 4, b16), "BO": (256, b16),
     "BR": (2048, b16), "NB": (128 * 4, b16), "OX": (1024, b16), "WV": (1136, b16), "NXR": (896, b16), "PGm": (1024, b16),
-    "RB": (128 * 5, b16), "HB": (256, b16), "TRI": (256, b16), "TRc": (128, b16), "CM": (240, b16), "SH": (320, b16),
-    "nf": (8, b16),
+    "RB": (128 * 5, b16), "HB": (256, b16), "TRI": (256, b16), "TRc": (512, b16), "CM": (240, b16), "eps": (512, b16),
 }
-ALIAS = {"XY16": ("Q16", 0, 1024), "PI2": ("NZ", 0, 1024), "PT": ("DD", 0, 1024), "Zp": ("cgx", 0, 512), "Zt": ("cgx", 512, 512),
-         "G1": ("cgx", 0, 1024), "csg": ("CDX", 0, 1024), "eq2": ("CDY", 0, 1024), "PG": ("RR", 4096, 4096), "eab": ("EA", 0, 256),
-         "dc": ("ND", 0, 512), "sq": ("SS", 256, 512),
-         "tb": ("CDX", 0, 1024), "WX": ("cb", 0, 512), "wout": ("cb", 512, 512), "LDI": ("PI", 0, 512)}
+ALIAS = {"XY16": ("Q16", 0, 1024), "PI2": ("NZ", 0, 1024), "PT": ("Q16", 1024, 1024), "tc": ("EQ", 0, 256), "Zp": ("cgx", 0, 512), "Zt": ("cgx", 512, 512),
+         "G1": ("cgx", 0, 1024), "csg": ("CDX", 0, 1024), "eq2": ("CDY", 0, 1024), "PG": ("RR", 0, 4096), "eab": ("EA", 0, 256),
+         "one": ("CDY", 0, 1024), "one2": ("CDY", 0, 1024), "SH": ("ES", 0, 320), "dc": ("ND", 0, 512), "sq": ("SS", 512, 512),
+         "tb": ("CDX", 0, 1024), "PP": ("cb", 0, 1024), "wout": ("ZW", 0, 512), "EMs": ("nq", 0, 384), "LDI": ("PI", 0, 512),
+         "vio": ("eg", 0, 384), "CI": ("UI", 0, 64), "ia": ("UI", 64, 128), "ib": ("UI", 192, 64), "ic": ("UI", 256, 64),
+         "BI": ("UI", 320, 128), "BJ": ("UI", 448, 128)}
 PLACE = {}
 SCRATCH = {}
 for _k, (_w, _d) in _B.items():
@@ -45,18 +46,22 @@ for _k, (_w, _d) in _B.items():
         SCRATCH["pool_" + _d] = ("sbuf", [128, _o + (_w + 15) // 16 * 16], _d)
 for _i in range(8):
     SCRATCH["P%d" % _i] = ("psum", [128, 512], f32)
-NDMA = 100
+NDMA = 130
 SEMAPHORES = ["qt", "qv", "qa", "qg", "ls", "aP", "aW"] + ["a%s%d" % (_c, _i) for _c in "xy" for _i in range(3)] \
     + ["d%d" % _i for _i in range(NDMA)]
 SZ = {f32: 4, f16: 2, b16: 2, i32: 4, u16: 2}
-CY = 0.83e-3 * 1.1
+CY = 0.83e-3 * 1.05
 GA = 1.56
 HOP = 0.12
-DLAT = 2.6
+DLAT = 2.1
 BIG = 65536.0
-GROUPS = [((0, 1), 1, 1), ((2, 3), 1, 1), ((4, 5), 1, 1), ((6,), 1, 1), ((7,), 0, 0)]
-TRIES = 1500
-MARGIN = 0.5
+GROUPS = [((0, 1), 2, 1), ((2, 3), 2, 1), ((4, 5), 2, 1), ((6, 7), 1, 1)]
+GROUPS = [GROUPS, GROUPS, GROUPS]
+ZSUM = ((0,), (1,), (2,))
+TRIES = 5000
+SEED = 1
+RES = 3
+OPT = {"sign": "a", "s1dma": 1, "flexg": 1, "gmv": 1}
 
 
 def S(name, a=0, b=None, step=1, p=None):
@@ -162,17 +167,17 @@ def build():
     def act(out, a, fn, bias=None, scale=None):
         return add([a_act(out, a, fn, bias, scale)], aps(a, bias, scale), [out])
 
-    def mv(out, a, scale=None, bias=None):
+    def mv(out, a, scale=None, bias=None, vfirst=False):
         if scale is None and bias is None:
             alts = [a_act(out, a, F.Copy), v_cp(out, a)]
         elif bias is None:
             alts = [a_act(out, a, F.Copy, scale=scale), v_ts(out, a, scale, A.mult)]
         else:
             alts = [a_act(out, a, F.Identity, bias=bias), v_ts(out, a, bias, A.add)]
-        return add(alts, aps(a, scale, bias), [out])
+        return add(alts[::-1] if vfirst else alts, aps(a, scale, bias), [out])
 
     def gather(out, a):
-        return act(out, a, F.Copy)
+        return mv(out, a) if OPT["flexg"] else act(out, a, F.Copy)
 
     def relu(out, a):
         return add([a_act(out, a, F.Relu), v_ts(out, a, 0.0, A.max)], [a], [out])
@@ -187,6 +192,11 @@ def build():
     def asel(out, a, pat, base, op=A.is_equal):
         return add([("g", "affine_select", (out, a, pat, op, 0.0, base, 1), {}, 0.17 + 2 * width(out) * CY)], [a], [out])
 
+    def gmv(out, a):
+        n = width(out)
+        alts = [("g", "affine_select", (out, a, [[0, n]], A.is_ge, 0.0, 0, 1), {}, 0.17 + 2 * n * CY), a_act(out, a, F.Copy), v_cp(out, a)]
+        return add(alts if OPT["gmv"] else alts[1:], [a], [out])
+
     def mm(groups, after=(), start=True, stop=True):
         rd, wr, c = [], [], 0.03
         for out, terms in groups:
@@ -198,6 +208,8 @@ def build():
 
     def dma(eng, out, a, acc=False, lat=2.2):
         nd[0] += 1
+        if acc:
+            lat = DLAT + 0.27 * width(out) * size(out) / 1024
         return add([(eng, "dma", (out, a, acc, "d%d" % (nd[0] - 1)), {}, 1.0 if eng == "g" else 0.1)],
                    aps(a) + ([out] if acc else []), aps(out), lat=lat)
 
@@ -237,7 +249,7 @@ def build():
     ts(wcol, lo8, -1023.0, A.mult, 1024.0, A.add)
     ts(c1("col", 11), c1("RM", 8), 8.0, A.mult, c1("RM", 0), A.add)
     tt(ccol, c1("col", 11), c1("RM", 4), A.add)
-    ts(keyc, kcol, -512.0, A.mult, 3584.0 - 8192.0, A.add)
+    ts(keyc, kcol, -512.0, A.mult, 3584.0 - (9 if OPT["sign"] == "v" else 1) * 4096.0, A.add)
     ts(c1("col", 12), gcol, 15.0, A.add)
     ts(c1("col", 13), pcol, 16.0, A.add)
     ts(c1("col", 14), bcol, 0.0, A.is_equal)
@@ -254,9 +266,10 @@ def build():
         mv(blk("SX", t), IND(S("XW", 0, 512), S("bo")))
         mv(blk("SY", t), IND(S("YW", 0, 512), S("bo")))
         ne = 2 if more else 4
-        send(more + [(blk("SX", t), "LX", 384 * t, 128, "ax%d" % t, ne), (blk("SY", t), "LY", 384 * t, 128, "ay%d" % t, ne)])
-        mv(S("XW", 512, 896), blk("LX", t, 384))
-        mv(S("YW", 512, 896), blk("LY", t, 384))
+        send(more + [(blk("SX", t), "LX", 384 * (t % 2), 128, "ax%d" % t, ne),
+                     (blk("SY", t), "LY", 384 * (t % 2), 128, "ay%d" % t, ne)])
+        mv(S("XW", 512, 896), blk("LX", t % 2, 384))
+        mv(S("YW", 512, 896), blk("LY", t % 2, 384))
     border(0, [(S("SP"), "PW", 512, 128, "aP", 4)])
     mv(S("SW"), IND(S("WW", 0, 512), S("bo")))
     send([(S("SW"), "WW", 512, 128, "aW", 8)])
@@ -265,11 +278,13 @@ def build():
     ms(S("one"), 1.0)
     iota(S("IG"), [[16, 8], [0, 16]], 0)
     iota(S("IH"), [[1, 16], [0, 8]], 0)
-    I, NI, I32x, IBn, I896, N896, ILO = (blk("IDS", k) for k in range(7))
-    for m, c in ((I, 1.0), (NI, -1.0), (I32x, 32.0), (IBn, -BIG), (I896, 896.0), (N896, -896.0), (ILO, lo8),
-                 (S("I1023"), 1023.0)):
-        ts(m, IX, pcol, A.is_equal, c, A.mult)
-    I32, NI32, RT1, RT2, RT4, SH0, SH1, BF0, BF8 = (blk("F32", k) for k in range(9))
+    I, NI, I32x, IBn, I896, N896, ILO, Ith, IM, NIM = (blk("IDS", k) for k in range(10))
+    ts(I, IX, pcol, A.is_equal)
+    for m, c in ((NI, -1.0), (I32x, 32.0), (IBn, -BIG), (I896, 896.0), (N896, -896.0), (ILO, lo8), (Ith, 1.0 / 32),
+                 (IM, 1.5 * 2 ** 29), (NIM, -1.5 * 2 ** 29)):
+        mv(m, I, scale=c, vfirst=True)
+    I32, NI32, RT1, RT2, RT4, SH0, SH1, BF0, BF8, I32th = (blk("F32", k) for k in range(10))
+    mv(I32th, Ith)
     mv(I32, I)
     mv(NI32, NI)
     for m, k in ((RT1, 1), (RT2, 2), (RT4, 4)):
@@ -280,10 +295,10 @@ def build():
     for h, m in enumerate((SH0, SH1)):
         asel(m, S("one", 0, 128), [[-16, 8], [1000, 2], [-1, 8]], -1000 * h)
     GSk = []
-    for k, c in enumerate((1.0, wcol, -4096.0, 1.0 / 16, ccol)):
+    for k, c in enumerate((wcol, 4096.0 if OPT["sign"] == "v" else -2048.0, 1.0 / 16, ccol)):
         ts(blk("GSB", k, 144), S("IX", 0, 144), c1("col", 12), A.is_equal, c, A.mult)
         GSk.append([S("GSB", 144 * k + 15 - r, 144 * k + 143 - r) for r in range(16)])
-    GS, GSW, GSK, GS16, GSC = GSk
+    GSW, GSK, GS16, GSC = GSk
     BO, BO8 = blk("BO", 0), blk("BO", 1)
     ts(BO, S("IG"), gcol, A.is_equal)
     ts(BO8, S("IG"), gcol, A.is_equal, lo8, A.mult)
@@ -292,7 +307,7 @@ def build():
     BR = [blk("BR", r) for r in range(16)]
     NB0, NB8, NB5, NB4 = (blk("NB", k) for k in range(4))
     for m, r, c in ((NB0, 0, -1.0), (NB8, 8, -1.0), (NB5, 5, -896.0), (NB4, 4, -1.0)):
-        ts(m, BO, c1("RM", r), A.mult, c, A.mult)
+        mv(m, BR[r], scale=c, vfirst=True)
     mv(BF0, BO, scale=c1("RM", 0))
     mv(BF8, BO, scale=c1("RM", 8))
     for xy in range(2):
@@ -311,21 +326,26 @@ def build():
     asel(blk("TRI", 1), blk("TRI", 0), [[-1, 128]], 0, A.is_ge)
     tt(blk("TRI", 1), blk("TRI", 0), blk("TRI", 1), A.subtract)
     TRI = blk("TRI", 1)
-    ts(S("TRc"), IX, pcol, A.is_le, 4096.0, A.mult)
+    ts(blk("TRc", 0), IX, pcol, A.is_le, 4096.0, A.mult)
+    for u in range(1, 4):
+        dma("s", blk("TRc", u), blk("TRc", 0))
     ms(S("CM"), 0.0)
     ms(S("CM", 112, 128), -16.0)
     for b in range(2):
         ts(blk("SH", b, 160), S("IX", 0, 160), c1("col", 13), A.is_equal, c1("col", 14 + b), A.mult)
-    ts(S("MK"), S("IX", 0, 16), hcol, A.is_equal, -1.0, A.mult)
+    ms(S("DD", 0, 1024), 0.0)
+    dma("s", S("DD", 1024, 2048), S("DD", 0, 1024))
+    for u in range(1, 4):
+        dma("s", blk("DD", u, 2048), blk("DD", 0, 2048))
     ts(S("dum"), S("IX", 0, 8), 16.0, A.mult, rcol, A.add)
     ts(S("dum"), S("dum"), 520.0, A.add)
-    iota(S("tb"), [[0, 128], [1, 8]], 0)
-    ts(S("MD", 0, 1024), S("tb"), kcol, A.is_equal)
-    ts(S("MD", 1024, 1040), S("tb", 0, 16), kcol, A.is_equal)
+    ts(S("e8"), S("IX", 0, 8), kcol, A.is_equal)
+    for k in range(8):
+        mv(blk("G8", k, 144), blk("GSB", 0, 144), scale=c1("e8", k), vfirst=True)
     iota(S("vio"), [[-1, 3], [4, 128]], 3)
-    ms(S("WV"), 0.0)
+    dma("s", S("WV"), S("DD", 0, 1136))
     for u in range(8):
-        mv(S("WV", 128 * u + 112, 128 * u + 128), sub(I896, 16 * u, 16 * u + 16))
+        dma("s", S("WV", 128 * u + 112, 128 * u + 128), sub(I896, 16 * u, 16 * u + 16))
     iota(S("Z2", 0, 2 * ZC), [[0, 2 * ZC]], 0)
     for s in (1, 2):
         dma("s", blk("Z2", s, 2 * ZC), S("Z2", 0, 2 * ZC))
@@ -354,9 +374,9 @@ def build():
             mm([(S(bk, 128 * u, 128 * u + 128), [(blk(src, 4 * h + u), m)]) for u in range(4)])
             mv(blk(dst, h, 512), S(bk))
     dma("s", S("LDI"), "ld")
-    ms(S("LD2", 0, 1024, 2), 0.0)
+    iota(S("LD2", 0, 1024, 2), [[0, 512]], 0)
     cp(S("LD2", 1, 1024, 2), S("LDI"))
-    ms(S("one", 512, 1024), 1.0 / 64)
+    ms(S("eps"), 1.0 / 64)
     bk = bank()
     mm([(S(bk, 128 * t + 64 * xy, 128 * t + 64 * xy + 64),
          [(RB[8 * xy, h], S("PW", 256 * h + 3 - t, 256 * h + 256, 4)) for h in range(2)]) for t in range(3) for xy in range(2)])
@@ -365,14 +385,32 @@ def build():
     mm([(S(bk, 128 * t, 128 * t + 128), [(ILO, blk("vio", t))] + [(m, S("PW", 3 - t, 512, 4)) for m in (RB[0, 1], RB8, NB5)])
         for t in range(2)])
     mv(S("VJ", 0, 256), S(bk, 0, 256))
+    asel(S("EB"), S("one2"), [[-1, 64], [0, 16]], 0)
+
+    def spread(x, scale, slot):
+        n = width(x)
+        rows = (0, n, 1)
+        bk = bank()
+        mm([(S(bk, 0, 128, 1, rows), [(x, I)])])
+        xt = S("ST", 128 * (slot // 2 % 2), 128 * (slot // 2 % 2) + 128, 1, rows)
+        mv(xt, S(bk, 0, 128, 1, rows), scale=scale)
+
+        def make(u):
+            bn = bank()
+            mm([(S(bn), [(xt, S("EB", 512 * u, 512 * u + 512, 1, rows))])])
+            return bn
+        return [lambda u=u: make(u) for u in range(n // 32)]
     tag[0] = "pos"
-    for chunks, _, _ in GROUPS:
+    for chunks, _, _ in GROUPS[0]:
         a, b = chunks[0], chunks[-1] + 1
         gather(S("PG", 512 * a, 512 * b), IND(S("PW"), S("Lo", 32 * a, 32 * b)))
     bk = bank()
     mm([(S(bk), [(GSC[8 + k], S("PG", k, 4096, 8)) for k in range(8)])])
     tt(S("LT", 0, 512), S(bk), S("LT", 0, 512), A.add)
-    for chunks, _, _ in GROUPS:
+    bk = bank()
+    mm([(S(bk, 8 * u, 8 * u + 8), [(blk("PG", u), sub(NB4, 0, 128, 16))]) for u in range(32)])
+    ts(S("SS", 0, 256), S(bk, 0, 256), 0.0, A.is_equal)
+    for chunks, _, _ in GROUPS[0]:
         a, b = chunks[0], chunks[-1] + 1
         for B in chunks:
             for xy, nm, m in ((1, "DYT", NB8), (0, "DXT", NB0)):
@@ -382,14 +420,13 @@ def build():
         for xy, nm in enumerate(("DXT", "DYT")):
             act(S("sq", 256 * xy + 32 * a, 256 * xy + 32 * b), S(nm, 512 * a, 512 * b, 16), F.Square, scale=8.0)
         tt(S("tc", 32 * a, 32 * b), S("sq", 32 * a, 32 * b), S("sq", 256 + 32 * a, 256 + 32 * b), A.add)
-        for B in chunks:
-            bk = bank()
-            mm([(S(bk, i, 512, 16), [(NI, blk("tc", B, 32))]) for i in range(16)])
-            mv(blk("NT", B, 512), S(bk))
+        for B, bk in zip(chunks, spread(S("tc", 32 * a, 32 * b), -1.0, a)):
+            mv(blk("NT", B, 512), S(bk()))
     for xy, nm in enumerate(("DXT", "DYT")):
-        mv(blk("dc", xy, 256), S(nm, 0, 4096, 16))
+        mv(blk("dc", xy, 256), S(nm, 0, 4096, 16), scale=-1.0 / 32)
     for u in range(16):
-        mv(blk("DD", u, 512), S("dc"), scale=c1("MK", u))
+        rows = (8 * u, 8 * u + 8, 1)
+        dma("s", S("DD", 512 * u, 512 * u + 512, 1, rows), S("dc", 0, 512, 1, rows))
 
     def reg(bk, k, w=128):
         return S(bk, w * k, w * k + w)
@@ -408,9 +445,10 @@ def build():
         mm([(S(bk, 0, 64), [(SH0, half("LT", 0)), (SH1, half("LT", 1))])])
         ts(S("O1"), S(bk, 0, 64), 512.0, A.min)
         mv(S("UL"), S(bk, 0, 64))
-        tt(S("G1"), IND(S("LT", 0, 520), S("O1")), S("MD", t, t + 1024), A.mult)
+        gather(S("G1"), IND(S("LT", 0, 520), S("O1")))
         bk = bank()
-        mm([(S(bk, 0, 64), [(GSW[r], S("G1", r, 1024, 16)) for r in range(16)])])
+        mm([(S(bk, 0, 64), [(S("G8", 144 * ((r + t) % 8) + 15 - r, 144 * ((r + t) % 8) + 143 - r), S("G1", r, 1024, 16))
+                            for r in range(16)])])
         cp(S("CI"), S(bk, 0, 64))
         ts(S("ib"), S("CI"), 1023, A.bitwise_and)
         ts(S("O2"), S("ib"), 511.0, A.min)
@@ -419,6 +457,7 @@ def build():
             ts(blk("ia", xy, 64), S("CI"), 10 + 3 * xy, A.arith_shift_right, 7, A.bitwise_and)
         tt(S("dL"), S("ia"), blk("PVL", t), A.subtract)
         act(S("sqL"), S("dL"), F.Square, scale=8.0)
+        tt(S("tL"), blk("sqL", 0, 64), blk("sqL", 1, 64), A.add)
         ts(S("ic"), S("CI"), 3, A.bitwise_and)
         ts(blk("FB", 0, 64), S("ic"), float(rho), A.is_equal)
         ts(blk("FB", 1, 64), S("CL"), 512.0, A.is_ge)
@@ -438,13 +477,21 @@ def build():
                 bks.append(bank())
                 mm([(reg(bks[-1], k, 64), [(I, S(nm, 8 * h + k, 1024, 16)), (NI, blk("xa", 2 * xy + h, 64))]) for k in range(8)])
             tt(H("cb"), S(bks[0]), H("CDY"), A.mult)
-            tt(S(bks[1]), S(bks[1]), H("CDX"), A.mult)
-            tt(S(bks[1]), S(bks[1]), H("cb"), A.add)
-            act(H("cb"), S(bks[1]), F.Abs)
+            if OPT["s1dma"]:
+                tt(H("PX"), S(bks[1]), H("CDX"), A.mult)
+                dma("g", H("PX"), H("cb"), acc=True, lat=DLAT)
+                act(H("cb"), H("PX"), F.Abs)
+            else:
+                tt(S(bks[1]), S(bks[1]), H("CDX"), A.mult)
+                tt(S(bks[1]), S(bks[1]), H("cb"), A.add)
+                act(H("cb"), S(bks[1]), F.Abs)
             bk = bank()
-            mm([(reg(bk, k, 64), [(NI32, blk("cb", 8 * h + k, 64)), (BR[8 * h + k], blk("sqL", 0, 64)),
-                                  (BR[8 * h + k], blk("sqL", 1, 64))]) for k in range(8)])
-            act(H("csg"), S(bk), F.Sign, bias=0.5)
+            if OPT["sign"] == "v":
+                mm([(reg(bk, k, 64), [(BR[8 * h + k], blk("tL", 0, 64))]) for k in range(8)])
+                tt(H("csg"), S(bk), H("cb"), A.is_lt)
+            else:
+                mm([(reg(bk, k, 64), [(BR[8 * h + k], blk("tL", 0, 64)), (NI32, blk("cb", 8 * h + k, 64))]) for k in range(8)])
+                act(H("csg"), S(bk), F.Sign, bias=0.5)
         bk = bank()
         mm([(S(bk, 0, 64), [(I, S("CL"))] + [(IBn, blk("EQ", m, 64)) for m in range(8)] + [(IBn, blk("FB", m, 64)) for m in range(2)]
              + [(GSK[r], blk("csg", r, 64)) for r in range(16)])])
@@ -469,8 +516,8 @@ def build():
         mv(S("Cn"), S("C16"), scale=-1.0)
         for h in range(2):
             bk = bank()
-            mm([(reg(bk, k % 4), [(S("C16"), blk("PGm", k)), (blk("PGm", k), S("Cn")), (I, S("TRc"))]) for k in range(4 * h, 4 * h + 4)])
-            ts(blk("eq2", h, 512), S(bk), 0.0, A.is_equal)
+            mm([(reg(bk, k % 4), [(S("C16"), blk("PGm", k)), (blk("PGm", k), S("Cn"))]) for k in range(4 * h, 4 * h + 4)])
+            tt(blk("eq2", h, 512), S(bk), S("TRc"), A.is_equal)
         mv(S("LTc"), IND(S("LT", 0, 512), O3))
         ts(blk("ef", 1), S("LTc"), 896.0, A.is_equal)
         bk = bank()
@@ -483,8 +530,8 @@ def build():
         tt(blk("cf", 2, 8), S(bk, 0, 8), blk("cf", 1, 8), A.mult)
         tt(blk("cf", 3, 8), blk("cf", 2, 8), blk("cf", 0, 8), A.add)
         cp(blk("Oc", t, 8), blk("cf", 3, 8))
-        ts(blk("Ox", t, 8), blk("cf", 3, 8), 2.0, A.mult)
-        ts(blk("Oy", t, 8), blk("cf", 3, 8), 2.0, A.mult, 1.0, A.add)
+        ts(blk("Oxy", 2 * t, 8), blk("cf", 3, 8), 2.0, A.mult)
+        ts(blk("Oxy", 2 * t + 1, 8), blk("cf", 3, 8), 2.0, A.mult, 1.0, A.add)
         mv(S("EP"), IND(S("PW", 0, 512), O3))
         mv(blk("EWC", t), IND(S("WW", 0, 512), O3))
         bk = bank()
@@ -509,7 +556,7 @@ def build():
         for xy, nm in enumerate(("XW", "YW")):
             mv(S("eg", 256 * xy, 256 * xy + n), IND(S(nm, 0, 512), S("O3", 8 * s0, 8 * s1)))
         bk = bank()
-        mm([(reg(bk, 2 * u + xy), [(I, blk("eg", 2 * xy + u)), (NI32, S(nm, 3 - s, 512, 4))])
+        mm([(reg(bk, 2 * u + xy), [(I, blk("eg", 2 * xy + u)), (NI, blk("xa", xy)) if s == t else (NI32, S(nm, 3 - s, 512, 4))])
             for u, s in enumerate(ss) for xy, nm in enumerate(("XW", "YW"))])
         tt(S("EA", 0, 2 * n), S(bk, 0, 2 * n), S("ED", 256 * s0, 256 * s1), A.mult)
         bz = bank()
@@ -532,12 +579,14 @@ def build():
             ts(al, S(bk, 0, n), 35.5, A.is_ge)
             tt(em, S("em", 0, n), al, A.mult)
         tt(S("EQq", 128 * s0, 128 * s1), S(bz, 0, n), em, A.mult)
-        mv(S("nq", 128 * s0, 128 * s1), S("EQq", 128 * s0, 128 * s1), scale=-1.0)
-        for s in ss:
+        bk = bank()
+        mm([(reg(bk, 2 * u + xy), [(I32, blk("EQq", s))]) for u, s in enumerate(ss) for xy in range(2)])
+        tt(S("EA", 0, 2 * n), S(bk, 0, 2 * n), S("ED", 256 * s0, 256 * s1), A.mult)
+        for u, s in enumerate(ss):
             o = 2 * ZC * s
-            for xy, off in enumerate(("Ox", "Oy")):
-                tt(S("Z2", o + 2 * (3 - s) + xy, o + 1024, 8), blk("EQq", s), blk("ED", 2 * s + xy), A.mult)
-                tt(IND(S("Z2", o, o + 2 * ZC), blk(off, s, 8)), blk("nq", s), blk("ED", 2 * s + xy), A.mult)
+            for xy in range(2):
+                mv(S("Z2", o + 2 * (3 - s) + xy, o + 1024, 8), blk("EA", 2 * u + xy))
+            ts(IND(S("Z2", o, o + 2 * ZC), blk("Oxy", s, 16)), blk("EA", u, 256), -1.0, A.mult, 0.0, A.add)
         if t == 2:
             bk = bank()
             mm([(reg(bk, u), [(I, blk("EM", 3 * r + s)) for r in range(s, 3)]) for u, s in enumerate(ss)])
@@ -569,52 +618,55 @@ def build():
                 g_ = R(nm, B, B + 1)
                 mm([(reg(bks[-1][1], j), [(OX[xy][j], blk("UT", B)), (sub(g_, 128 * j, 128 * j + 128), NI)]) for j in range(4)])
             tt(R("PB", B, B + 1), bks[0], C("DYT", B), A.mult)
-            more = ([] if dma1 else [R("PB", B, B + 1)]) + ([C("Q16", B)] if t else [])
-            tt(bks[1] if more else R("ZB", B, B + 1), bks[1], C("DXT", B), A.mult)
+            both = t and dma1 == 2
+            more = [] if both else ([] if dma1 else [R("PB", B, B + 1)]) + ([C("ZB", B)] if t else [])
+            tt(bks[1] if more else R("PX" if both else "ZB", B, B + 1), bks[1], C("DXT", B), A.mult)
             for m, x in enumerate(more):
                 tt(bks[1] if m + 1 < len(more) else R("ZB", B, B + 1), bks[1], x, A.add)
         if dma1:
             dma("g", R("ZB"), R("PB"), acc=True, lat=DLAT)
-        act(R("PB"), R("ZB"), F.Abs)
+        if both:
+            dma("g", R("ZB"), R("PX"), acc=True, lat=DLAT)
+        act(R("AB"), R("ZB"), F.Abs)
         if dma2:
-            dma("g", R("PB"), S("NT", 512 * a, 512 * b), acc=True, lat=DLAT)
-            relu(R("R0"), R("PB"))
+            dma("g", R("AB"), S("NT", 512 * a, 512 * b), acc=True, lat=DLAT)
+            relu(R("R0"), R("AB"))
         else:
             for B in chunks:
                 bk = S(bank())
-                mm([(bk, [(I32, R("PB", B, B + 1)), (I, C("NT", B))])])
+                mm([(bk, [(I32, R("AB", B, B + 1)), (I, C("NT", B))])])
                 relu(R("R0", B, B + 1), bk)
         nonzero(R("NZ"), R("R0"))
         n = 32 * len(chunks)
         bk = bank()
         nz = R("NZ")
-        mm([(S(bk, 0, n), [(I, sub(nz, i, 16 * n, 16)) for i in range(16)]
-             + ([(I32x, S("SS", 256 * t - 256 + 32 * a, 256 * t - 256 + 32 * b))] if t else []))], stop=t > 0)
-        if t == 0:
-            mm([(S(bk, 8 * u, 8 * u + 8), [(blk("PG", 4 * a + u), sub(NB4, 0, 128, 16))]) for u in range(n // 8)], start=False, stop=False)
-            mm([(S(bk, 0, n), [(I32x, S("one", 512, 512 + n))])], start=False)
-        stay = ts(S("SS", 256 * t + 32 * a, 256 * t + 32 * b), S(bk, 0, n), 35.5 if t else 4.0, A.is_ge)
-        for B in chunks:
-            bk = bank()
-            mm([(S(bk, i, 512, 16), [(S("I1023"), blk("SS", 8 * t + B, 32))]) for i in range(16)])
-            r = C("RR", 8 * t + B) if t < 2 else R("R2", B, B + 1)
+        was, now = (S("SS", 256 * u + 32 * a, 256 * u + 32 * b) for u in (t, t + 1))
+        mm([(S(bk, 0, n), [(I32x, was)] + [(I, sub(nz, i, 16 * n, 16)) for i in range(16)])])
+        stay = ts(now, S(bk, 0, n), 35.5, A.is_ge)
+        for B, mk in zip(chunks, spread(now, 1023.0, a)):
+            bk = mk()
+            r = R("R0", B, B + 1) if t else C("RR", B)
             tt(r, S(bk), R("R0", B, B + 1), A.min)
             bk = bank()
             add([a_act(S(bk), R("ZB", B, B + 1), F.Sign)], [R("ZB", B, B + 1)], [S(bk)], after=[stay])
-            tt(C("Q16", B), S(bk), r, A.mult)
+            q = R("Q16", B, B + 1)
+            iq = tt(q, S(bk), r, A.mult)
             if B % 4 == 0:
                 h = B // 4
                 acc.append(bank())
-                mm([(S(acc[h]), [(I32x, blk("UT", h, 512))])], stop=False)
-                mm([(reg(acc[h], u), [(blk("LD2", 4 * h + u), I)]) for u in range(4)], start=False, stop=False)
+                mm([(S(acc[h]), [(I, blk("UT", h, 512)), (I, S("eps"))])], stop=False, after=[stay])
+                mm([(reg(acc[h], u), [(blk("LD2", 4 * h + u), Ith)]) for u in range(4)], start=False, stop=False)
             o = 128 * (B % 4)
             mm([(S(acc[B // 4], o + 16 * g, o + 16 * g + 16, 1, (32 * j, 32 * j + 32, 1)),
-                 [(S("DD", 32 * B + 8 * j + g, 8192, 256), blk("Q16", 32 * B + 8 * j + g, 16))])
+                 [(S("DD", 32 * B + 8 * j + g, 8192, 256), sub(q, 128 * j + 16 * g, 128 * j + 16 * g + 16))])
                 for j in range(4) for g in range(8)], start=False, stop=False)
+            if t < 2:
+                gmv(C("ZB", B), q)
+            if t == 1 and B == b - 1:
+                dma("g", S("RR", 512 * a, 512 * b), R("R0"), acc=True, lat=DLAT)
             if t == 2:
                 bk = bank()
-                mm([(reg(bk, j), [(blk("RR", 32 * u + 4 * B + j), I) for u in range(2)]
-                     + [(sub(r, 128 * j, 128 * j + 128), I)]) for j in range(4)])
+                mm([(reg(bk, j), [(blk("RR", 4 * B + j), I), (sub(r, 128 * j, 128 * j + 128), I)]) for j in range(4)])
                 pp = blk("PP", B % 2, 512)
                 gather(pp, IND(S("WW"), blk("Lo", B, 32)))
                 tt(pp, S(bk), pp, A.mult)
@@ -623,12 +675,11 @@ def build():
                 mm([(reg(wb[-1], B % 4, 64), [(I32, sub(pp, k, 512, 8)) for k in range(8)])])
 
     def update(t, h, acc):
-        for s in range(t + 1):
+        for s in ZSUM[t]:
             o = 2 * ZC * s + 512 * h
-            mm([(reg(acc[h], u), [(S("Z2", o + 128 * u, o + 128 * u + 128), I32)]) for u in range(4)], start=False, stop=False)
-        mm([(S(acc[h]), [(I32x, S("one", 512, 1024))])], start=False)
-        ts(blk("UI", h, 512), S(acc[h]), 1.0 / 32, A.mult)
-        ts(blk("UT", h, 512), blk("UI", h, 512), -1023.0, A.max, 1023.0, A.min)
+            mm([(reg(acc[h], u), [(S("Z2", o + 128 * u, o + 128 * u + 128), I32th)]) for u in range(4)], start=False, stop=False)
+        mm([(S(acc[h]), [(IM, S("eps")), (NIM, S("eps"))])], start=False)
+        ts(blk("UT", h, 512), S(acc[h]), -1023.0, A.max, 1023.0, A.min)
         for xy, nm in enumerate(("XW", "YW")):
             bk = bank()
             mm([(reg(bk, u, 64), [(blk("UT", 4 * h + u), sub(I, xy, 128, 2))]) for u in range(4)])
@@ -640,15 +691,22 @@ def build():
         tag[0] = "s1_%d" % t
         step1(t)
         tag[0] = "ex_%d" % t
+        z2 = lambda s: S("Z2", 2 * ZC * s, 2 * ZC * s + 1024)
+        zw = lambda s: S("ZW", ZC * s, ZC * s + 512)
+        if t == 2:
+            dma("s", z2(1), S("ZW", 0, 1024))
         if t:
             extra(0, t, t)
-        extra(t, t + 1, t)
         if t == 2:
-            bk = bank()
-            mm([(S(bk), [(I32, S("ZW", ZC * s, ZC * s + 512)) for s in range(3)])])
-            mv(S("WX"), S(bk))
+            dma("g", z2(1), z2(0), acc=True, lat=DLAT)
+            dma("g", zw(1), zw(0), acc=True, lat=DLAT)
+        extra(t, t + 1, t)
+        if t:
+            dma("g", z2(t), z2(t - 1), acc=True, lat=DLAT)
+        if t == 2:
+            dma("g", zw(2), zw(1), acc=True, lat=DLAT)
         acc, wb = [], []
-        for chunks, dma1, dma2 in GROUPS:
+        for chunks, dma1, dma2 in GROUPS[t]:
             tag[0] = "m%d_%d" % (t, chunks[0])
             group(t, chunks, dma1, dma2, acc, wb)
         tag[0] = "up_%d" % t
@@ -657,7 +715,7 @@ def build():
         if t < 2:
             border(t + 1, [])
             bk = bank()
-            mm([(S(bk, u, 256, 8), [(S("WV", 128 * u + 112 - 16 * g, 128 * u + 240 - 16 * g), S("SS", 256 * t + g, 256 * t + 256, 8))
+            mm([(S(bk, u, 256, 8), [(S("WV", 128 * u + 112 - 16 * g, 128 * u + 240 - 16 * g), S("SS", 256 * t + 256 + g, 256 * t + 512, 8))
                                     for g in range(8)]) for u in range(8)])
             tt(blk("ND", t, 256), S("AI"), S(bk, 0, 256), A.subtract)
             if t == 0:
@@ -666,7 +724,7 @@ def build():
             mm([(S(bk, h, 512, 2), [(blk("HB", h), blk("ND", t, 256))]) for h in range(2)])
             tt(S("LT", 0, 512), S(bk), S("LT", 0, 512), A.max)
     for h in range(2):
-        tt(blk("wout", h, 256), S(wb[h], 0, 256), blk("WX", h, 256), A.add)
+        tt(blk("wout", h, 256), S(wb[h], 0, 256), S("ZW", 2 * ZC + 256 * h, 2 * ZC + 256 * h + 256), A.add)
         dma("s", ("yw", 256 * h, 256 * h + 256), blk("wout", h, 256))
     return ops
 
@@ -687,7 +745,7 @@ def depend(ops):
                 if ps:
                     if not (summand(o) and summand(ops[j])):
                         d[j] = d.get(j, False) or not (is_mm(o) and is_mm(ops[j]))
-                elif b > x[2] and x[3] > a and (w or wj) and (pj is None or x[5] is None or pj == x[5]):
+                elif b > x[2] and x[3] > a and (w or wj) and not (pj and x[5] and pj != x[5] and pj[2] == 16):
                     d[j] = True
             if ps:
                 users.setdefault(nm, set()).add(i)
@@ -703,86 +761,123 @@ def depend(ops):
 def schedule(ops, tries):
     n = len(ops)
     deps, users = depend(ops)
+    alts = [o["alts"] for o in ops]
+    lat = [o["lat"] for o in ops]
     succ = [[] for _ in range(n)]
     for i in range(n):
         for j in deps[i]:
-            succ[j].append(i)
+            succ[j].append((i, HOP if deps[i][j] else 0.0))
+    first = dict((min(u), nm) for nm, u in users.items())
+    banks = [sorted(set(x[1] for x in o["rd"] + o["wr"] if x[1][0] == "@")) for o in ops]
+
+    def place(pr, pick):
+        left = dict((nm, len(u)) for nm, u in users.items())
+        waiting = sorted(first, reverse=True)
+        last, phys, held = {}, {}, {}
+        free = dict((b, (0.0, None)) for b in range(8))
+        fin, est = [0.0] * n, [0.0] * n
+        cnt = [len(d) for d in deps]
+        ready = dict((e, []) for e in "tvagsr")
+        efree = dict((e, 0.0) for e in "tvagsr")
+        for i in range(n):
+            if cnt[i] == 0:
+                ready[alts[i][pick[i]][0]].append(i)
+        order = []
+        for _ in range(n):
+            nf = len(free)
+            fb = min(v[0] for v in free.values()) if nf else 0.0
+            while waiting and waiting[-1] in held:
+                waiting.pop()
+            best = None
+            for e, L in ready.items():
+                ef = efree[e]
+                c = []
+                for i in L:
+                    s = est[i]
+                    if i in first:
+                        if nf < (1 if i == waiting[-1] else RES):
+                            continue
+                        if fb > s:
+                            s = fb
+                    c.append((s if s > ef else ef, i))
+                if c:
+                    m = min(c)[0]
+                    if best is None or m < best[0]:
+                        best = (m, e, c)
+            if best is None:
+                return None
+            m, e, c = best
+            s, i = max((x for x in c if x[0] <= m + 0.05), key=lambda x: pr[x[1]])
+            if i in first:
+                b = min(free, key=lambda k: free[k][0])
+                held[i] = free.pop(b)[1]
+                phys[first[i]] = b
+            efree[e] = s + alts[i][pick[i]][4]
+            f = fin[i] = efree[e] + lat[i]
+            order.append(i)
+            ready[e].remove(i)
+            for nm in banks[i]:
+                left[nm] -= 1
+                last[nm] = max(last.get(nm, 0.0), f)
+                if left[nm] == 0:
+                    free[phys[nm]] = (last[nm] + HOP, nm)
+            for j, h in succ[i]:
+                if est[j] < f + h:
+                    est[j] = f + h
+                cnt[j] -= 1
+                if cnt[j] == 0:
+                    ready[alts[j][pick[j]][0]].append(j)
+        return max(fin), order, phys, fin, held
+
+    def chain(cur, pick):
+        order, fin = cur[1], cur[3]
+        prev, last = {}, {}
+        for i in order:
+            e = alts[i][pick[i]][0]
+            prev[i] = last.get(e)
+            last[e] = i
+        i = max(order, key=lambda k: fin[k])
+        out = []
+        while i is not None:
+            out.append(i)
+            c = [(fin[j], j) for j in deps[i]]
+            if prev[i] is not None:
+                c.append((fin[prev[i]] - lat[prev[i]], prev[i]))
+            i = max(c)[1] if c else None
+        return out
+
     pr = [0.0] * n
     for i in range(n - 1, -1, -1):
-        pr[i] = ops[i]["alts"][0][4] + ops[i]["lat"] + max([pr[j] + HOP for j in succ[i]] + [0.0])
-    rng = np.random.default_rng(1)
-    best = place(ops, deps, succ, users, pr)
+        pr[i] = alts[i][0][4] + lat[i] + max([pr[j] + h for j, h in succ[i]] + [0.0])
+    pick = [0] * n
+    rng = np.random.default_rng(SEED)
+    cur = place(pr, pick)
+    ch = chain(cur, pick)
     for _ in range(tries):
-        q = list(pr)
-        for _r in range(3):
-            a = int(rng.integers(0, n))
-            d = float(rng.normal()) * 4.0
-            for i in range(a, min(n, a + int(rng.integers(1, 40)))):
+        q, p = pr, pick
+        L = ch if rng.random() < 0.8 else range(n)
+        if rng.random() < 0.45:
+            L = [i for i in L if len(alts[i]) > 1]
+            p = list(pick)
+            a = int(rng.integers(0, len(L) + 1))
+            for i in L[a:a + int(rng.integers(1, 3))]:
+                p[i] = (p[i] + 1 + int(rng.integers(0, len(alts[i]) - 1))) % len(alts[i])
+        else:
+            q = list(pr)
+            a = L[int(rng.integers(0, len(L)))]
+            d = float(rng.normal()) * 3.0
+            w = int(rng.integers(0, 10))
+            for i in range(max(0, a - w), min(n, a + w + 1)):
                 q[i] += d
-        new = place(ops, deps, succ, users, q)
-        if new is not None and (best is None or max(new[3]) <= max(best[3])):
-            best, pr = new, q
-    return best
-
-
-def place(ops, deps, succ, users, pr):
-    n = len(ops)
-    deps = [dict(d) for d in deps]
-    first = dict((min(u), nm) for nm, u in users.items())
-    left = dict((nm, len(u)) for nm, u in users.items())
-    banks = [set(x[1] for x in o["rd"] + o["wr"] if x[1][0] == "@") for o in ops]
-    waiting = sorted(first)
-    phys = {}
-    free = dict((b, (0.0, [])) for b in range(8))
-    fin = [None] * n
-    way = [None] * n
-    cnt = [len(deps[i]) for i in range(n)]
-    ready = [i for i in range(n) if cnt[i] == 0]
-    est = dict((i, 0.0) for i in ready)
-    efree = dict((e, 0.0) for e in "tvagsr")
-    order = []
-    while ready:
-        cand = []
-        fb = min(v[0] for v in free.values()) if free else 0.0
-        for i in ready:
-            s = est[i]
-            if i in first:
-                if len(free) < (1 if i == waiting[0] else 3):
-                    continue
-                s = max(s, fb)
-            alts = ops[i]["alts"]
-            own = max(s, efree[alts[0][0]])
-            cand.append((own, i, alts[0]))
-            for alt in alts[1:]:
-                if max(s, efree[alt[0]]) + alt[4] + MARGIN < own + alts[0][4]:
-                    cand.append((max(s, efree[alt[0]]), i, alt))
-        if not cand:
-            return None
-        s0, _, alt0 = min(cand, key=lambda c: c[0])
-        e = alt0[0]
-        s, i, alt = max((c for c in cand if c[2][0] == e and c[0] <= s0 + 0.05),
-                        key=lambda c: pr[c[1]] - (0.0 if c[2] is ops[c[1]]["alts"][0] else 3.0))
-        if i in first:
-            b = min(free, key=lambda k: free[k][0])
-            for j in free.pop(b)[1]:
-                deps[i][j] = True
-            phys[first[i]] = b
-            waiting.remove(i)
-        efree[e] = s + alt[4]
-        fin[i] = efree[e] + ops[i]["lat"]
-        way[i] = alt
-        order.append(i)
-        ready.remove(i)
-        for nm in banks[i]:
-            left[nm] -= 1
-            if left[nm] == 0:
-                free[phys[nm]] = (max(fin[j] for j in users[nm]) + HOP, list(users[nm]))
-        for j in succ[i]:
-            cnt[j] -= 1
-            if cnt[j] == 0:
-                est[j] = max(fin[k] + (HOP if deps[j][k] else 0.0) for k in deps[j])
-                ready.append(j)
-    return order, deps, phys, fin, way
+        new = place(q, p)
+        if new is not None and new[0] <= cur[0] + 0.03 * rng.random():
+            cur, pr, pick = new, q, p
+            ch = chain(cur, pick)
+    _, order, phys, fin, held = cur
+    for i, nm in held.items():
+        for j in users.get(nm, ()):
+            deps[i][j] = True
+    return order, deps, phys, fin, [alts[i][pick[i]] for i in range(n)]
 
 
 PLAN = []

@@ -8,30 +8,32 @@ _B = {
     "XW": (904, f32), "YW": (904, f32), "WW": (904, f32), "PW": (912, b16), "UT": (1024, f16), "LD2": (1024, f16),
     "DXT": (4096, b16), "DYT": (4096, b16), "NT": (4096, b16), "DD": (8192, b16), "Q16": (2048, f16), "RR": (4096, f16),
     "gx": (2048, f16), "gy": (2048, f16), "PB": (2048, f32), "AB": (2048, f32), "ZB": (4096, f32),
-    "R0": (2048, f16), "NZ": (2048, b16), "UI": (1024, i32), "PI": (512, i32), "NBI": (256, i32),
+    "R0": (4096, f16), "UI": (1024, i32), "PI": (512, i32), "NBI": (256, i32),
     "BDI": (8, i32), "Lo": (256, u16), "bo": (8, u16), "SX": (384, f16), "SY": (384, f16), "LX": (768, f16),
     "LY": (768, f16), "SP": (128, b16), "SW": (128, f32), "PX": (2048, f32), "LT": (ZC, f32), "Z2": (6 * ZC, f32), "ZW": (3 * ZC, f32),
     "SS": (1024, b16), "AI": (256, b16), "ND": (512, b16),
-    "cgx": (1024, f16), "cgy": (1024, f16), "CDX": (1024, b16), "CDY": (1024, b16), "cb": (1024, f32),
+    "cgx": (1024, f16), "cgy": (1024, f16), "CD": (2048, b16), "cb": (1024, f32),
     "EQ": (512, b16), "xa": (256, f16),
     "O1": (64, u16), "O2": (64, u16), "UL": (64, f16),
-    "CL": (64, f16), "FB": (128, b16), "dL": (128, b16), "sqL": (128, b16), "tL": (64, b16), "KY": (256, f32), "PVL": (384, f32),
+    "CL": (64, f16), "FB": (256, b16), "dL": (192, b16), "sqL": (128, b16), "KY": (256, f32), "PVL": (384, f32),
     "ef": (256, b16), "hn": (128, b16), "t1": (128, f16), "c16": (128, f16),
     "C16": (128, f16), "Cn": (128, f16), "O3": (24, u16), "Oc": (24, u16), "Oxy": (48, u16),
     "cf": (40, f32), "dum": (8, f32), "LTc": (128, f32), "AL": (384, b16), "DN": (128, b16), "FE": (512, b16),
-    "NV": (128, f32), "NC": (256, f32), "VJ": (256, f32), "EP": (128, b16), "ED": (768, f32),
-    "nq": (384, f32), "ES": (768, b16), "EWC": (384, f32), "EQq": (384, f32), "EM": (1152, f16), "eg": (512, f16),
+    "NV": (256, f16), "NC": (256, f32), "VJ": (256, f32), "EP": (128, b16), "ED": (768, f32),
+    "nq": (384, f32), "ES": (768, b16), "EWC": (384, f32), "EQq": (384, f16), "EM": (1152, f16), "eg": (512, f16),
     "EA": (512, f32), "em": (256, f16), "enz": (256, b16), "G8": (144 * 8, b16),
     "ci": (16, i32), "cj": (24, i32), "col": (40, f32), "RM": (16, f32), "e8": (8, f32),
     "IX": (256, b16), "IG": (128, b16), "IH": (128, b16),
     "IDS": (128 * 10, b16), "ST": (256, f16), "EB": (1024, b16), "F32": (128 * 10, f32), "GSB": (144 * 4, b16), "BO": (256, b16),
-    "BR": (2048, b16), "NB": (128 * 4, b16), "OX": (1024, b16), "WV": (1136, b16), "NXR": (896, b16), "PGm": (1024, b16),
-    "RB": (128 * 5, b16), "HB": (256, b16), "TRI": (256, b16), "TRc": (512, b16), "CM": (240, b16), "eps": (512, b16),
+    "BR": (2048, b16), "NB": (128 * 4, b16), "OX": (1024, b16), "WV": (272, b16), "HBR": (1024, b16), "PGm": (1024, b16),
+    "RB": (128 * 5, b16), "HB": (512, b16), "TRI": (256, b16), "TRc": (512, b16), "CM": (240, b16), "eps": (512, b16),
+    "run": (512, b16),
 }
-ALIAS = {"XY16": ("Q16", 0, 1024), "PI2": ("NZ", 0, 1024), "PT": ("Q16", 1024, 1024), "tc": ("EQ", 0, 256), "Zp": ("cgx", 0, 512), "Zt": ("cgx", 512, 512),
-         "G1": ("cgx", 0, 1024), "csg": ("CDX", 0, 1024), "eq2": ("CDY", 0, 1024), "PG": ("RR", 0, 4096), "eab": ("EA", 0, 256),
-         "one": ("CDY", 0, 1024), "one2": ("CDY", 0, 1024), "SH": ("ES", 0, 320), "dc": ("ND", 0, 512), "sq": ("SS", 512, 512),
-         "tb": ("CDX", 0, 1024), "PP": ("cb", 0, 1024), "wout": ("ZW", 0, 512), "EMs": ("nq", 0, 384), "LDI": ("PI", 0, 512),
+ALIAS = {"XY16": ("Q16", 0, 1024), "PI2": ("NT", 0, 1024), "PT": ("Q16", 1024, 1024), "tc": ("EQ", 0, 256), "Zp": ("cgx", 0, 512), "Zt": ("cgx", 512, 512),
+         "G1": ("cgx", 0, 1024), "G2": ("R0", 0, 1024), "csg": ("CD", 0, 1024), "eq2": ("CD", 1024, 1024), "CDX": ("CD", 0, 1024),
+         "CDY": ("CD", 1024, 1024), "PG": ("RR", 0, 4096), "eab": ("EA", 0, 256),
+         "one": ("CD", 1024, 1024), "SH": ("ES", 0, 320), "dc": ("ND", 0, 512), "sq": ("SS", 512, 512),
+         "PP": ("cb", 0, 1024), "wout": ("Z2", 0, 512), "EMs": ("nq", 0, 384), "LDI": ("PI", 0, 512),
          "vio": ("eg", 0, 384), "CI": ("UI", 0, 64), "ia": ("UI", 64, 128), "ib": ("UI", 192, 64), "ic": ("UI", 256, 64),
          "BI": ("UI", 320, 128), "BJ": ("UI", 448, 128)}
 PLACE = {}
@@ -44,24 +46,31 @@ for _k, (_w, _d) in _B.items():
         _o = SCRATCH.get("pool_" + _d, (0, [128, 0]))[1][1]
         PLACE[_k] = ("pool_" + _d, _o)
         SCRATCH["pool_" + _d] = ("sbuf", [128, _o + (_w + 15) // 16 * 16], _d)
-for _i in range(8):
-    SCRATCH["P%d" % _i] = ("psum", [128, 512], f32)
+for _i in range(4):
+    SCRATCH["P%d" % _i] = ("psum", [128, 1024], f32)
 NDMA = 130
-SEMAPHORES = ["qt", "qv", "qa", "qg", "ls", "aP", "aW"] + ["a%s%d" % (_c, _i) for _c in "xy" for _i in range(3)] \
+SEMAPHORES = ["qt", "qv", "qa", "qg", "ls", "aP", "aW0", "aW1"] + ["a%s%d" % (_c, _i) for _c in "xy" for _i in range(3)] \
     + ["d%d" % _i for _i in range(NDMA)]
 SZ = {f32: 4, f16: 2, b16: 2, i32: 4, u16: 2}
 CY = 0.83e-3 * 1.05
 GA = 1.56
-HOP = 0.12
-DLAT = 2.1
+HOP = 0.17
+COSTS = [((CY, GA, 3.8, 2.0, 1.15, 0.25, 1.0, 1.0, 5.5), HOP, 1.0),
+         ((0.83e-3 * 1.35, 1.9, 5.0, 2.4, 1.6, 0.25, 1.2, 1.5, 6.5), 0.16, 0.5),
+         ((0.83e-3 * 1.1, 1.3, 3.0, 2.9, 2.0, 0.4, 1.5, 2.5, 8.0), 0.2, 0.8)]
 BIG = 65536.0
-GROUPS = [((0, 1), 2, 1), ((2, 3), 2, 1), ((4, 5), 2, 1), ((6, 7), 1, 1)]
+GROUPS = [((0, 1), 1, 0), ((2, 3), 2, 0), ((4, 5), 1, 0), ((6, 7), 1, 0)]
 GROUPS = [GROUPS, GROUPS, GROUPS]
 ZSUM = ((0,), (1,), (2,))
-TRIES = 5000
-SEED = 1
+TRIES = 400
+STARTS = (2,)
+MILE = 2.0
+TURNS = 6
+HEAT = 0.03
+POLISH = 4
+MEAN = 0.3
 RES = 3
-OPT = {"sign": "a", "s1dma": 1, "flexg": 1, "gmv": 1}
+OPT = {"int": 0, "early": 1, "wide": 0, "scan": (4, 5, 6, 7), "init": 1, "s1dma": 1, "flexg": 1, "gmv": 1}
 
 
 def S(name, a=0, b=None, step=1, p=None):
@@ -99,17 +108,18 @@ def sub(x, a, b, step=1, p=None):
     return ("ap", x[1], x[2] + a, x[2] + b, step, p)
 
 
-def build():
+def build(CY, GA, SCAT, DLAT, ACC, ISSUE, GISSUE, CALL, FAR):
     ops = []
     nb = [0]
     nd = [0]
     tag = ["setup"]
+    sent = []
 
-    def bank():
+    def bank(k=1):
         nb[0] += 1
-        return "@%d" % nb[0]
+        return ("@%d" if k == 1 else "@D%d") % nb[0]
 
-    def add(alts, rd, wr, lat=0.0, after=()):
+    def add(alts, rd, wr, lat=0.0, after=(), move=0.0):
         r, w = [], []
         for x in rd:
             r += [x[1], x[2]] if x[0] == "ind" else [x]
@@ -119,13 +129,13 @@ def build():
                 r.append(x[2])
             else:
                 w.append(x)
-        ops.append(dict(alts=alts, rd=r, wr=w, lat=lat, after=list(after), tag=tag[0]))
+        ops.append(dict(alts=alts, rd=r, wr=w, lat=lat, after=list(after), tag=tag[0], move=move))
         return len(ops) - 1
 
     def vcost(out, ins, two):
         n = width(ins[0]) if ins else width(out)
         if out[0] == "ind":
-            return 0.05 + 3.8 * n * CY
+            return 0.05 + SCAT * n * CY
         if ins and ins[0][0] == "ind":
             return 0.05 + GA * n * CY
         if two:
@@ -182,20 +192,24 @@ def build():
     def relu(out, a):
         return add([a_act(out, a, F.Relu), v_ts(out, a, 0.0, A.max)], [a], [out])
 
+    def over(out, a, c, sign=1.0):
+        return add([v_ts(out, a, sign * c, A.is_gt if sign > 0 else A.is_lt), a_act(out, a, F.Relu, bias=-c, scale=sign)], [a], [out])
+
     def nonzero(out, a):
         return add([v_ts(out, a, 0.0, A.is_gt), a_act(out, a, F.Sign)], [a], [out])
 
-    def iota(out, pat, base, cm=0):
+    def iota(out, pat, base, cm=0, after=()):
         kw = {} if _B[out[1]][1] == i32 else {"allow_small_or_imprecise_dtypes": True}
-        return add([("g", "iota", (out, pat, base, cm), kw, 0.13 + 2 * width(out) * CY)], [], [out])
+        return add([("g", "iota", (out, pat, base, cm), kw, 0.13 + 2 * width(out) * CY)], [], [out], after=after)
 
-    def asel(out, a, pat, base, op=A.is_equal):
-        return add([("g", "affine_select", (out, a, pat, op, 0.0, base, 1), {}, 0.17 + 2 * width(out) * CY)], [a], [out])
+    def asel(out, a, pat, base, op=A.is_equal, after=()):
+        return add([("g", "affine_select", (out, a, pat, op, 0.0, base, 1), {}, 0.17 + 2 * width(out) * CY)], [a], [out],
+                   after=after)
 
-    def gmv(out, a):
+    def gmv(out, a, turn=0):
         n = width(out)
         alts = [("g", "affine_select", (out, a, [[0, n]], A.is_ge, 0.0, 0, 1), {}, 0.17 + 2 * n * CY), a_act(out, a, F.Copy), v_cp(out, a)]
-        return add(alts if OPT["gmv"] else alts[1:], [a], [out])
+        return add(alts[turn:] + alts[:turn], [a], [out])
 
     def mm(groups, after=(), start=True, stop=True):
         rd, wr, c = [], [], 0.03
@@ -206,17 +220,22 @@ def build():
                 c += max(min(64, width(l)), width(r)) * (4 if size(r) == 4 else 1) * CY / 2
         return add([("t", "mm", (groups, start, stop), {}, c)], rd, wr, after=after)
 
-    def dma(eng, out, a, acc=False, lat=2.2):
+    def dma(eng, out, a, acc=False, lat=2.2, after=()):
         nd[0] += 1
-        if acc:
-            lat = DLAT + 0.27 * width(out) * size(out) / 1024
-        return add([(eng, "dma", (out, a, acc, "d%d" % (nd[0] - 1)), {}, 1.0 if eng == "g" else 0.1)],
-                   aps(a) + ([out] if acc else []), aps(out), lat=lat)
+        x = out if is_ap(out) else a
+        return add([(eng, "dma", (out, a, acc, "d%d" % (nd[0] - 1)), {}, GISSUE if eng == "g" else ISSUE)],
+                   aps(a) + (aps(out) if acc else []), aps(out), lat=DLAT, after=after,
+                   move=0.21 * (ACC if acc else 1.0) * width(x) * size(x) / 1024)
+
+    def dmas(eng, pairs, rd, wr, move):
+        nd[0] += 1
+        return add([(eng, "dmas", (pairs, "d%d" % (nd[0] - 1)), {}, ISSUE * len(pairs))], rd, wr, lat=DLAT, move=move)
 
     def send(parts):
-        i = add([("g", "send", (parts,), {}, 1.0)], [p[0] for p in parts], [])
+        i = add([("g", "send", (parts,), {}, CALL)], [p[0] for p in parts], [])
+        sent[:] = sent or [i]
         for src, nm, a, w, sem, ne in parts:
-            add([("r", "recv", (sem, ne), {}, 0.0)], [], [S(nm, a, a + 3 * w)], lat=4.5, after=[i])
+            add([("r", "recv", (sem, ne), {}, 0.0)], [], [S(nm, a + d * w, a + d * w + width(src)) for d in range(3)], lat=FAR, after=[i])
 
     def blk(name, k, w=128):
         return S(name, k * w, (k + 1) * w)
@@ -235,12 +254,14 @@ def build():
     iota(S("ci", 0, 8), [[0, 8]], 0, 1)
     iota(S("ci", 8, 16), [[1, 8]], 0, 1)
     iota(S("IX"), [[1, 256]], 0)
-    for k, m in enumerate((15, 112, 127, 7, 16, 120)):
-        ts(c1("cj", k), c1("ci", 0), m, A.bitwise_and)
-    ts(c1("cj", 6), c1("ci", 0), 3, A.arith_shift_right)
+    ts(c1("ci", 0), c1("ci", 2), 15, A.bitwise_and)
+    ts(c1("ci", 1), c1("ci", 2), 112, A.bitwise_and)
+    ts(c1("ci", 3), c1("ci", 2), 120, A.bitwise_and)
+    ts(c1("ci", 4), c1("ci", 2), 3, A.arith_shift_right)
     ts(S("cj", 8, 16), S("ci", 8, 16), 7, A.bitwise_and)
-    cp(S("col", 0, 7), S("cj", 0, 7))
-    rcol, gcol, pcol, kcol, bcol, ocol, hcol = (c1("col", k) for k in range(7))
+    cp(S("col", 0, 5), S("ci", 0, 5))
+    cp(c1("col", 5), c1("cj", 8))
+    rcol, gcol, pcol, ocol, hcol, kcol = (c1("col", k) for k in range(6))
     IX = S("IX", 0, 128)
     ts(S("RM"), S("IX", 0, 16), rcol, A.is_equal)
     ts(S("col", 16, 24), S("cj", 8, 16), ocol, A.add)
@@ -249,18 +270,17 @@ def build():
     ts(wcol, lo8, -1023.0, A.mult, 1024.0, A.add)
     ts(c1("col", 11), c1("RM", 8), 8.0, A.mult, c1("RM", 0), A.add)
     tt(ccol, c1("col", 11), c1("RM", 4), A.add)
-    ts(keyc, kcol, -512.0, A.mult, 3584.0 - (9 if OPT["sign"] == "v" else 1) * 4096.0, A.add)
+    ts(keyc, kcol, -512.0, A.mult, 3584.0 - 9 * 4096.0, A.add)
     ts(c1("col", 12), gcol, 15.0, A.add)
-    ts(c1("col", 13), pcol, 16.0, A.add)
-    ts(c1("col", 14), bcol, 0.0, A.is_equal)
-    ts(c1("col", 15), bcol, 16.0, A.is_equal)
     ts(S("PW", 0, 512), S("PI"), c1("RM", 5), A.add)
-    ts(S("PW", 896, 912), S("RM"), 0.0, A.mult, c1("RM", 4), A.add)
-    ts(S("PW", 896, 912), S("PW", 896, 912), 896.0, A.mult)
+    ts(c1("col", 13), c1("RM", 4), 664.0, A.mult)
+    ts(c1("col", 14), c1("RM", 8), 29.0, A.mult, c1("col", 13), A.add)
+    ts(S("PW", 896, 912), S("RM"), 0.0, A.mult, c1("col", 14), A.add)
     cp(S("bo"), S("BDI"))
     mv(S("SP"), IND(S("PW", 0, 512), S("bo")))
-    cp(S("XW", 0, 512), S("UI", 0, 512))
-    cp(S("YW", 0, 512), S("UI", 512, 1024))
+    whole = (lambda out, a: mv(out, a, vfirst=True)) if OPT["int"] else cp
+    whole(S("XW", 0, 512), S("UI", 0, 512))
+    whole(S("YW", 0, 512), S("UI", 512, 1024))
 
     def border(t, more):
         mv(blk("SX", t), IND(S("XW", 0, 512), S("bo")))
@@ -268,14 +288,14 @@ def build():
         ne = 2 if more else 4
         send(more + [(blk("SX", t), "LX", 384 * (t % 2), 128, "ax%d" % t, ne),
                      (blk("SY", t), "LY", 384 * (t % 2), 128, "ay%d" % t, ne)])
-        mv(S("XW", 512, 896), blk("LX", t % 2, 384))
-        mv(S("YW", 512, 896), blk("LY", t % 2, 384))
-    border(0, [(S("SP"), "PW", 512, 128, "aP", 4)])
+        gmv(S("XW", 512, 896), blk("LX", t % 2, 384), 1)
+        gmv(S("YW", 512, 896), blk("LY", t % 2, 384), 1)
+    send([(S("SP"), "PW", 512, 128, "aP", 8)])
     mv(S("SW"), IND(S("WW", 0, 512), S("bo")))
-    send([(S("SW"), "WW", 512, 128, "aW", 8)])
+    border(0, [(blk("SW", u, 64), "WW", 512 + 64 * u, 128, "aW%d" % u, 2) for u in range(2)])
     for nm in ("XW", "YW", "WW"):
         ms(S(nm, 896, 904), 0.0)
-    ms(S("one"), 1.0)
+    ms(S("one", 0, 512), 1.0)
     iota(S("IG"), [[16, 8], [0, 16]], 0)
     iota(S("IH"), [[1, 16], [0, 8]], 0)
     I, NI, I32x, IBn, I896, N896, ILO, Ith, IM, NIM = (blk("IDS", k) for k in range(10))
@@ -289,25 +309,32 @@ def build():
     mv(NI32, NI)
     for m, k in ((RT1, 1), (RT2, 2), (RT4, 4)):
         ts(m, IX, c1("col", 16 + k), A.is_equal)
-    for k in range(1, 8):
-        ts(blk("NXR", k - 1), IX, c1("col", 16 + k), A.is_equal, -1.0, A.mult)
-    NXR = [NI] + [blk("NXR", k) for k in range(7)]
+    ms(S("DD", 0, 1024), 0.0)
+    dma("s", S("DD", 1024, 2048), S("DD", 0, 1024))
+    for u in range(1, 4):
+        dma("s", blk("DD", u, 2048), blk("DD", 0, 2048))
+
+    def rows_of(dst, src, k, step):
+        w = width(src)
+        dma("s", S(dst, 0, k * w), S("DD", 0, k * w))
+        dmas("s", [(S(dst, w * u, w * u + w, 1, (u, 128, step)), sub(src, 0, w, 1, (u, 128, step))) for u in range(k)],
+             [src], [S(dst, 0, k * w)], 0.3)
     for h, m in enumerate((SH0, SH1)):
         asel(m, S("one", 0, 128), [[-16, 8], [1000, 2], [-1, 8]], -1000 * h)
     GSk = []
-    for k, c in enumerate((wcol, 4096.0 if OPT["sign"] == "v" else -2048.0, 1.0 / 16, ccol)):
+    for k, c in enumerate((wcol, 4096.0, 1.0 / 16, ccol)):
         ts(blk("GSB", k, 144), S("IX", 0, 144), c1("col", 12), A.is_equal, c, A.mult)
         GSk.append([S("GSB", 144 * k + 15 - r, 144 * k + 143 - r) for r in range(16)])
-    GSW, GSK, GS16, GSC = GSk
+    GSK, GS16, GSC = GSk[1:]
     BO, BO8 = blk("BO", 0), blk("BO", 1)
     ts(BO, S("IG"), gcol, A.is_equal)
     ts(BO8, S("IG"), gcol, A.is_equal, lo8, A.mult)
-    for h in range(2):
-        asel(blk("BR", h, 1024), S("one"), [[-1, 8], [-16, 8], [0, 16]], -8 * h)
+    for h in range(4):
+        asel(blk("BR", h, 512), S("one", 0, 512), [[-1, 4], [-16, 8], [0, 16]], -4 * h, after=sent)
     BR = [blk("BR", r) for r in range(16)]
-    NB0, NB8, NB5, NB4 = (blk("NB", k) for k in range(4))
-    for m, r, c in ((NB0, 0, -1.0), (NB8, 8, -1.0), (NB5, 5, -896.0), (NB4, 4, -1.0)):
-        mv(m, BR[r], scale=c, vfirst=True)
+    NB0, NB8, NB5 = (blk("NB", k) for k in range(3))
+    for m, r, c in ((NB0, 0, -1.0), (NB8, 8, -1.0), (NB5, 5, -896.0)):
+        ts(m, BO, c1("RM", r), A.mult, c, A.mult)
     mv(BF0, BO, scale=c1("RM", 0))
     mv(BF8, BO, scale=c1("RM", 8))
     for xy in range(2):
@@ -320,8 +347,12 @@ def build():
     RB8 = blk("RB", 4)
     mv(RB8, RB[8, 1], scale=8.0)
     for h in range(2):
-        asel(blk("HB", h), S("one", 0, 128), [[-16, 8], [0, 2], [-1, 8]], -8 * h)
-    asel(S("PGm"), S("one"), [[-16, 8], [0, 128]], 0)
+        asel(blk("HB", h), S("one", 0, 128), [[-16, 8], [0, 2], [-1, 8]], -8 * h, after=sent)
+    mv(blk("HB", 1, 256), blk("HB", 0, 256), scale=-1.0, vfirst=True)
+    for h in range(2):
+        asel(blk("PGm", h, 512), S("one", 0, 512), [[-16, 4], [0, 128]], -64 * h, after=sent)
+        asel(blk("HBR", h, 512), S("one", 0, 512), [[-1, 4], [-8, 16], [0, 8]], -4 * h, after=sent)
+        asel(blk("EB", h, 512), S("one", 0, 512), [[-1, 32], [0, 16]], -32 * h, after=sent)
     ts(blk("TRI", 0), S("IH"), hcol, A.is_equal, -1.0, A.mult)
     asel(blk("TRI", 1), blk("TRI", 0), [[-1, 128]], 0, A.is_ge)
     tt(blk("TRI", 1), blk("TRI", 0), blk("TRI", 1), A.subtract)
@@ -329,28 +360,17 @@ def build():
     ts(blk("TRc", 0), IX, pcol, A.is_le, 4096.0, A.mult)
     for u in range(1, 4):
         dma("s", blk("TRc", u), blk("TRc", 0))
-    ms(S("CM"), 0.0)
-    ms(S("CM", 112, 128), -16.0)
     for b in range(2):
-        ts(blk("SH", b, 160), S("IX", 0, 160), c1("col", 13), A.is_equal, c1("col", 14 + b), A.mult)
-    ms(S("DD", 0, 1024), 0.0)
-    dma("s", S("DD", 1024, 2048), S("DD", 0, 1024))
-    for u in range(1, 4):
-        dma("s", blk("DD", u, 2048), blk("DD", 0, 2048))
+        asel(blk("SH", b, 160), S("one", 0, 160), [[-32, 5], [1000 - 2000 * b - 16, 2], [-1, 16]], 16 - 1000 + 1000 * b)
     ts(S("dum"), S("IX", 0, 8), 16.0, A.mult, rcol, A.add)
     ts(S("dum"), S("dum"), 520.0, A.add)
-    ts(S("e8"), S("IX", 0, 8), kcol, A.is_equal)
-    for k in range(8):
-        mv(blk("G8", k, 144), blk("GSB", 0, 144), scale=c1("e8", k), vfirst=True)
-    iota(S("vio"), [[-1, 3], [4, 128]], 3)
-    dma("s", S("WV"), S("DD", 0, 1136))
-    for u in range(8):
-        dma("s", S("WV", 128 * u + 112, 128 * u + 128), sub(I896, 16 * u, 16 * u + 16))
-    iota(S("Z2", 0, 2 * ZC), [[0, 2 * ZC]], 0)
-    for s in (1, 2):
-        dma("s", blk("Z2", s, 2 * ZC), S("Z2", 0, 2 * ZC))
-    dma("s", S("ZW", 0, 2 * ZC), S("Z2", 0, 2 * ZC))
-    dma("s", S("ZW", 2 * ZC, 3 * ZC), S("Z2", 0, ZC))
+    rows_of("G8", S("GSB", 0, 144), 8, 8)
+    iota(S("vio"), [[-1, 3], [4, 128]], 3, after=sent)
+    dma("s", S("CM"), S("DD", 0, 240))
+    ms(S("CM", 112, 128), -16.0)
+    iota(S("ZW", 0, ZC), [[0, ZC]], 0, after=sent)
+    dmas("s", [(blk("ZW", u, ZC), S("ZW", 0, ZC)) for u in (1, 2)] + [(blk("Z2", u, ZC), S("ZW", 0, ZC)) for u in range(6)],
+         [S("ZW", 0, ZC)], [S("ZW", ZC, 3 * ZC), S("Z2")], 4.4)
     ms(S("Zp"), 0.0)
     ms(S("LT", 512, ZC), 896.0)
     for k in range(8):
@@ -366,17 +386,21 @@ def build():
     cp(S("Lo"), S(bk, 0, 256))
     ts(S("AI"), S(bk, 0, 256), 896.0, A.not_equal, 896.0, A.mult)
     for xy in range(2):
-        cp(S("XY16", xy, 1024, 2), blk("UI", xy, 512))
+        mv(S("XY16", xy, 1024, 2), S(("XW", "YW")[xy], 0, 512))
         mv(S("PI2", xy, 1024, 2), S("PW", 0, 512), scale=c1("RM", 8 * xy))
     for src, dst, m in (("XY16", "UT", I), ("PI2", "PT", BO)):
         for h in range(2):
             bk = bank()
             mm([(S(bk, 128 * u, 128 * u + 128), [(blk(src, 4 * h + u), m)]) for u in range(4)])
             mv(blk(dst, h, 512), S(bk))
+    dma("s", S("WV"), S("DD", 0, 272))
+    dmas("s", [(S("WV", 32 * u + 16, 32 * u + 32), sub(I896, 16 * u, 16 * u + 16)) for u in range(8)], [I896], [S("WV")], 0.3)
     dma("s", S("LDI"), "ld")
-    iota(S("LD2", 0, 1024, 2), [[0, 512]], 0)
+    iota(S("LD2", 0, 1024, 2), [[0, 512]], 0, after=sent)
     cp(S("LD2", 1, 1024, 2), S("LDI"))
     ms(S("eps"), 1.0 / 64)
+    iota(S("run"), [[0, 64], [1, 8]], 0, after=sent)
+    ts(S("run"), S("run"), 1.0, A.min)
     bk = bank()
     mm([(S(bk, 128 * t + 64 * xy, 128 * t + 64 * xy + 64),
          [(RB[8 * xy, h], S("PW", 256 * h + 3 - t, 256 * h + 256, 4)) for h in range(2)]) for t in range(3) for xy in range(2)])
@@ -385,7 +409,6 @@ def build():
     mm([(S(bk, 128 * t, 128 * t + 128), [(ILO, blk("vio", t))] + [(m, S("PW", 3 - t, 512, 4)) for m in (RB[0, 1], RB8, NB5)])
         for t in range(2)])
     mv(S("VJ", 0, 256), S(bk, 0, 256))
-    asel(S("EB"), S("one2"), [[-1, 64], [0, 16]], 0)
 
     def spread(x, scale, slot):
         n = width(x)
@@ -395,11 +418,14 @@ def build():
         xt = S("ST", 128 * (slot // 2 % 2), 128 * (slot // 2 % 2) + 128, 1, rows)
         mv(xt, S(bk, 0, 128, 1, rows), scale=scale)
 
-        def make(u):
-            bn = bank()
-            mm([(S(bn), [(xt, S("EB", 512 * u, 512 * u + 512, 1, rows))])])
-            return bn
-        return [lambda u=u: make(u) for u in range(n // 32)]
+        def make(lo, hi):
+            bn = bank(hi - lo)
+            mm([(S(bn, 512 * (u - lo), 512 * (u - lo) + 512), [(xt, S("EB", 512 * u, 512 * u + 512, 1, rows))]) for u in range(lo, hi)])
+            return S(bn, 0, 512 * (hi - lo))
+        return make
+
+    def units(a, b, wide):
+        return [(a, b)] if wide else [(B, B + 1) for B in range(a, b)]
     tag[0] = "pos"
     for chunks, _, _ in GROUPS[0]:
         a, b = chunks[0], chunks[-1] + 1
@@ -407,93 +433,98 @@ def build():
     bk = bank()
     mm([(S(bk), [(GSC[8 + k], S("PG", k, 4096, 8)) for k in range(8)])])
     tt(S("LT", 0, 512), S(bk), S("LT", 0, 512), A.add)
-    bk = bank()
-    mm([(S(bk, 8 * u, 8 * u + 8), [(blk("PG", u), sub(NB4, 0, 128, 16))]) for u in range(32)])
-    ts(S("SS", 0, 256), S(bk, 0, 256), 0.0, A.is_equal)
     for chunks, _, _ in GROUPS[0]:
         a, b = chunks[0], chunks[-1] + 1
-        for B in chunks:
+        for lo, hi in units(a, b, OPT["wide"] & 1):
             for xy, nm, m in ((1, "DYT", NB8), (0, "DXT", NB0)):
-                bk = bank()
-                mm([(S(bk, 128 * j, 128 * j + 128), [(OX[xy][j], blk("PT", B)), (blk("PG", 4 * B + j), m)]) for j in range(4)])
-                mv(blk(nm, B, 512), S(bk))
+                bk = bank(hi - lo)
+                mm([(S(bk, 128 * u, 128 * u + 128), [(OX[xy][u % 4], blk("PT", lo + u // 4)), (blk("PG", 4 * lo + u), m)])
+                    for u in range(4 * (hi - lo))])
+                mv(S(nm, 512 * lo, 512 * hi), S(bk, 0, 512 * (hi - lo)))
         for xy, nm in enumerate(("DXT", "DYT")):
             act(S("sq", 256 * xy + 32 * a, 256 * xy + 32 * b), S(nm, 512 * a, 512 * b, 16), F.Square, scale=8.0)
         tt(S("tc", 32 * a, 32 * b), S("sq", 32 * a, 32 * b), S("sq", 256 + 32 * a, 256 + 32 * b), A.add)
-        for B, bk in zip(chunks, spread(S("tc", 32 * a, 32 * b), -1.0, a)):
-            mv(blk("NT", B, 512), S(bk()))
+        mk = spread(S("tc", 32 * a, 32 * b), -1.0, a)
+        for lo, hi in units(a, b, OPT["wide"] & 1):
+            mv(S("NT", 512 * lo, 512 * hi), mk(lo - a, hi - a))
     for xy, nm in enumerate(("DXT", "DYT")):
         mv(blk("dc", xy, 256), S(nm, 0, 4096, 16), scale=-1.0 / 32)
-    for u in range(16):
-        rows = (8 * u, 8 * u + 8, 1)
-        dma("s", S("DD", 512 * u, 512 * u + 512, 1, rows), S("dc", 0, 512, 1, rows))
+    dmas("s", [(S("DD", 512 * u, 512 * u + 512, 1, (8 * u, 8 * u + 8, 1)), S("dc", 0, 512, 1, (8 * u, 8 * u + 8, 1)))
+               for u in range(16)], [S("dc")], [S("DD")], 1.0)
 
     def reg(bk, k, w=128):
         return S(bk, w * k, w * k + w)
 
-    def step1(t):
-        rho = 3 - t
-        half = lambda nm, h: S(nm, 256 * h + rho, 256 * h + 256, 4)
-        act_ = lambda nm: S(nm, rho, 512, 4)
-        for xy, nm in enumerate(("XW", "YW")):
-            mv(blk("xa", xy), act_(nm))
-        ts(blk("ef", 0), act_("LT"), 896.0, A.is_equal)
+    def rows(t):
         bk = bank()
-        mm([(reg(bk, 0), [(BO8, blk("ef", 0))])])
-        ts(S("hn"), reg(bk, 0), 0.0, A.is_equal)
+        mm([(S(bk, 0, 64), [(m, S("LT", 256 * h + 3 - t, 256 * h + 256, 4)) for h, m in enumerate((SH0, SH1))])])
+        return S(bk, 0, 64)
+
+    def named(t, buf):
+        gather(S(buf), IND(S("LT", 0, 520), S("O1")))
         bk = bank()
-        mm([(S(bk, 0, 64), [(SH0, half("LT", 0)), (SH1, half("LT", 1))])])
-        ts(S("O1"), S(bk, 0, 64), 512.0, A.min)
-        mv(S("UL"), S(bk, 0, 64))
-        gather(S("G1"), IND(S("LT", 0, 520), S("O1")))
-        bk = bank()
-        mm([(S(bk, 0, 64), [(S("G8", 144 * ((r + t) % 8) + 15 - r, 144 * ((r + t) % 8) + 143 - r), S("G1", r, 1024, 16))
+        mm([(S(bk, 0, 64), [(S("G8", 144 * ((r + t) % 8) + 15 - r, 144 * ((r + t) % 8) + 143 - r), S(buf, r, 1024, 16))
                             for r in range(16)])])
-        cp(S("CI"), S(bk, 0, 64))
+        return S(bk, 0, 64)
+
+    def candidates(t):
+        rho = 3 - t
+        bk = rows(t)
+        ts(S("O1"), bk, 512.0, A.min)
+        if t == 0 or not OPT["early"]:
+            mv(S("UL"), bk)
+        cp(S("CI"), named(t, "G1"))
         ts(S("ib"), S("CI"), 1023, A.bitwise_and)
         ts(S("O2"), S("ib"), 511.0, A.min)
         cp(S("CL"), S("ib"))
         for xy in range(2):
             ts(blk("ia", xy, 64), S("CI"), 10 + 3 * xy, A.arith_shift_right, 7, A.bitwise_and)
-        tt(S("dL"), S("ia"), blk("PVL", t), A.subtract)
-        act(S("sqL"), S("dL"), F.Square, scale=8.0)
-        tt(S("tL"), blk("sqL", 0, 64), blk("sqL", 1, 64), A.add)
+        tt(S("dL", 0, 128), S("ia"), blk("PVL", t), A.subtract)
+        act(S("sqL"), S("dL", 0, 128), F.Square, scale=8.0)
+        tt(blk("dL", 2, 64), blk("sqL", 0, 64), blk("sqL", 1, 64), A.add)
         ts(S("ic"), S("CI"), 3, A.bitwise_and)
         ts(blk("FB", 0, 64), S("ic"), float(rho), A.is_equal)
-        ts(blk("FB", 1, 64), S("CL"), 512.0, A.is_ge)
-        bk = bank()
-        mm([(reg(bk, m, 64), [(I, S("CL")), (NXR[m], S("UL"))]) for m in range(8)])
-        ts(S("EQ"), S(bk), 0.0, A.is_equal)
-        gather(S("cgy"), IND(S("YW", 0, 512), S("O2")))
-        gather(S("cgx"), IND(S("XW", 0, 512), S("O2")))
+        over(blk("FB", 1, 64), S("CL"), 511.0)
         for h in range(2):
-            H = lambda nm: blk(nm, h, 512)
             for xy, nm in ((1, "CDY"), (0, "CDX")):
                 bk = bank()
                 mm([(reg(bk, k, 64), [(BR[8 * h + k], blk("dL", xy, 64))]) for k in range(8)])
-                mv(H(nm), S(bk))
-            bks = []
-            for xy, nm in ((1, "cgy"), (0, "cgx")):
-                bks.append(bank())
-                mm([(reg(bks[-1], k, 64), [(I, S(nm, 8 * h + k, 1024, 16)), (NI, blk("xa", 2 * xy + h, 64))]) for k in range(8)])
-            tt(H("cb"), S(bks[0]), H("CDY"), A.mult)
-            if OPT["s1dma"]:
-                tt(H("PX"), S(bks[1]), H("CDX"), A.mult)
-                dma("g", H("PX"), H("cb"), acc=True, lat=DLAT)
-                act(H("cb"), H("PX"), F.Abs)
-            else:
-                tt(S(bks[1]), S(bks[1]), H("CDX"), A.mult)
-                tt(S(bks[1]), S(bks[1]), H("cb"), A.add)
-                act(H("cb"), S(bks[1]), F.Abs)
-            bk = bank()
-            if OPT["sign"] == "v":
-                mm([(reg(bk, k, 64), [(BR[8 * h + k], blk("tL", 0, 64))]) for k in range(8)])
-                tt(H("csg"), S(bk), H("cb"), A.is_lt)
-            else:
-                mm([(reg(bk, k, 64), [(BR[8 * h + k], blk("tL", 0, 64)), (NI32, blk("cb", 8 * h + k, 64))]) for k in range(8)])
-                act(H("csg"), S(bk), F.Sign, bias=0.5)
+                mv(blk(nm, h, 512), S(bk))
+
+    def step1(t):
+        rho = 3 - t
+        act_ = lambda nm: S(nm, rho, 512, 4)
+        for xy, nm in enumerate(("XW", "YW")):
+            gmv(blk("xa", xy), act_(nm), 1)
+        over(blk("ef", 0), act_("LT"), 895.0)
         bk = bank()
-        mm([(S(bk, 0, 64), [(I, S("CL"))] + [(IBn, blk("EQ", m, 64)) for m in range(8)] + [(IBn, blk("FB", m, 64)) for m in range(2)]
+        mm([(reg(bk, 0), [(BO8, blk("ef", 0))])])
+        over(S("hn"), reg(bk, 0), -1.0, -1.0)
+        if t and OPT["early"]:
+            mv(S("UL"), rows(t))
+            over(blk("FB", 2, 64), S("UL"), 511.0)
+            over(blk("FB", 3, 64), named(t, "G2"), 896.0 * 1024)
+        bk = bank()
+        mm([(reg(bk, m, 64), [(NI, S("CL")), (blk("HBR", m), S("UL"))]) for m in range(8)])
+        ts(S("EQ"), S(bk), 0.0, A.is_equal)
+        gather(S("cgy"), IND(S("YW", 0, 512), S("O2")))
+        gather(S("cgx"), IND(S("XW", 0, 512), S("O2")))
+        for lo, hi in units(0, 2, OPT["wide"] & 2):
+            H = lambda nm: S(nm, 512 * lo, 512 * hi)
+            rs = range(8 * lo, 8 * hi)
+
+            def fill(terms):
+                bk = bank(hi - lo)
+                mm([(reg(bk, r - 8 * lo, 64), terms(r)) for r in rs])
+                return S(bk, 0, 512 * (hi - lo))
+            by, bx = (fill(lambda r: [(I, S(nm, r, 1024, 16)), (NI, blk("xa", 2 * xy + r // 8, 64))]) for xy, nm in ((1, "cgy"), (0, "cgx")))
+            tt(H("cb"), by, H("CDY"), A.mult)
+            tt(H("PX"), bx, H("CDX"), A.mult)
+            dma("g", H("PX"), H("cb"), acc=True)
+            act(H("cb"), H("PX"), F.Abs)
+            tt(H("csg"), fill(lambda r: [(BR[r], blk("dL", 2, 64))]), H("cb"), A.is_lt)
+        bk = bank()
+        mm([(S(bk, 0, 64), [(I, S("CL"))] + [(IBn, blk("EQ", m, 64)) for m in range(8)] + [(IBn, blk("FB", m, 64)) for m in range(4 if t and OPT["early"] else 2)]
              + [(GSK[r], blk("csg", r, 64)) for r in range(16)])])
         mv(blk("KY", 0, 64), S(bk, 0, 64), bias=keyc)
         for n, m in enumerate((RT1, RT2, RT4)):
@@ -511,7 +542,6 @@ def build():
         O3 = blk("O3", t, 8)
         cp(O3, S(bk, 0, 8))
         mv(blk("cf", 0, 8), S(bk, 0, 8))
-        tt(blk("cf", 1, 8), S("dum"), blk("cf", 0, 8), A.subtract)
         tt(S("C16"), S("c16"), S("t1"), A.add)
         mv(S("Cn"), S("C16"), scale=-1.0)
         for h in range(2):
@@ -519,7 +549,7 @@ def build():
             mm([(reg(bk, k % 4), [(S("C16"), blk("PGm", k)), (blk("PGm", k), S("Cn"))]) for k in range(4 * h, 4 * h + 4)])
             tt(blk("eq2", h, 512), S(bk), S("TRc"), A.is_equal)
         mv(S("LTc"), IND(S("LT", 0, 512), O3))
-        ts(blk("ef", 1), S("LTc"), 896.0, A.is_equal)
+        over(blk("ef", 1), S("LTc"), 895.0)
         bk = bank()
         mm([(reg(bk, 0), [(BO8, blk("ef", 1)), (NI, S("t1"))] + [(S("CM", 112 - 16 * k, 240 - 16 * k), blk("eq2", k)) for k in range(8)])])
         ts(S("DN"), reg(bk, 0), 0.5, A.is_lt)
@@ -527,8 +557,8 @@ def build():
             ts(blk("AL", t), reg(bk, 0), 0.5, A.is_ge)
         bk = bank()
         mm([(S(bk, 0, 8), [(GS16[r], S("DN", r, 128, 16)) for r in range(16)])])
-        tt(blk("cf", 2, 8), S(bk, 0, 8), blk("cf", 1, 8), A.mult)
-        tt(blk("cf", 3, 8), blk("cf", 2, 8), blk("cf", 0, 8), A.add)
+        tt(blk("cf", 2, 8), S(bk, 0, 8), S("dum"), A.mult)
+        tt(blk("cf", 3, 8), blk("cf", 2, 8), blk("cf", 0, 8), A.max)
         cp(blk("Oc", t, 8), blk("cf", 3, 8))
         ts(blk("Oxy", 2 * t, 8), blk("cf", 3, 8), 2.0, A.mult)
         ts(blk("Oxy", 2 * t + 1, 8), blk("cf", 3, 8), 2.0, A.mult, 1.0, A.add)
@@ -544,11 +574,13 @@ def build():
             relu(blk("FE", t, 256), S(bk, 0, 256))
             bk = bank()
             mm([(reg(bk, 0), [(ILO, S("c16"))] + [(m, S("EP")) for m in (RB[0, 1], RB8, NB5)])])
-            tt(S("NV"), reg(bk, 0), blk("FE", 2 * t), A.mult)
-            tt(blk("NC", 0), blk("FE", 2 * t + 1), blk("VJ", t), A.mult)
-            tt(blk("NC", 1), blk("NC", 0), S("LTc"), A.add)
+            tt(blk("NV", 0), reg(bk, 0), blk("FE", 2 * t), A.mult)
+            tt(blk("NV", 1), blk("FE", 2 * t + 1), blk("VJ", t), A.mult)
+            bk = bank()
+            mm([(reg(bk, u), [(I, blk("NV", u)), (I32, x)]) for u, x in enumerate((act_("LT"), S("LTc")))])
+            mv(blk("NC", 1), reg(bk, 1))
             cp(IND(S("LT"), blk("Oc", t, 8)), blk("NC", 1))
-            tt(act_("LT"), act_("LT"), S("NV"), A.add)
+            mv(act_("LT"), reg(bk, 0))
 
     def extra(s0, s1, t):
         ss = range(s0, s1)
@@ -560,7 +592,7 @@ def build():
             for u, s in enumerate(ss) for xy, nm in enumerate(("XW", "YW"))])
         tt(S("EA", 0, 2 * n), S(bk, 0, 2 * n), S("ED", 256 * s0, 256 * s1), A.mult)
         bz = bank()
-        mm([(reg(bz, u), [(I32, blk("EA", 2 * u)), (I32, blk("EA", 2 * u + 1))] + ([(I32, blk("EQq", s))] if s < t else []))
+        mm([(reg(bz, u), [(I32, blk("EA", 2 * u)), (I32, blk("EA", 2 * u + 1))] + ([(I, blk("EQq", s))] if s < t else []))
             for u, s in enumerate(ss)])
         act(S("eab", 0, n), S(bz, 0, n), F.Abs)
         act(S(bz, 0, n), S(bz, 0, n), F.Sign)
@@ -580,20 +612,20 @@ def build():
             tt(em, S("em", 0, n), al, A.mult)
         tt(S("EQq", 128 * s0, 128 * s1), S(bz, 0, n), em, A.mult)
         bk = bank()
-        mm([(reg(bk, 2 * u + xy), [(I32, blk("EQq", s))]) for u, s in enumerate(ss) for xy in range(2)])
+        mm([(reg(bk, 2 * u + xy), [(I, blk("EQq", s))]) for u, s in enumerate(ss) for xy in range(2)])
         tt(S("EA", 0, 2 * n), S(bk, 0, 2 * n), S("ED", 256 * s0, 256 * s1), A.mult)
         for u, s in enumerate(ss):
             o = 2 * ZC * s
             for xy in range(2):
-                mv(S("Z2", o + 2 * (3 - s) + xy, o + 1024, 8), blk("EA", 2 * u + xy))
+                gmv(S("Z2", o + 2 * (3 - s) + xy, o + 1024, 8), blk("EA", 2 * u + xy), 1)
             ts(IND(S("Z2", o, o + 2 * ZC), blk("Oxy", s, 16)), blk("EA", u, 256), -1.0, A.mult, 0.0, A.add)
         if t == 2:
             bk = bank()
             mm([(reg(bk, u), [(I, blk("EM", 3 * r + s)) for r in range(s, 3)]) for u, s in enumerate(ss)])
             mv(S("EMs", 128 * s0, 128 * s1), S(bk, 0, n))
-            for s in ss:
+            for u, s in enumerate(ss):
                 o = ZC * s
-                tt(S("ZW", o + 3 - s, o + 512, 4), blk("EMs", s), blk("EWC", s), A.mult)
+                tt(S("ZW", o + 3 - s, o + 512, 4), reg(bk, u), blk("EWC", s), A.mult)
                 tt(IND(S("ZW", o, o + ZC), blk("Oc", s, 8)), blk("EMs", s), S("WW", 3 - s, 512, 4), A.mult)
         if s0 == 0 and t == 1:
             bk = bank()
@@ -603,7 +635,10 @@ def build():
             tt(blk("NC", 1), reg(bk, 1), blk("NC", 0), A.max)
             cp(IND(S("LT"), blk("Oc", 0, 8)), blk("NC", 1))
 
-    def group(t, chunks, dma1, dma2, acc, wb):
+    def kept(t, B):
+        return B >= 4 and GROUPS[t][B // 2][1] < 2
+
+    def group(t, chunks, dma1, wide, acc, wb):
         a, b = chunks[0], chunks[-1] + 1
         def R(nm, lo=a, hi=b):
             o = (8 * t + lo) % (_B[nm][0] // 512)
@@ -611,46 +646,48 @@ def build():
         C = lambda nm, B: blk(nm, B, 512)
         gather(R("gy"), IND(S("YW"), S("Lo", 32 * a, 32 * b)))
         gather(R("gx"), IND(S("XW"), S("Lo", 32 * a, 32 * b)))
-        for B in chunks:
+        W = lambda nm, lo, hi: S(nm, 512 * lo, 512 * hi)
+        both = t and dma1 == 2
+        for lo, hi in units(a, b, wide & 1):
             bks = []
             for xy, nm in ((1, "gy"), (0, "gx")):
-                bks.append(S(bank()))
-                g_ = R(nm, B, B + 1)
-                mm([(reg(bks[-1][1], j), [(OX[xy][j], blk("UT", B)), (sub(g_, 128 * j, 128 * j + 128), NI)]) for j in range(4)])
-            tt(R("PB", B, B + 1), bks[0], C("DYT", B), A.mult)
-            both = t and dma1 == 2
-            more = [] if both else ([] if dma1 else [R("PB", B, B + 1)]) + ([C("ZB", B)] if t else [])
-            tt(bks[1] if more else R("PX" if both else "ZB", B, B + 1), bks[1], C("DXT", B), A.mult)
+                bks.append(S(bank(hi - lo), 0, 512 * (hi - lo)))
+                g_ = R(nm, lo, hi)
+                for B in range(lo, hi):
+                    o = 4 * (B - lo)
+                    mm([(reg(bks[-1][1], o + j), [(OX[xy][j], blk("UT", B)), (sub(g_, 128 * (o + j), 128 * (o + j) + 128), NI)])
+                        for j in range(4)])
+            tt(R("PB", lo, hi), bks[0], W("DYT", lo, hi), A.mult)
+            more = [] if both else ([] if dma1 else [R("PB", lo, hi)]) + ([R("Q16", lo, hi) if kept(t, lo) else W("ZB", lo, hi)] if t else [])
+            tt(bks[1] if more else R("PX" if both else "ZB", lo, hi), bks[1], W("DXT", lo, hi), A.mult)
             for m, x in enumerate(more):
-                tt(bks[1] if m + 1 < len(more) else R("ZB", B, B + 1), bks[1], x, A.add)
+                tt(bks[1] if m + 1 < len(more) else R("ZB", lo, hi), bks[1], x, A.add)
         if dma1:
-            dma("g", R("ZB"), R("PB"), acc=True, lat=DLAT)
+            dma("g", R("ZB"), R("PB"), acc=True)
         if both:
-            dma("g", R("ZB"), R("PX"), acc=True, lat=DLAT)
-        act(R("AB"), R("ZB"), F.Abs)
-        if dma2:
-            dma("g", R("AB"), S("NT", 512 * a, 512 * b), acc=True, lat=DLAT)
-            relu(R("R0"), R("AB"))
-        else:
-            for B in chunks:
-                bk = S(bank())
-                mm([(bk, [(I32, R("AB", B, B + 1)), (I, C("NT", B))])])
-                relu(R("R0", B, B + 1), bk)
-        nonzero(R("NZ"), R("R0"))
+            dma("g", R("ZB"), R("PX"), acc=True)
+        yield
+        ab = "AB" if a < 4 else "PB"
+        act(R(ab), R("ZB"), F.Abs)
+        dma("g", R(ab), W("NT", a, b), acc=True)
+        relu(R("R0"), R(ab))
+        nz = R("gx" if a < 4 else "gy")
+        nonzero(nz, R("R0"))
         n = 32 * len(chunks)
         bk = bank()
-        nz = R("NZ")
         was, now = (S("SS", 256 * u + 32 * a, 256 * u + 32 * b) for u in (t, t + 1))
-        mm([(S(bk, 0, n), [(I32x, was)] + [(I, sub(nz, i, 16 * n, 16)) for i in range(16)])])
-        stay = ts(now, S(bk, 0, n), 35.5, A.is_ge)
-        for B, mk in zip(chunks, spread(now, 1023.0, a)):
-            bk = mk()
-            r = R("R0", B, B + 1) if t else C("RR", B)
-            tt(r, S(bk), R("R0", B, B + 1), A.min)
-            bk = bank()
-            add([a_act(S(bk), R("ZB", B, B + 1), F.Sign)], [R("ZB", B, B + 1)], [S(bk)], after=[stay])
+        mm([(S(bk, 0, n), ([(I32x, was)] if t else []) + [(I, sub(nz, i, 16 * n, 16)) for i in range(16)])])
+        stay = ts(now, S(bk, 0, n), 35.5 if t else 3.5, A.is_ge)
+        mk = spread(now, 1023.0, a)
+        for lo, hi in units(a, b, wide & 2):
+            r = R("R0", lo, hi) if t else W("RR", lo, hi)
+            tt(r, mk(lo - a, hi - a), R("R0", lo, hi), A.min)
+            bk = S(bank(hi - lo), 0, 512 * (hi - lo))
+            add([a_act(bk, R("ZB", lo, hi), F.Sign)], [R("ZB", lo, hi)], [bk], after=[stay])
+            tt(R("Q16", lo, hi), bk, r, A.mult)
+        for B in chunks:
+            r = R("R0", B, B + 1)
             q = R("Q16", B, B + 1)
-            iq = tt(q, S(bk), r, A.mult)
             if B % 4 == 0:
                 h = B // 4
                 acc.append(bank())
@@ -660,7 +697,7 @@ def build():
             mm([(S(acc[B // 4], o + 16 * g, o + 16 * g + 16, 1, (32 * j, 32 * j + 32, 1)),
                  [(S("DD", 32 * B + 8 * j + g, 8192, 256), sub(q, 128 * j + 16 * g, 128 * j + 16 * g + 16))])
                 for j in range(4) for g in range(8)], start=False, stop=False)
-            if t < 2:
+            if t < 2 and not kept(t + 1, B):
                 gmv(C("ZB", B), q)
             if t == 1 and B == b - 1:
                 dma("g", S("RR", 512 * a, 512 * b), R("R0"), acc=True, lat=DLAT)
@@ -669,10 +706,24 @@ def build():
                 mm([(reg(bk, j), [(blk("RR", 4 * B + j), I), (sub(r, 128 * j, 128 * j + 128), I)]) for j in range(4)])
                 pp = blk("PP", B % 2, 512)
                 gather(pp, IND(S("WW"), blk("Lo", B, 32)))
-                tt(pp, S(bk), pp, A.mult)
-                if B % 4 == 0:
-                    wb.append(bank())
-                mm([(reg(wb[-1], B % 4, 64), [(I32, sub(pp, k, 512, 8)) for k in range(8)])])
+                if B in OPT["scan"]:
+                    tt(S(bk), S(bk), pp, A.mult)
+                    add([("v", "scan", (pp, S("run"), S(bk), 0.0, A.mult, A.add), {}, vcost(pp, [S(bk)], False))],
+                        [S("run"), S(bk)], [pp])
+                    w = sub(pp, 7, 512, 8)
+                else:
+                    tt(pp, S(bk), pp, A.mult)
+                    bk = bank()
+                    w = S(bk, 0, 64)
+                    mm([(w, [(I32, sub(pp, k, 512, 8)) for k in range(8)])])
+                if B < 4:
+                    mv(blk("wout", B, 64), w)
+                else:
+                    tt(blk("wout", B, 64), w, S("ZW", 2 * ZC + 64 * B, 2 * ZC + 64 * B + 64), A.add)
+                if B == 3:
+                    dma("g", ("yw", 0, 256), blk("wout", 0, 256), acc=True, after=wb)
+                if B == 7:
+                    dma("s", ("yw", 256, 512), blk("wout", 1, 256))
 
     def update(t, h, acc):
         for s in ZSUM[t]:
@@ -689,6 +740,8 @@ def build():
 
     for t in range(3):
         tag[0] = "s1_%d" % t
+        if t == 0 or not OPT["early"]:
+            candidates(t)
         step1(t)
         tag[0] = "ex_%d" % t
         z2 = lambda s: S("Z2", 2 * ZC * s, 2 * ZC * s + 1024)
@@ -705,27 +758,28 @@ def build():
             dma("g", z2(t), z2(t - 1), acc=True, lat=DLAT)
         if t == 2:
             dma("g", zw(2), zw(1), acc=True, lat=DLAT)
-        acc, wb = [], []
-        for chunks, dma1, dma2 in GROUPS[t]:
+        acc, wb = [], [dma("s", ("yw", 0, 256), sub(zw(2), 0, 256))] if t == 2 else []
+        runs = [(chunks, group(t, chunks, dma1, dma2, acc, wb)) for chunks, dma1, dma2 in GROUPS[t]]
+        for chunks, run in runs + runs:
             tag[0] = "m%d_%d" % (t, chunks[0])
-            group(t, chunks, dma1, dma2, acc, wb)
+            next(run, None)
+        if t < 2 and OPT["early"]:
+            tag[0] = "ca_%d" % (t + 1)
+            candidates(t + 1)
         tag[0] = "up_%d" % t
         for h in range(2):
             update(t, h, acc)
         if t < 2:
             border(t + 1, [])
             bk = bank()
-            mm([(S(bk, u, 256, 8), [(S("WV", 128 * u + 112 - 16 * g, 128 * u + 240 - 16 * g), S("SS", 256 * t + 256 + g, 256 * t + 512, 8))
-                                    for g in range(8)]) for u in range(8)])
-            tt(blk("ND", t, 256), S("AI"), S(bk, 0, 256), A.subtract)
-            if t == 0:
-                tt(S("AI"), S("AI"), blk("ND", 0, 256), A.subtract)
+            mm([(S(bk, u, 256, 8, (32 * m, 32 * m + 32, 1)),
+                 [(S("WV", 32 * u + 16 - 16 * g, 32 * u + 48 - 16 * g), S("SS", 256 * t + 256 + 2 * m + g, 256 * t + 512, 8))
+                  for g in range(2)]) for u in range(8) for m in range(4)])
+            mv(blk("ND", t, 256), S(bk, 0, 256))
             bk = bank()
-            mm([(S(bk, h, 512, 2), [(blk("HB", h), blk("ND", t, 256))]) for h in range(2)])
+            mm([(S(bk, h, 512, 2), [(blk("HB", h), blk("ND", 0, 256) if t else S("AI")), (blk("HB", 2 + h), blk("ND", t, 256))])
+                for h in range(2)])
             tt(S("LT", 0, 512), S(bk), S("LT", 0, 512), A.max)
-    for h in range(2):
-        tt(blk("wout", h, 256), S(wb[h], 0, 256), S("ZW", 2 * ZC + 256 * h, 2 * ZC + 256 * h + 256), A.add)
-        dma("s", ("yw", 256 * h, 256 * h + 256), blk("wout", h, 256))
     return ops
 
 
@@ -758,11 +812,12 @@ def depend(ops):
     return deps, users
 
 
-def schedule(ops, tries):
+def schedule(ops, tries, seed):
     n = len(ops)
     deps, users = depend(ops)
     alts = [o["alts"] for o in ops]
     lat = [o["lat"] for o in ops]
+    move = [o["move"] for o in ops]
     succ = [[] for _ in range(n)]
     for i in range(n):
         for j in deps[i]:
@@ -770,22 +825,33 @@ def schedule(ops, tries):
     first = dict((min(u), nm) for nm, u in users.items())
     banks = [sorted(set(x[1] for x in o["rd"] + o["wr"] if x[1][0] == "@")) for o in ops]
 
-    def place(pr, pick):
-        left = dict((nm, len(u)) for nm, u in users.items())
-        waiting = sorted(first, reverse=True)
-        last, phys, held = {}, {}, {}
-        free = dict((b, (0.0, None)) for b in range(8))
-        fin, est = [0.0] * n, [0.0] * n
-        cnt = [len(d) for d in deps]
+    def place(pr, pick, old=None, moved=()):
+        if old is None:
+            left = dict((nm, len(u)) for nm, u in users.items())
+            waiting = sorted(first, reverse=True)
+            last, phys, held = {}, {}, {}
+            free = dict((b, (0.0, None)) for b in range(8))
+            fin, est, since = [0.0] * n, [0.0] * n, [0] * n
+            cnt = [len(d) for d in deps]
+            efree = dict((e, 0.0) for e in "tvagsrd")
+            open_ = [i for i in range(n) if cnt[i] == 0]
+            order, marks = [], []
+        else:
+            k = min(old[6][i] for i in moved) // 50
+            marks = old[5][:k]
+            left, waiting, last, phys, held, free, fin, est, since, cnt, efree, open_ = [x.copy() for x in old[5][k]]
+            order = old[1][:50 * k]
         ready = dict((e, []) for e in "tvagsr")
-        efree = dict((e, 0.0) for e in "tvagsr")
-        for i in range(n):
-            if cnt[i] == 0:
-                ready[alts[i][pick[i]][0]].append(i)
-        order = []
-        for _ in range(n):
-            nf = len(free)
-            fb = min(v[0] for v in free.values()) if nf else 0.0
+        place_of = {}
+        for i in open_:
+            ready[alts[i][pick[i]][0]].append(i)
+        for step in range(len(order), n):
+            if step % 50 == 0:
+                marks.append([x.copy() for x in (left, waiting, last, phys, held, free, fin, est, since, cnt, efree)]
+                             + [sorted(i for L in ready.values() for i in L)])
+            pairs = sorted((max(free[b][0], free[b + 1][0]), b) for b in free if b % 2 == 0 and b + 1 in free)
+            alone = sorted((free[b][0], b) for b in free if b ^ 1 not in free)
+            halves = sorted((free[b][0], b) for b in free if b ^ 1 in free)
             while waiting and waiting[-1] in held:
                 waiting.pop()
             best = None
@@ -795,10 +861,17 @@ def schedule(ops, tries):
                 for i in L:
                     s = est[i]
                     if i in first:
-                        if nf < (1 if i == waiting[-1] else RES):
+                        two = first[i][1] == "D"
+                        if i != waiting[-1] and len(free) < RES + two:
                             continue
-                        if fb > s:
-                            s = fb
+                        got = pairs if two else alone
+                        if not two and halves and not (got and got[0][0] <= max(s, ef, halves[0][0])):
+                            got = halves
+                        if not got:
+                            continue
+                        place_of[i] = got[0][1]
+                        if got[0][0] > s:
+                            s = got[0][0]
                     c.append((s if s > ef else ef, i))
                 if c:
                     m = min(c)[0]
@@ -809,25 +882,29 @@ def schedule(ops, tries):
             m, e, c = best
             s, i = max((x for x in c if x[0] <= m + 0.05), key=lambda x: pr[x[1]])
             if i in first:
-                b = min(free, key=lambda k: free[k][0])
-                held[i] = free.pop(b)[1]
-                phys[first[i]] = b
+                b = phys[first[i]] = place_of[i]
+                held[i] = [free.pop(k)[1] for k in range(b, b + 1 + (first[i][1] == "D"))]
             efree[e] = s + alts[i][pick[i]][4]
-            f = fin[i] = efree[e] + lat[i]
+            f = efree[e]
+            if move[i]:
+                f = efree["d"] = max(f, efree["d"]) + move[i]
+            f = fin[i] = f + lat[i]
             order.append(i)
             ready[e].remove(i)
             for nm in banks[i]:
                 left[nm] -= 1
                 last[nm] = max(last.get(nm, 0.0), f)
                 if left[nm] == 0:
-                    free[phys[nm]] = (last[nm] + HOP, nm)
+                    for k in range(phys[nm], phys[nm] + 1 + (nm[1] == "D")):
+                        free[k] = (last[nm] + HOP, nm)
             for j, h in succ[i]:
                 if est[j] < f + h:
                     est[j] = f + h
                 cnt[j] -= 1
                 if cnt[j] == 0:
                     ready[alts[j][pick[j]][0]].append(j)
-        return max(fin), order, phys, fin, held
+                    since[j] = step
+        return max(fin), order, phys, fin, held, marks, since
 
     def chain(cur, pick):
         order, fin = cur[1], cur[3]
@@ -842,42 +919,156 @@ def schedule(ops, tries):
             out.append(i)
             c = [(fin[j], j) for j in deps[i]]
             if prev[i] is not None:
-                c.append((fin[prev[i]] - lat[prev[i]], prev[i]))
+                c.append((fin[prev[i]] - lat[prev[i]] - move[prev[i]], prev[i]))
             i = max(c)[1] if c else None
         return out
 
     pr = [0.0] * n
     for i in range(n - 1, -1, -1):
-        pr[i] = alts[i][0][4] + lat[i] + max([pr[j] + h for j, h in succ[i]] + [0.0])
+        pr[i] = alts[i][0][4] + lat[i] + move[i] + max([pr[j] + h for j, h in succ[i]] + [0.0])
+    sends = [i for i in range(n) if alts[i][0][1] == "send" and ops[i]["tag"] != "setup"]
+    worth = lambda c: c[0] + MILE * sum(c[3][i] for i in sends)
     pick = [0] * n
-    rng = np.random.default_rng(SEED)
+    rng = np.random.default_rng(seed)
     cur = place(pr, pick)
     ch = chain(cur, pick)
-    for _ in range(tries):
+    best = (cur, pick)
+    for it in range(tries):
         q, p = pr, pick
         L = ch if rng.random() < 0.8 else range(n)
         if rng.random() < 0.45:
             L = [i for i in L if len(alts[i]) > 1]
             p = list(pick)
             a = int(rng.integers(0, len(L) + 1))
-            for i in L[a:a + int(rng.integers(1, 3))]:
+            moved = L[a:a + int(rng.integers(1, 3))]
+            for i in moved:
                 p[i] = (p[i] + 1 + int(rng.integers(0, len(alts[i]) - 1))) % len(alts[i])
         else:
             q = list(pr)
             a = L[int(rng.integers(0, len(L)))]
             d = float(rng.normal()) * 3.0
             w = int(rng.integers(0, 10))
-            for i in range(max(0, a - w), min(n, a + w + 1)):
+            moved = range(max(0, a - w), min(n, a + w + 1))
+            for i in moved:
                 q[i] += d
-        new = place(q, p)
-        if new is not None and new[0] <= cur[0] + 0.03 * rng.random():
+        if not moved:
+            continue
+        new = place(q, p, cur, moved)
+        if new is not None and worth(new) <= worth(cur) + HEAT * (1.0 - it / tries) * rng.random():
             cur, pr, pick = new, q, p
             ch = chain(cur, pick)
-    _, order, phys, fin, held = cur
-    for i, nm in held.items():
-        for j in users.get(nm, ()):
-            deps[i][j] = True
-    return order, deps, phys, fin, [alts[i][pick[i]] for i in range(n)]
+            if cur[0] < best[0][0]:
+                best = (cur, pick)
+    cur, pick = best
+    order, phys, fin, held = cur[1:5]
+    for i, nms in held.items():
+        for nm in nms:
+            for j in users.get(nm, ()):
+                deps[i][j] = True
+    order, pick, fin = polish([(ops, HOP, 1.0)], deps, order, pick, rng, POLISH * tries)
+    return order, deps, phys, fin, pick
+
+
+def plan(starts, tries):
+    views = [(build(*c), hop, weight) for c, hop, weight in COSTS]
+    ops = views[0][0]
+    order, deps, phys, fin, pick = min((schedule(ops, tries, seed) for seed in starts), key=lambda c: max(c[3]))
+    rng = np.random.default_rng(0)
+    base, users = depend(ops)
+    first = dict((min(u), nm) for nm, u in users.items())
+    for turn in range(TURNS):
+        at = dict((i, k) for k, i in enumerate(order))
+        owner, where, more = dict((b, None) for b in range(8)), {}, [dict(d) for d in base]
+        for i in order:
+            if i in first:
+                free = [(max([fin[j] for j in users.get(nm, ())] + [0.0]), b) for b, nm in owner.items()
+                        if nm is None or max(at[j] for j in users[nm]) < at[i]]
+                b = where[first[i]] = min(free)[1]
+                more[i].update((j, True) for j in users.get(owner[b], ()))
+                owner[b] = first[i]
+        new = polish(views[:1], more, order, pick, rng, 2 * tries)
+        if max(new[2]) < max(fin):
+            (order, pick, fin), deps, phys = new, more, where
+    order, pick, fin = polish(views, deps, order, pick, rng, 40 * tries)
+    return ops, order, deps, phys, fin, [o["alts"][k] for o, k in zip(ops, pick)]
+
+
+def polish(views, deps, order, pick, rng, tries):
+    n = len(deps)
+    alts = [o["alts"] for o in views[0][0]]
+    data = [([o["alts"] for o in ops], [(o["lat"], o["move"]) for o in ops],
+             [[(j, hop if w else 0.0) for j, w in d.items()] for d in deps], weight) for ops, hop, weight in views]
+    succ = [[] for _ in range(n)]
+    for i in range(n):
+        for j in deps[i]:
+            succ[j].append(i)
+
+    def run(order, pick, bound=1e9):
+        total, pairs, first = 0.0, [], None
+        for k, (alts, tail, pred, weight) in enumerate(data):
+            x, fin, p = one(order, pick, alts, tail, pred)
+            total += weight * x
+            pairs += p
+            first = first or (fin, x)
+            if k == 0 and x > bound + 1.0:
+                return (1e9,)
+        return total, first[0], pairs, first[1]
+
+    def one(order, pick, alts, tail, pred):
+        fin, why = [0.0] * n, [None] * n
+        efree, last = dict((e, 0.0) for e in "tvagsrd"), {}
+        for i in order:
+            alt = alts[i][pick[i]]
+            e = alt[0]
+            s, w = efree[e], (last.get(e), True)
+            for j, h in pred[i]:
+                if fin[j] + h > s:
+                    s, w = fin[j] + h, (j, False)
+            f = efree[e] = s + alt[4]
+            if tail[i][1]:
+                f = efree["d"] = max(f, efree["d"]) + tail[i][1]
+            fin[i], why[i], last[e] = f + tail[i][0], w, i
+        i = fin.index(max(fin))
+        pairs = []
+        while why[i][0] is not None:
+            if why[i][1]:
+                pairs.append((why[i][0], i))
+            i = why[i][0]
+        return max(fin) + MEAN * sum(fin) / n, fin, pairs
+
+    cur = run(order, pick)
+    for _ in range(tries):
+        a, b = cur[2][int(rng.integers(0, len(cur[2])))]
+        o, p = order, pick
+        u = rng.random()
+        if u < 0.25:
+            i = (a, b)[int(rng.integers(0, 2))]
+            if len(alts[i]) < 2:
+                continue
+            p = list(pick)
+            p[i] = (p[i] + 1 + int(rng.integers(0, len(alts[i]) - 1))) % len(alts[i])
+        else:
+            x, y = order.index(a), order.index(b)
+            x = max(0, x - int(rng.integers(0, 12))) if u < 0.5 else x
+            y = min(n - 1, y + int(rng.integers(0, 12))) if u > 0.75 else y
+            part = order[x:y + 1]
+            if u < 0.625:
+                take = {b}
+                for i in part[::-1]:
+                    if any(j in take for j in succ[i]):
+                        take.add(i)
+                part = [i for i in part if i in take] + [i for i in part if i not in take]
+            else:
+                take = {a}
+                for i in part:
+                    if any(j in take for j in deps[i]):
+                        take.add(i)
+                part = [i for i in part if i not in take] + [i for i in part if i in take]
+            o = order[:x] + part + order[y + 1:]
+        new = run(o, p, cur[3])
+        if new[0] <= cur[0]:
+            cur, order, pick = new, o, p
+    return order, pick, cur[1]
 
 
 PLAN = []
@@ -888,8 +1079,7 @@ def rank_program(g, core, T, topo):
     if rank is None:
         return
     if not PLAN:
-        ops = build()
-        PLAN.append((ops,) + schedule(ops, TRIES))
+        PLAN.append(plan(STARTS, TRIES))
     ops, order, deps, phys, fin, way = PLAN[0]
     N = len(T.cores)
     peers = [T.cores[(rank + d) % N] for d in range(1, N)]
@@ -897,14 +1087,14 @@ def rank_program(g, core, T, topo):
     queue = {"t": g.tensor, "v": g.vector, "a": g.scalar, "g": g, "s": g.sync}
     call = {"tensor_tensor": g.vector.tensor_tensor, "tensor_scalar": g.vector.tensor_scalar,
             "tensor_copy": g.vector.tensor_copy, "memset": g.vector.memset, "transpose": g.vector.transpose,
-            "activation": g.scalar.activation, "iota": g.iota, "affine_select": g.affine_select}
+            "activation": g.scalar.activation, "iota": g.iota, "scan": g.vector.tensor_tensor_scan, "affine_select": g.affine_select}
 
     def ap(x):
         if not is_ap(x):
             return x
         if x[0] == "ind":
             return ap(x[1]).indirect(ap(x[2]))
-        nm, o = ("P%d" % phys[x[1]], 0) if x[1][0] == "@" else PLACE[x[1]]
+        nm, o = ("P%d" % (phys[x[1]] // 2), phys[x[1]] % 2 * 512) if x[1][0] == "@" else PLACE[x[1]]
         p = slice(None) if x[5] is None else slice(*x[5])
         return T[nm][p, o + x[2]:o + x[3]] if x[4] == 1 else T[nm][p, o + x[2]:o + x[3]:x[4]]
 
@@ -944,7 +1134,7 @@ def rank_program(g, core, T, topo):
                 for d, p in enumerate(peers):
                     rid, pid = topo.addr(p, core)
                     ids.append(DstId(rid=rid, pnc=pid))
-                    dsts.append(ap(S(nm, c0 + d * w, c0 + (d + 1) * w)))
+                    dsts.append(ap(S(nm, c0 + d * w, c0 + d * w + width(src))))
                 trs.append(RemoteDMATransfer(dst_ids=ids, dma_engine_mask=sum(1 << x for x in eng[used:used + ne]),
                                              remote_sem=T.sem[sem], src=ap(src), dsts=dsts))
                 used += ne
@@ -955,6 +1145,11 @@ def rank_program(g, core, T, topo):
             q.dma_start(side(a[0]), side(a[1]), **({"accum_op": A.add} if a[2] else {})).then_inc(T.sem[a[3]], 16)
             mark[i] = (a[3], 16)
             total[a[3]] = 16
+        elif kind == "dmas":
+            for out, src in a[0]:
+                q.dma_start(side(out), side(src)).then_inc(T.sem[a[1]], 16)
+            mark[i] = (a[1], 16 * len(a[0]))
+            total[a[1]] = mark[i][1]
         else:
             if kind == "mm":
                 for out, terms in a[0]:

import numpy as np
from concourse.bass import DstId, RemoteDMATransfer
from concourse.mybir import AluOpType as A, ActivationFunctionType as F

f32, f16, b16, i32, u16 = "float32", "float16", "bfloat16", "int32", "uint16"
ZC = 648
_B = {
    "XW": (904, f32), "YW": (904, f32), "WW": (904, f32), "PW": (912, b16), "UT": (1024, f16), "LD2": (1024, f16),
    "DXT": (4096, b16), "DYT": (4096, b16), "NT": (4096, b16), "DD": (8192, b16), "Q16": (2048, f16), "RR": (4096, f16),
    "gx": (2048, f16), "gy": (2048, f16), "PB": (2048, f32), "AB": (2048, f32), "ZB": (4096, f32),
    "R0": (4096, f16), "UI": (1024, i32), "PI": (512, i32), "NBI": (256, i32),
    "BDI": (8, i32), "Lo": (256, u16), "bo": (8, u16), "SX": (384, f16), "SY": (384, f16), "LX": (768, f16),
    "LY": (768, f16), "SP": (128, b16), "SW": (128, f32), "PX": (2048, f32), "LT": (ZC, f32), "Z2": (6 * ZC, f32), "ZW": (3 * ZC, f32),
    "SS": (1024, b16), "AI": (256, b16), "ND": (512, b16),
    "cgx": (1024, f16), "cgy": (1024, f16), "CD": (2048, b16), "cb": (1024, f32),
    "EQ": (512, b16), "xa": (256, f16),
    "O1": (64, u16), "O2": (64, u16), "UL": (64, f16),
    "CL": (64, f16), "FB": (256, b16), "dL": (192, b16), "sqL": (128, b16), "KY": (256, f32), "PVL": (384, f32),
    "ef": (256, b16), "hn": (128, b16), "t1": (128, f16), "c16": (128, f16),
    "C16": (128, f16), "Cn": (128, f16), "O3": (24, u16), "Oc": (24, u16), "Oxy": (48, u16),
    "cf": (40, f32), "dum": (8, f32), "LTc": (128, f32), "AL": (384, b16), "DN": (128, b16), "FE": (512, b16),
    "NV": (256, f16), "NC": (256, f32), "VJ": (256, f32), "EP": (128, b16), "ED": (768, f32),
    "nq": (384, f32), "ES": (768, b16), "EWC": (384, f32), "EQq": (384, f16), "EM": (1152, f16), "eg": (512, f16),
    "EA": (512, f32), "em": (256, f16), "enz": (256, b16), "G8": (144 * 8, b16),
    "ci": (16, i32), "cj": (24, i32), "col": (40, f32), "RM": (16, f32), "e8": (8, f32),
    "IX": (256, b16), "IG": (128, b16), "IH": (128, b16),
    "IDS": (128 * 10, b16), "ST": (256, f16), "EB": (1024, b16), "F32": (128 * 10, f32), "GSB": (144 * 4, b16), "BO": (256, b16),
    "BR": (2048, b16), "NB": (128 * 4, b16), "OX": (1024, b16), "WV": (272, b16), "HBR": (1024, b16), "PGm": (1024, b16),
    "RB": (128 * 5, b16), "HB": (512, b16), "TRI": (256, b16), "TRc": (512, b16), "CM": (240, b16), "eps": (512, b16),
    "run": (512, b16),
}
ALIAS = {"XY16": ("Q16", 0, 1024), "PI2": ("NT", 0, 1024), "PT": ("Q16", 1024, 1024), "tc": ("EQ", 0, 256), "Zp": ("cgx", 0, 512), "Zt": ("cgx", 512, 512),
         "G1": ("cgx", 0, 1024), "G2": ("R0", 0, 1024), "csg": ("CD", 0, 1024), "eq2": ("CD", 1024, 1024), "CDX": ("CD", 0, 1024),
         "CDY": ("CD", 1024, 1024), "PG": ("RR", 0, 4096), "eab": ("EA", 0, 256),
         "one": ("CD", 1024, 1024), "SH": ("ES", 0, 320), "dc": ("ND", 0, 512), "sq": ("SS", 512, 512),
         "PP": ("cb", 0, 1024), "wout": ("Z2", 0, 512), "EMs": ("nq", 0, 384), "LDI": ("PI", 0, 512),
         "vio": ("eg", 0, 384), "CI": ("UI", 0, 64), "ia": ("UI", 64, 128), "ib": ("UI", 192, 64), "ic": ("UI", 256, 64),
         "BI": ("UI", 320, 128), "BJ": ("UI", 448, 128)}
PLACE = {}
SCRATCH = {}
for _k, (_w, _d) in _B.items():
    if _w > 400:
        PLACE[_k] = (_k, 0)
        SCRATCH[_k] = ("sbuf", [128, _w], _d)
    else:
        _o = SCRATCH.get("pool_" + _d, (0, [128, 0]))[1][1]
        PLACE[_k] = ("pool_" + _d, _o)
        SCRATCH["pool_" + _d] = ("sbuf", [128, _o + (_w + 15) // 16 * 16], _d)
for _i in range(4):
    SCRATCH["P%d" % _i] = ("psum", [128, 1024], f32)
NDMA = 130
SEMAPHORES = ["qt", "qv", "qa", "qg", "ls", "aP", "aW0", "aW1"] + ["a%s%d" % (_c, _i) for _c in "xy" for _i in range(3)] \
    + ["d%d" % _i for _i in range(NDMA)]
SZ = {f32: 4, f16: 2, b16: 2, i32: 4, u16: 2}
CY = 0.83e-3 * 1.05
GA = 1.56
HOP = 0.17
COSTS = [((CY, GA, 3.8, 2.0, 1.15, 0.25, 1.0, 1.0, 5.5), HOP, 1.0),
         ((0.83e-3 * 1.35, 1.9, 5.0, 2.4, 1.6, 0.25, 1.2, 1.5, 6.5), 0.16, 0.5),
         ((0.83e-3 * 1.1, 1.3, 3.0, 2.9, 2.0, 0.4, 1.5, 2.5, 8.0), 0.2, 0.8)]
BIG = 65536.0
GROUPS = [((0, 1), 1, 0), ((2, 3), 2, 0), ((4, 5), 1, 0), ((6, 7), 1, 0)]
GROUPS = [GROUPS, GROUPS, GROUPS]
ZSUM = ((0,), (1,), (2,))
TRIES = 400
STARTS = (2,)
MILE = 2.0
TURNS = 6
HEAT = 0.03
POLISH = 4
MEAN = 0.3
RES = 3
OPT = {"int": 0, "early": 1, "wide": 0, "scan": (4, 5, 6, 7), "init": 1, "s1dma": 1, "flexg": 1, "gmv": 1}


def S(name, a=0, b=None, step=1, p=None):
    if name in ALIAS:
        real, o, w = ALIAS[name]
        return ("ap", real, o + a, o + (w if b is None else b), step, p)
    if b is None:
        b = _B[name][0] if name in _B else 512
    return ("ap", name, a, b, step, p)


def IND(win, off):
    return ("ind", win, off)


def is_ap(x):
    return isinstance(x, tuple) and len(x) > 0 and x[0] in ("ap", "ind")


def width(x):
    if x[0] == "ind":
        return 16 * (x[2][3] - x[2][2])
    return len(range(x[2], x[3], x[4]))


def psum(x):
    return x[0] == "ap" and x[1][0] == "@"


def size(x):
    return 4 if psum(x) else SZ[_B[x[1]][1]]


def sub(x, a, b, step=1, p=None):
    return ("ap", x[1], x[2] + a, x[2] + b, step, p)


def build(CY, GA, SCAT, DLAT, ACC, ISSUE, GISSUE, CALL, FAR):
    ops = []
    nb = [0]
    nd = [0]
    tag = ["setup"]
    sent = []

    def bank(k=1):
        nb[0] += 1
        return ("@%d" if k == 1 else "@D%d") % nb[0]

    def add(alts, rd, wr, lat=0.0, after=(), move=0.0):
        r, w = [], []
        for x in rd:
            r += [x[1], x[2]] if x[0] == "ind" else [x]
        for x in wr:
            if x[0] == "ind":
                w.append(x[1])
                r.append(x[2])
            else:
                w.append(x)
        ops.append(dict(alts=alts, rd=r, wr=w, lat=lat, after=list(after), tag=tag[0], move=move))
        return len(ops) - 1

    def vcost(out, ins, two):
        n = width(ins[0]) if ins else width(out)
        if out[0] == "ind":
            return 0.05 + SCAT * n * CY
        if ins and ins[0][0] == "ind":
            return 0.05 + GA * n * CY
        if two:
            c = 1 if any(psum(x) for x in ins) else 2
        else:
            c = 0.5 if all(size(x) == 2 for x in [out] + ins) else 1
        return 0.05 + max(64, n * c) * CY

    def v_ts(out, a, s1, op0, s2=None, op1=None):
        args = (out, a, s1, s2, op0) if op1 is None else (out, a, s1, s2, op0, op1)
        return ("v", "tensor_scalar", args, {}, vcost(out, [a], False))

    def v_cp(out, a):
        return ("v", "tensor_copy", (out, a), {}, vcost(out, [a], False))

    def a_act(out, a, fn, bias=None, scale=None):
        kw = {}
        if bias is not None:
            kw["bias"] = bias
        if scale is not None:
            kw["scale"] = scale
        return ("a", "activation", (out, a, fn), kw, 0.07 + max(64, width(a) * (GA if a[0] == "ind" else 1)) * CY)

    def aps(*xs):
        return [x for x in xs if is_ap(x)]

    def tt(out, a, b, op):
        return add([("v", "tensor_tensor", (out, a, b, op), {}, vcost(out, [a, b], True))], [a, b], [out])

    def ts(out, a, s1, op0, s2=None, op1=None):
        return add([v_ts(out, a, s1, op0, s2, op1)], aps(a, s1, s2), [out])

    def cp(out, a):
        return add([v_cp(out, a)], [a], [out])

    def ms(out, c):
        return add([("v", "memset", (out, c), {}, vcost(out, [], False))], [], [out])

    def act(out, a, fn, bias=None, scale=None):
        return add([a_act(out, a, fn, bias, scale)], aps(a, bias, scale), [out])

    def mv(out, a, scale=None, bias=None, vfirst=False):
        if scale is None and bias is None:
            alts = [a_act(out, a, F.Copy), v_cp(out, a)]
        elif bias is None:
            alts = [a_act(out, a, F.Copy, scale=scale), v_ts(out, a, scale, A.mult)]
        else:
            alts = [a_act(out, a, F.Identity, bias=bias), v_ts(out, a, bias, A.add)]
        return add(alts[::-1] if vfirst else alts, aps(a, scale, bias), [out])

    def gather(out, a):
        return mv(out, a) if OPT["flexg"] else act(out, a, F.Copy)

    def relu(out, a):
        return add([a_act(out, a, F.Relu), v_ts(out, a, 0.0, A.max)], [a], [out])

    def over(out, a, c, sign=1.0):
        return add([v_ts(out, a, sign * c, A.is_gt if sign > 0 else A.is_lt), a_act(out, a, F.Relu, bias=-c, scale=sign)], [a], [out])

    def nonzero(out, a):
        return add([v_ts(out, a, 0.0, A.is_gt), a_act(out, a, F.Sign)], [a], [out])

    def iota(out, pat, base, cm=0, after=()):
        kw = {} if _B[out[1]][1] == i32 else {"allow_small_or_imprecise_dtypes": True}
        return add([("g", "iota", (out, pat, base, cm), kw, 0.13 + 2 * width(out) * CY)], [], [out], after=after)

    def asel(out, a, pat, base, op=A.is_equal, after=()):
        return add([("g", "affine_select", (out, a, pat, op, 0.0, base, 1), {}, 0.17 + 2 * width(out) * CY)], [a], [out],
                   after=after)

    def gmv(out, a, turn=0):
        n = width(out)
        alts = [("g", "affine_select", (out, a, [[0, n]], A.is_ge, 0.0, 0, 1), {}, 0.17 + 2 * n * CY), a_act(out, a, F.Copy), v_cp(out, a)]
        return add(alts[turn:] + alts[:turn], [a], [out])

    def mm(groups, after=(), start=True, stop=True):
        rd, wr, c = [], [], 0.03
        for out, terms in groups:
            wr.append(out)
            for l, r in terms:
                rd += [l, r]
                c += max(min(64, width(l)), width(r)) * (4 if size(r) == 4 else 1) * CY / 2
        return add([("t", "mm", (groups, start, stop), {}, c)], rd, wr, after=after)

    def dma(eng, out, a, acc=False, lat=2.2, after=()):
        nd[0] += 1
        x = out if is_ap(out) else a
        return add([(eng, "dma", (out, a, acc, "d%d" % (nd[0] - 1)), {}, GISSUE if eng == "g" else ISSUE)],
                   aps(a) + (aps(out) if acc else []), aps(out), lat=DLAT, after=after,
                   move=0.21 * (ACC if acc else 1.0) * width(x) * size(x) / 1024)

    def dmas(eng, pairs, rd, wr, move):
        nd[0] += 1
        return add([(eng, "dmas", (pairs, "d%d" % (nd[0] - 1)), {}, ISSUE * len(pairs))], rd, wr, lat=DLAT, move=move)

    def send(parts):
        i = add([("g", "send", (parts,), {}, CALL)], [p[0] for p in parts], [])
        sent[:] = sent or [i]
        for src, nm, a, w, sem, ne in parts:
            add([("r", "recv", (sem, ne), {}, 0.0)], [], [S(nm, a + d * w, a + d * w + width(src)) for d in range(3)], lat=FAR, after=[i])

    def blk(name, k, w=128):
        return S(name, k * w, (k + 1) * w)

    def c1(name, k):
        return S(name, k, k + 1)

    dma("s", S("BDI"), "bord")
    ms(S("PI"), 0)
    dma("s", S("PI", p=(0, 128, 16)), "px")
    dma("a", S("PI", p=(8, 128, 16)), "py")
    dma("s", S("UI", 0, 512), "ux")
    dma("a", S("UI", 512, 1024), "uy")
    dma("s", S("NBI"), "nb")
    dma("a", S("WW", 0, 512), "wt")
    iota(S("ci", 0, 8), [[0, 8]], 0, 1)
    iota(S("ci", 8, 16), [[1, 8]], 0, 1)
    iota(S("IX"), [[1, 256]], 0)
    ts(c1("ci", 0), c1("ci", 2), 15, A.bitwise_and)
    ts(c1("ci", 1), c1("ci", 2), 112, A.bitwise_and)
    ts(c1("ci", 3), c1("ci", 2), 120, A.bitwise_and)
    ts(c1("ci", 4), c1("ci", 2), 3, A.arith_shift_right)
    ts(S("cj", 8, 16), S("ci", 8, 16), 7, A.bitwise_and)
    cp(S("col", 0, 5), S("ci", 0, 5))
    cp(c1("col", 5), c1("cj", 8))
    rcol, gcol, pcol, ocol, hcol, kcol = (c1("col", k) for k in range(6))
    IX = S("IX", 0, 128)
    ts(S("RM"), S("IX", 0, 16), rcol, A.is_equal)
    ts(S("col", 16, 24), S("cj", 8, 16), ocol, A.add)
    lo8, wcol, ccol, keyc = (c1("col", k) for k in range(7, 11))
    ts(lo8, rcol, 8.0, A.is_lt)
    ts(wcol, lo8, -1023.0, A.mult, 1024.0, A.add)
    ts(c1("col", 11), c1("RM", 8), 8.0, A.mult, c1("RM", 0), A.add)
    tt(ccol, c1("col", 11), c1("RM", 4), A.add)
    ts(keyc, kcol, -512.0, A.mult, 3584.0 - 9 * 4096.0, A.add)
    ts(c1("col", 12), gcol, 15.0, A.add)
    ts(S("PW", 0, 512), S("PI"), c1("RM", 5), A.add)
    ts(c1("col", 13), c1("RM", 4), 664.0, A.mult)
    ts(c1("col", 14), c1("RM", 8), 29.0, A.mult, c1("col", 13), A.add)
    ts(S("PW", 896, 912), S("RM"), 0.0, A.mult, c1("col", 14), A.add)
    cp(S("bo"), S("BDI"))
    mv(S("SP"), IND(S("PW", 0, 512), S("bo")))
    whole = (lambda out, a: mv(out, a, vfirst=True)) if OPT["int"] else cp
    whole(S("XW", 0, 512), S("UI", 0, 512))
    whole(S("YW", 0, 512), S("UI", 512, 1024))

    def border(t, more):
        mv(blk("SX", t), IND(S("XW", 0, 512), S("bo")))
        mv(blk("SY", t), IND(S("YW", 0, 512), S("bo")))
        ne = 2 if more else 4
        send(more + [(blk("SX", t), "LX", 384 * (t % 2), 128, "ax%d" % t, ne),
                     (blk("SY", t), "LY", 384 * (t % 2), 128, "ay%d" % t, ne)])
        gmv(S("XW", 512, 896), blk("LX", t % 2, 384), 1)
        gmv(S("YW", 512, 896), blk("LY", t % 2, 384), 1)
    send([(S("SP"), "PW", 512, 128, "aP", 8)])
    mv(S("SW"), IND(S("WW", 0, 512), S("bo")))
    border(0, [(blk("SW", u, 64), "WW", 512 + 64 * u, 128, "aW%d" % u, 2) for u in range(2)])
    for nm in ("XW", "YW", "WW"):
        ms(S(nm, 896, 904), 0.0)
    ms(S("one", 0, 512), 1.0)
    iota(S("IG"), [[16, 8], [0, 16]], 0)
    iota(S("IH"), [[1, 16], [0, 8]], 0)
    I, NI, I32x, IBn, I896, N896, ILO, Ith, IM, NIM = (blk("IDS", k) for k in range(10))
    ts(I, IX, pcol, A.is_equal)
    for m, c in ((NI, -1.0), (I32x, 32.0), (IBn, -BIG), (I896, 896.0), (N896, -896.0), (ILO, lo8), (Ith, 1.0 / 32),
                 (IM, 1.5 * 2 ** 29), (NIM, -1.5 * 2 ** 29)):
        mv(m, I, scale=c, vfirst=True)
    I32, NI32, RT1, RT2, RT4, SH0, SH1, BF0, BF8, I32th = (blk("F32", k) for k in range(10))
    mv(I32th, Ith)
    mv(I32, I)
    mv(NI32, NI)
    for m, k in ((RT1, 1), (RT2, 2), (RT4, 4)):
        ts(m, IX, c1("col", 16 + k), A.is_equal)
    ms(S("DD", 0, 1024), 0.0)
    dma("s", S("DD", 1024, 2048), S("DD", 0, 1024))
    for u in range(1, 4):
        dma("s", blk("DD", u, 2048), blk("DD", 0, 2048))

    def rows_of(dst, src, k, step):
        w = width(src)
        dma("s", S(dst, 0, k * w), S("DD", 0, k * w))
        dmas("s", [(S(dst, w * u, w * u + w, 1, (u, 128, step)), sub(src, 0, w, 1, (u, 128, step))) for u in range(k)],
             [src], [S(dst, 0, k * w)], 0.3)
    for h, m in enumerate((SH0, SH1)):
        asel(m, S("one", 0, 128), [[-16, 8], [1000, 2], [-1, 8]], -1000 * h)
    GSk = []
    for k, c in enumerate((wcol, 4096.0, 1.0 / 16, ccol)):
        ts(blk("GSB", k, 144), S("IX", 0, 144), c1("col", 12), A.is_equal, c, A.mult)
        GSk.append([S("GSB", 144 * k + 15 - r, 144 * k + 143 - r) for r in range(16)])
    GSK, GS16, GSC = GSk[1:]
    BO, BO8 = blk("BO", 0), blk("BO", 1)
    ts(BO, S("IG"), gcol, A.is_equal)
    ts(BO8, S("IG"), gcol, A.is_equal, lo8, A.mult)
    for h in range(4):
        asel(blk("BR", h, 512), S("one", 0, 512), [[-1, 4], [-16, 8], [0, 16]], -4 * h, after=sent)
    BR = [blk("BR", r) for r in range(16)]
    NB0, NB8, NB5 = (blk("NB", k) for k in range(3))
    for m, r, c in ((NB0, 0, -1.0), (NB8, 8, -1.0), (NB5, 5, -896.0)):
        ts(m, BO, c1("RM", r), A.mult, c, A.mult)
    mv(BF0, BO, scale=c1("RM", 0))
    mv(BF8, BO, scale=c1("RM", 8))
    for xy in range(2):
        asel(blk("OX", xy, 512), S("one", 0, 512), [[-32, 4], [-2, 16], [0, 8]], -xy)
    OX = [[blk("OX", 4 * xy + j) for j in range(4)] for xy in range(2)]
    RB = {}
    for m, (r, h) in enumerate(((0, 0), (0, 1), (8, 0), (8, 1))):
        RB[r, h] = blk("RB", m)
        asel(RB[r, h], S("one", 0, 128), [[-16, 8], [1000, 2], [0, 8]], -r - 1000 * h)
    RB8 = blk("RB", 4)
    mv(RB8, RB[8, 1], scale=8.0)
    for h in range(2):
        asel(blk("HB", h), S("one", 0, 128), [[-16, 8], [0, 2], [-1, 8]], -8 * h, after=sent)
    mv(blk("HB", 1, 256), blk("HB", 0, 256), scale=-1.0, vfirst=True)
    for h in range(2):
        asel(blk("PGm", h, 512), S("one", 0, 512), [[-16, 4], [0, 128]], -64 * h, after=sent)
        asel(blk("HBR", h, 512), S("one", 0, 512), [[-1, 4], [-8, 16], [0, 8]], -4 * h, after=sent)
        asel(blk("EB", h, 512), S("one", 0, 512), [[-1, 32], [0, 16]], -32 * h, after=sent)
    ts(blk("TRI", 0), S("IH"), hcol, A.is_equal, -1.0, A.mult)
    asel(blk("TRI", 1), blk("TRI", 0), [[-1, 128]], 0, A.is_ge)
    tt(blk("TRI", 1), blk("TRI", 0), blk("TRI", 1), A.subtract)
    TRI = blk("TRI", 1)
    ts(blk("TRc", 0), IX, pcol, A.is_le, 4096.0, A.mult)
    for u in range(1, 4):
        dma("s", blk("TRc", u), blk("TRc", 0))
    for b in range(2):
        asel(blk("SH", b, 160), S("one", 0, 160), [[-32, 5], [1000 - 2000 * b - 16, 2], [-1, 16]], 16 - 1000 + 1000 * b)
    ts(S("dum"), S("IX", 0, 8), 16.0, A.mult, rcol, A.add)
    ts(S("dum"), S("dum"), 520.0, A.add)
    rows_of("G8", S("GSB", 0, 144), 8, 8)
    iota(S("vio"), [[-1, 3], [4, 128]], 3, after=sent)
    dma("s", S("CM"), S("DD", 0, 240))
    ms(S("CM", 112, 128), -16.0)
    iota(S("ZW", 0, ZC), [[0, ZC]], 0, after=sent)
    dmas("s", [(blk("ZW", u, ZC), S("ZW", 0, ZC)) for u in (1, 2)] + [(blk("Z2", u, ZC), S("ZW", 0, ZC)) for u in range(6)],
         [S("ZW", 0, ZC)], [S("ZW", ZC, 3 * ZC), S("Z2")], 4.4)
    ms(S("Zp"), 0.0)
    ms(S("LT", 512, ZC), 896.0)
    for k in range(8):
        cp(S("Zp", k, 512, 16), blk("NBI", k, 32))
    add([("v", "transpose", (S("Zt"), S("Zp")), {}, 0.05 + 256 * CY)], [S("Zp")], [S("Zt")])
    bk = bank()
    mm([(S(bk, 32 * j + 16 * b, 32 * j + 16 * b + 16),
         [(S("SH", 160 * b + 16 - 16 * (gp - b), 160 * b + 144 - 16 * (gp - b)), S("Zt", 32 * j + 16 * gp, 32 * j + 16 * gp + 16))
          for gp in range(2)]) for j in range(16) for b in range(2)])
    mv(S("LT", 0, 512), S(bk))
    bk = bank()
    mm([(S(bk, 0, 256), [(SH0, S("LT", 0, 512, 2)), (SH1, S("LT", 1, 512, 2))])])
    cp(S("Lo"), S(bk, 0, 256))
    ts(S("AI"), S(bk, 0, 256), 896.0, A.not_equal, 896.0, A.mult)
    for xy in range(2):
        mv(S("XY16", xy, 1024, 2), S(("XW", "YW")[xy], 0, 512))
        mv(S("PI2", xy, 1024, 2), S("PW", 0, 512), scale=c1("RM", 8 * xy))
    for src, dst, m in (("XY16", "UT", I), ("PI2", "PT", BO)):
        for h in range(2):
            bk = bank()
            mm([(S(bk, 128 * u, 128 * u + 128), [(blk(src, 4 * h + u), m)]) for u in range(4)])
            mv(blk(dst, h, 512), S(bk))
    dma("s", S("WV"), S("DD", 0, 272))
    dmas("s", [(S("WV", 32 * u + 16, 32 * u + 32), sub(I896, 16 * u, 16 * u + 16)) for u in range(8)], [I896], [S("WV")], 0.3)
    dma("s", S("LDI"), "ld")
    iota(S("LD2", 0, 1024, 2), [[0, 512]], 0, after=sent)
    cp(S("LD2", 1, 1024, 2), S("LDI"))
    ms(S("eps"), 1.0 / 64)
    iota(S("run"), [[0, 64], [1, 8]], 0, after=sent)
    ts(S("run"), S("run"), 1.0, A.min)
    bk = bank()
    mm([(S(bk, 128 * t + 64 * xy, 128 * t + 64 * xy + 64),
         [(RB[8 * xy, h], S("PW", 256 * h + 3 - t, 256 * h + 256, 4)) for h in range(2)]) for t in range(3) for xy in range(2)])
    mv(S("PVL"), S(bk, 0, 384))
    bk = bank()
    mm([(S(bk, 128 * t, 128 * t + 128), [(ILO, blk("vio", t))] + [(m, S("PW", 3 - t, 512, 4)) for m in (RB[0, 1], RB8, NB5)])
        for t in range(2)])
    mv(S("VJ", 0, 256), S(bk, 0, 256))

    def spread(x, scale, slot):
        n = width(x)
        rows = (0, n, 1)
        bk = bank()
        mm([(S(bk, 0, 128, 1, rows), [(x, I)])])
        xt = S("ST", 128 * (slot // 2 % 2), 128 * (slot // 2 % 2) + 128, 1, rows)
        mv(xt, S(bk, 0, 128, 1, rows), scale=scale)

        def make(lo, hi):
            bn = bank(hi - lo)
            mm([(S(bn, 512 * (u - lo), 512 * (u - lo) + 512), [(xt, S("EB", 512 * u, 512 * u + 512, 1, rows))]) for u in range(lo, hi)])
            return S(bn, 0, 512 * (hi - lo))
        return make

    def units(a, b, wide):
        return [(a, b)] if wide else [(B, B + 1) for B in range(a, b)]
    tag[0] = "pos"
    for chunks, _, _ in GROUPS[0]:
        a, b = chunks[0], chunks[-1] + 1
        gather(S("PG", 512 * a, 512 * b), IND(S("PW"), S("Lo", 32 * a, 32 * b)))
    bk = bank()
    mm([(S(bk), [(GSC[8 + k], S("PG", k, 4096, 8)) for k in range(8)])])
    tt(S("LT", 0, 512), S(bk), S("LT", 0, 512), A.add)
    for chunks, _, _ in GROUPS[0]:
        a, b = chunks[0], chunks[-1] + 1
        for lo, hi in units(a, b, OPT["wide"] & 1):
            for xy, nm, m in ((1, "DYT", NB8), (0, "DXT", NB0)):
                bk = bank(hi - lo)
                mm([(S(bk, 128 * u, 128 * u + 128), [(OX[xy][u % 4], blk("PT", lo + u // 4)), (blk("PG", 4 * lo + u), m)])
                    for u in range(4 * (hi - lo))])
                mv(S(nm, 512 * lo, 512 * hi), S(bk, 0, 512 * (hi - lo)))
        for xy, nm in enumerate(("DXT", "DYT")):
            act(S("sq", 256 * xy + 32 * a, 256 * xy + 32 * b), S(nm, 512 * a, 512 * b, 16), F.Square, scale=8.0)
        tt(S("tc", 32 * a, 32 * b), S("sq", 32 * a, 32 * b), S("sq", 256 + 32 * a, 256 + 32 * b), A.add)
        mk = spread(S("tc", 32 * a, 32 * b), -1.0, a)
        for lo, hi in units(a, b, OPT["wide"] & 1):
            mv(S("NT", 512 * lo, 512 * hi), mk(lo - a, hi - a))
    for xy, nm in enumerate(("DXT", "DYT")):
        mv(blk("dc", xy, 256), S(nm, 0, 4096, 16), scale=-1.0 / 32)
    dmas("s", [(S("DD", 512 * u, 512 * u + 512, 1, (8 * u, 8 * u + 8, 1)), S("dc", 0, 512, 1, (8 * u, 8 * u + 8, 1)))
               for u in range(16)], [S("dc")], [S("DD")], 1.0)

    def reg(bk, k, w=128):
        return S(bk, w * k, w * k + w)

    def rows(t):
        bk = bank()
        mm([(S(bk, 0, 64), [(m, S("LT", 256 * h + 3 - t, 256 * h + 256, 4)) for h, m in enumerate((SH0, SH1))])])
        return S(bk, 0, 64)

    def named(t, buf):
        gather(S(buf), IND(S("LT", 0, 520), S("O1")))
        bk = bank()
        mm([(S(bk, 0, 64), [(S("G8", 144 * ((r + t) % 8) + 15 - r, 144 * ((r + t) % 8) + 143 - r), S(buf, r, 1024, 16))
                            for r in range(16)])])
        return S(bk, 0, 64)

    def candidates(t):
        rho = 3 - t
        bk = rows(t)
        ts(S("O1"), bk, 512.0, A.min)
        if t == 0 or not OPT["early"]:
            mv(S("UL"), bk)
        cp(S("CI"), named(t, "G1"))
        ts(S("ib"), S("CI"), 1023, A.bitwise_and)
        ts(S("O2"), S("ib"), 511.0, A.min)
        cp(S("CL"), S("ib"))
        for xy in range(2):
            ts(blk("ia", xy, 64), S("CI"), 10 + 3 * xy, A.arith_shift_right, 7, A.bitwise_and)
        tt(S("dL", 0, 128), S("ia"), blk("PVL", t), A.subtract)
        act(S("sqL"), S("dL", 0, 128), F.Square, scale=8.0)
        tt(blk("dL", 2, 64), blk("sqL", 0, 64), blk("sqL", 1, 64), A.add)
        ts(S("ic"), S("CI"), 3, A.bitwise_and)
        ts(blk("FB", 0, 64), S("ic"), float(rho), A.is_equal)
        over(blk("FB", 1, 64), S("CL"), 511.0)
        for h in range(2):
            for xy, nm in ((1, "CDY"), (0, "CDX")):
                bk = bank()
                mm([(reg(bk, k, 64), [(BR[8 * h + k], blk("dL", xy, 64))]) for k in range(8)])
                mv(blk(nm, h, 512), S(bk))

    def step1(t):
        rho = 3 - t
        act_ = lambda nm: S(nm, rho, 512, 4)
        for xy, nm in enumerate(("XW", "YW")):
            gmv(blk("xa", xy), act_(nm), 1)
        over(blk("ef", 0), act_("LT"), 895.0)
        bk = bank()
        mm([(reg(bk, 0), [(BO8, blk("ef", 0))])])
        over(S("hn"), reg(bk, 0), -1.0, -1.0)
        if t and OPT["early"]:
            mv(S("UL"), rows(t))
            over(blk("FB", 2, 64), S("UL"), 511.0)
            over(blk("FB", 3, 64), named(t, "G2"), 896.0 * 1024)
        bk = bank()
        mm([(reg(bk, m, 64), [(NI, S("CL")), (blk("HBR", m), S("UL"))]) for m in range(8)])
        ts(S("EQ"), S(bk), 0.0, A.is_equal)
        gather(S("cgy"), IND(S("YW", 0, 512), S("O2")))
        gather(S("cgx"), IND(S("XW", 0, 512), S("O2")))
        for lo, hi in units(0, 2, OPT["wide"] & 2):
            H = lambda nm: S(nm, 512 * lo, 512 * hi)
            rs = range(8 * lo, 8 * hi)

            def fill(terms):
                bk = bank(hi - lo)
                mm([(reg(bk, r - 8 * lo, 64), terms(r)) for r in rs])
                return S(bk, 0, 512 * (hi - lo))
            by, bx = (fill(lambda r: [(I, S(nm, r, 1024, 16)), (NI, blk("xa", 2 * xy + r // 8, 64))]) for xy, nm in ((1, "cgy"), (0, "cgx")))
            tt(H("cb"), by, H("CDY"), A.mult)
            tt(H("PX"), bx, H("CDX"), A.mult)
            dma("g", H("PX"), H("cb"), acc=True)
            act(H("cb"), H("PX"), F.Abs)
            tt(H("csg"), fill(lambda r: [(BR[r], blk("dL", 2, 64))]), H("cb"), A.is_lt)
        bk = bank()
        mm([(S(bk, 0, 64), [(I, S("CL"))] + [(IBn, blk("EQ", m, 64)) for m in range(8)] + [(IBn, blk("FB", m, 64)) for m in range(4 if t and OPT["early"] else 2)]
             + [(GSK[r], blk("csg", r, 64)) for r in range(16)])])
        mv(blk("KY", 0, 64), S(bk, 0, 64), bias=keyc)
        for n, m in enumerate((RT1, RT2, RT4)):
            bk = bank()
            mm([(S(bk, 0, 64), [(m, blk("KY", n, 64))])])
            tt(blk("KY", n + 1, 64), S(bk, 0, 64), blk("KY", n, 64), A.max)
        bk = bank()
        mm([(reg(bk, h, 64), [((BF0, BF8)[h], blk("KY", 3, 64)), (IBn, blk("hn", h, 64))]) for h in range(2)])
        cp(S("BI"), reg(bk, 0))
        ts(S("t1"), reg(bk, 0), 0.0, A.is_lt, 1024.0, A.mult)
        ts(S("BJ"), S("BI"), 511, A.bitwise_and)
        cp(S("c16"), S("BJ"))
        bk = bank()
        mm([(S(bk, 0, 8), [(GS16[r], S("c16", r, 128, 16)) for r in range(16)])])
        O3 = blk("O3", t, 8)
        cp(O3, S(bk, 0, 8))
        mv(blk("cf", 0, 8), S(bk, 0, 8))
        tt(S("C16"), S("c16"), S("t1"), A.add)
        mv(S("Cn"), S("C16"), scale=-1.0)
        for h in range(2):
            bk = bank()
            mm([(reg(bk, k % 4), [(S("C16"), blk("PGm", k)), (blk("PGm", k), S("Cn"))]) for k in range(4 * h, 4 * h + 4)])
            tt(blk("eq2", h, 512), S(bk), S("TRc"), A.is_equal)
        mv(S("LTc"), IND(S("LT", 0, 512), O3))
        over(blk("ef", 1), S("LTc"), 895.0)
        bk = bank()
        mm([(reg(bk, 0), [(BO8, blk("ef", 1)), (NI, S("t1"))] + [(S("CM", 112 - 16 * k, 240 - 16 * k), blk("eq2", k)) for k in range(8)])])
        ts(S("DN"), reg(bk, 0), 0.5, A.is_lt)
        if t < 2:
            ts(blk("AL", t), reg(bk, 0), 0.5, A.is_ge)
        bk = bank()
        mm([(S(bk, 0, 8), [(GS16[r], S("DN", r, 128, 16)) for r in range(16)])])
        tt(blk("cf", 2, 8), S(bk, 0, 8), S("dum"), A.mult)
        tt(blk("cf", 3, 8), blk("cf", 2, 8), blk("cf", 0, 8), A.max)
        cp(blk("Oc", t, 8), blk("cf", 3, 8))
        ts(blk("Oxy", 2 * t, 8), blk("cf", 3, 8), 2.0, A.mult)
        ts(blk("Oxy", 2 * t + 1, 8), blk("cf", 3, 8), 2.0, A.mult, 1.0, A.add)
        mv(S("EP"), IND(S("PW", 0, 512), O3))
        mv(blk("EWC", t), IND(S("WW", 0, 512), O3))
        bk = bank()
        mm([(reg(bk, xy), [(BR[8 * xy], S("EP")), ((NB0, NB8)[xy], act_("PW"))]) for xy in range(2)])
        mv(blk("ED", t, 256), S(bk, 0, 256))
        act(blk("ES", t, 256), S(bk, 0, 256), F.Square, scale=8.0)
        if t < 2:
            bk = bank()
            mm([(reg(bk, u), [(I, blk("ef", u)), (TRI, blk("ef", u)), (IBn, S("DN"))]) for u in range(2)])
            relu(blk("FE", t, 256), S(bk, 0, 256))
            bk = bank()
            mm([(reg(bk, 0), [(ILO, S("c16"))] + [(m, S("EP")) for m in (RB[0, 1], RB8, NB5)])])
            tt(blk("NV", 0), reg(bk, 0), blk("FE", 2 * t), A.mult)
            tt(blk("NV", 1), blk("FE", 2 * t + 1), blk("VJ", t), A.mult)
            bk = bank()
            mm([(reg(bk, u), [(I, blk("NV", u)), (I32, x)]) for u, x in enumerate((act_("LT"), S("LTc")))])
            mv(blk("NC", 1), reg(bk, 1))
            cp(IND(S("LT"), blk("Oc", t, 8)), blk("NC", 1))
            mv(act_("LT"), reg(bk, 0))

    def extra(s0, s1, t):
        ss = range(s0, s1)
        n = 128 * len(ss)
        for xy, nm in enumerate(("XW", "YW")):
            mv(S("eg", 256 * xy, 256 * xy + n), IND(S(nm, 0, 512), S("O3", 8 * s0, 8 * s1)))
        bk = bank()
        mm([(reg(bk, 2 * u + xy), [(I, blk("eg", 2 * xy + u)), (NI, blk("xa", xy)) if s == t else (NI32, S(nm, 3 - s, 512, 4))])
            for u, s in enumerate(ss) for xy, nm in enumerate(("XW", "YW"))])
        tt(S("EA", 0, 2 * n), S(bk, 0, 2 * n), S("ED", 256 * s0, 256 * s1), A.mult)
        bz = bank()
        mm([(reg(bz, u), [(I32, blk("EA", 2 * u)), (I32, blk("EA", 2 * u + 1))] + ([(I, blk("EQq", s))] if s < t else []))
            for u, s in enumerate(ss)])
        act(S("eab", 0, n), S(bz, 0, n), F.Abs)
        act(S(bz, 0, n), S(bz, 0, n), F.Sign)
        bk = bank()
        mm([(reg(bk, u), [(I32, blk("eab", u)), (NI, blk("ES", 2 * s)), (NI, blk("ES", 2 * s + 1))]
             + ([(IBn, S("DN"))] if s == t else [])) for u, s in enumerate(ss)])
        em = S("EM", 384 * t + 128 * s0, 384 * t + 128 * s1)
        al = S("AL", 128 * s0, 128 * s1)
        if s0 == t:
            ts(em, S(bk, 0, n), 0.0, A.max, 1023.0, A.min)
        else:
            ts(S("em", 0, n), S(bk, 0, n), 0.0, A.max, 1023.0, A.min)
            nonzero(S("enz", 0, n), S("em", 0, n))
            bk = bank()
            mm([(S(bk, 0, n), [(BO, S("enz", 0, n)), (I32x, al)])])
            ts(al, S(bk, 0, n), 35.5, A.is_ge)
            tt(em, S("em", 0, n), al, A.mult)
        tt(S("EQq", 128 * s0, 128 * s1), S(bz, 0, n), em, A.mult)
        bk = bank()
        mm([(reg(bk, 2 * u + xy), [(I, blk("EQq", s))]) for u, s in enumerate(ss) for xy in range(2)])
        tt(S("EA", 0, 2 * n), S(bk, 0, 2 * n), S("ED", 256 * s0, 256 * s1), A.mult)
        for u, s in enumerate(ss):
            o = 2 * ZC * s
            for xy in range(2):
                gmv(S("Z2", o + 2 * (3 - s) + xy, o + 1024, 8), blk("EA", 2 * u + xy), 1)
            ts(IND(S("Z2", o, o + 2 * ZC), blk("Oxy", s, 16)), blk("EA", u, 256), -1.0, A.mult, 0.0, A.add)
        if t == 2:
            bk = bank()
            mm([(reg(bk, u), [(I, blk("EM", 3 * r + s)) for r in range(s, 3)]) for u, s in enumerate(ss)])
            mv(S("EMs", 128 * s0, 128 * s1), S(bk, 0, n))
            for u, s in enumerate(ss):
                o = ZC * s
                tt(S("ZW", o + 3 - s, o + 512, 4), reg(bk, u), blk("EWC", s), A.mult)
                tt(IND(S("ZW", o, o + ZC), blk("Oc", s, 8)), blk("EMs", s), S("WW", 3 - s, 512, 4), A.mult)
        if s0 == 0 and t == 1:
            bk = bank()
            mm([(reg(bk, u), [(I896, blk("FE", u)), (N896, blk("AL", 0))]) for u in range(2)])
            tt(S("LT", 3, 512, 4), reg(bk, 0), S("LT", 3, 512, 4), A.max)
            mv(blk("NC", 0), IND(S("LT"), blk("Oc", 0, 8)))
            tt(blk("NC", 1), reg(bk, 1), blk("NC", 0), A.max)
            cp(IND(S("LT"), blk("Oc", 0, 8)), blk("NC", 1))

    def kept(t, B):
        return B >= 4 and GROUPS[t][B // 2][1] < 2

    def group(t, chunks, dma1, wide, acc, wb):
        a, b = chunks[0], chunks[-1] + 1
        def R(nm, lo=a, hi=b):
            o = (8 * t + lo) % (_B[nm][0] // 512)
            return S(nm, 512 * o, 512 * (o + hi - lo))
        C = lambda nm, B: blk(nm, B, 512)
        gather(R("gy"), IND(S("YW"), S("Lo", 32 * a, 32 * b)))
        gather(R("gx"), IND(S("XW"), S("Lo", 32 * a, 32 * b)))
        W = lambda nm, lo, hi: S(nm, 512 * lo, 512 * hi)
        both = t and dma1 == 2
        for lo, hi in units(a, b, wide & 1):
            bks = []
            for xy, nm in ((1, "gy"), (0, "gx")):
                bks.append(S(bank(hi - lo), 0, 512 * (hi - lo)))
                g_ = R(nm, lo, hi)
                for B in range(lo, hi):
                    o = 4 * (B - lo)
                    mm([(reg(bks[-1][1], o + j), [(OX[xy][j], blk("UT", B)), (sub(g_, 128 * (o + j), 128 * (o + j) + 128), NI)])
                        for j in range(4)])
            tt(R("PB", lo, hi), bks[0], W("DYT", lo, hi), A.mult)
            more = [] if both else ([] if dma1 else [R("PB", lo, hi)]) + ([R("Q16", lo, hi) if kept(t, lo) else W("ZB", lo, hi)] if t else [])
            tt(bks[1] if more else R("PX" if both else "ZB", lo, hi), bks[1], W("DXT", lo, hi), A.mult)
            for m, x in enumerate(more):
                tt(bks[1] if m + 1 < len(more) else R("ZB", lo, hi), bks[1], x, A.add)
        if dma1:
            dma("g", R("ZB"), R("PB"), acc=True)
        if both:
            dma("g", R("ZB"), R("PX"), acc=True)
        yield
        ab = "AB" if a < 4 else "PB"
        act(R(ab), R("ZB"), F.Abs)
        dma("g", R(ab), W("NT", a, b), acc=True)
        relu(R("R0"), R(ab))
        nz = R("gx" if a < 4 else "gy")
        nonzero(nz, R("R0"))
        n = 32 * len(chunks)
        bk = bank()
        was, now = (S("SS", 256 * u + 32 * a, 256 * u + 32 * b) for u in (t, t + 1))
        mm([(S(bk, 0, n), ([(I32x, was)] if t else []) + [(I, sub(nz, i, 16 * n, 16)) for i in range(16)])])
        stay = ts(now, S(bk, 0, n), 35.5 if t else 3.5, A.is_ge)
        mk = spread(now, 1023.0, a)
        for lo, hi in units(a, b, wide & 2):
            r = R("R0", lo, hi) if t else W("RR", lo, hi)
            tt(r, mk(lo - a, hi - a), R("R0", lo, hi), A.min)
            bk = S(bank(hi - lo), 0, 512 * (hi - lo))
            add([a_act(bk, R("ZB", lo, hi), F.Sign)], [R("ZB", lo, hi)], [bk], after=[stay])
            tt(R("Q16", lo, hi), bk, r, A.mult)
        for B in chunks:
            r = R("R0", B, B + 1)
            q = R("Q16", B, B + 1)
            if B % 4 == 0:
                h = B // 4
                acc.append(bank())
                mm([(S(acc[h]), [(I, blk("UT", h, 512)), (I, S("eps"))])], stop=False, after=[stay])
                mm([(reg(acc[h], u), [(blk("LD2", 4 * h + u), Ith)]) for u in range(4)], start=False, stop=False)
            o = 128 * (B % 4)
            mm([(S(acc[B // 4], o + 16 * g, o + 16 * g + 16, 1, (32 * j, 32 * j + 32, 1)),
                 [(S("DD", 32 * B + 8 * j + g, 8192, 256), sub(q, 128 * j + 16 * g, 128 * j + 16 * g + 16))])
                for j in range(4) for g in range(8)], start=False, stop=False)
            if t < 2 and not kept(t + 1, B):
                gmv(C("ZB", B), q)
            if t == 1 and B == b - 1:
                dma("g", S("RR", 512 * a, 512 * b), R("R0"), acc=True, lat=DLAT)
            if t == 2:
                bk = bank()
                mm([(reg(bk, j), [(blk("RR", 4 * B + j), I), (sub(r, 128 * j, 128 * j + 128), I)]) for j in range(4)])
                pp = blk("PP", B % 2, 512)
                gather(pp, IND(S("WW"), blk("Lo", B, 32)))
                if B in OPT["scan"]:
                    tt(S(bk), S(bk), pp, A.mult)
                    add([("v", "scan", (pp, S("run"), S(bk), 0.0, A.mult, A.add), {}, vcost(pp, [S(bk)], False))],
                        [S("run"), S(bk)], [pp])
                    w = sub(pp, 7, 512, 8)
                else:
                    tt(pp, S(bk), pp, A.mult)
                    bk = bank()
                    w = S(bk, 0, 64)
                    mm([(w, [(I32, sub(pp, k, 512, 8)) for k in range(8)])])
                if B < 4:
                    mv(blk("wout", B, 64), w)
                else:
                    tt(blk("wout", B, 64), w, S("ZW", 2 * ZC + 64 * B, 2 * ZC + 64 * B + 64), A.add)
                if B == 3:
                    dma("g", ("yw", 0, 256), blk("wout", 0, 256), acc=True, after=wb)
                if B == 7:
                    dma("s", ("yw", 256, 512), blk("wout", 1, 256))

    def update(t, h, acc):
        for s in ZSUM[t]:
            o = 2 * ZC * s + 512 * h
            mm([(reg(acc[h], u), [(S("Z2", o + 128 * u, o + 128 * u + 128), I32th)]) for u in range(4)], start=False, stop=False)
        mm([(S(acc[h]), [(IM, S("eps")), (NIM, S("eps"))])], start=False)
        ts(blk("UT", h, 512), S(acc[h]), -1023.0, A.max, 1023.0, A.min)
        for xy, nm in enumerate(("XW", "YW")):
            bk = bank()
            mm([(reg(bk, u, 64), [(blk("UT", 4 * h + u), sub(I, xy, 128, 2))]) for u in range(4)])
            mv(blk(nm, h, 256), S(bk, 0, 256))
            if t == 2:
                dma("sa"[xy], ("y" + "xy"[xy], 256 * h, 256 * h + 256), blk(nm, h, 256))

    for t in range(3):
        tag[0] = "s1_%d" % t
        if t == 0 or not OPT["early"]:
            candidates(t)
        step1(t)
        tag[0] = "ex_%d" % t
        z2 = lambda s: S("Z2", 2 * ZC * s, 2 * ZC * s + 1024)
        zw = lambda s: S("ZW", ZC * s, ZC * s + 512)
        if t == 2:
            dma("s", z2(1), S("ZW", 0, 1024))
        if t:
            extra(0, t, t)
        if t == 2:
            dma("g", z2(1), z2(0), acc=True, lat=DLAT)
            dma("g", zw(1), zw(0), acc=True, lat=DLAT)
        extra(t, t + 1, t)
        if t:
            dma("g", z2(t), z2(t - 1), acc=True, lat=DLAT)
        if t == 2:
            dma("g", zw(2), zw(1), acc=True, lat=DLAT)
        acc, wb = [], [dma("s", ("yw", 0, 256), sub(zw(2), 0, 256))] if t == 2 else []
        runs = [(chunks, group(t, chunks, dma1, dma2, acc, wb)) for chunks, dma1, dma2 in GROUPS[t]]
        for chunks, run in runs + runs:
            tag[0] = "m%d_%d" % (t, chunks[0])
            next(run, None)
        if t < 2 and OPT["early"]:
            tag[0] = "ca_%d" % (t + 1)
            candidates(t + 1)
        tag[0] = "up_%d" % t
        for h in range(2):
            update(t, h, acc)
        if t < 2:
            border(t + 1, [])
            bk = bank()
            mm([(S(bk, u, 256, 8, (32 * m, 32 * m + 32, 1)),
                 [(S("WV", 32 * u + 16 - 16 * g, 32 * u + 48 - 16 * g), S("SS", 256 * t + 256 + 2 * m + g, 256 * t + 512, 8))
                  for g in range(2)]) for u in range(8) for m in range(4)])
            mv(blk("ND", t, 256), S(bk, 0, 256))
            bk = bank()
            mm([(S(bk, h, 512, 2), [(blk("HB", h), blk("ND", 0, 256) if t else S("AI")), (blk("HB", 2 + h), blk("ND", t, 256))])
                for h in range(2)])
            tt(S("LT", 0, 512), S(bk), S("LT", 0, 512), A.max)
    return ops


def depend(ops):
    is_mm = lambda o: o["alts"][0][1] == "mm"
    summand = lambda o: is_mm(o) and not o["alts"][0][2][1] and not o["alts"][0][2][2]
    hist, deps, users = {}, [], {}
    for i, o in enumerate(ops):
        d = dict((j, True) for j in o["after"])
        acc = [(x, False) for x in o["rd"]] + [(x, True) for x in o["wr"]]
        for x, w in acc:
            nm = x[1]
            ps = nm[0] == "@"
            for (j, a, b, wj, pj) in hist.get(nm, ()):
                if j == i:
                    continue
                if ps:
                    if not (summand(o) and summand(ops[j])):
                        d[j] = d.get(j, False) or not (is_mm(o) and is_mm(ops[j]))
                elif b > x[2] and x[3] > a and (w or wj) and not (pj and x[5] and pj != x[5] and pj[2] == 16):
                    d[j] = True
            if ps:
                users.setdefault(nm, set()).add(i)
        for x, w in acc:
            h = hist.setdefault(x[1], [])
            if w and x[4] == 1 and x[5] is None and x[1][0] != "@":
                h[:] = [e for e in h if not (x[2] <= e[1] and e[2] <= x[3])]
            h.append((i, x[2], x[3], w, x[5]))
        deps.append(d)
    return deps, users


def schedule(ops, tries, seed):
    n = len(ops)
    deps, users = depend(ops)
    alts = [o["alts"] for o in ops]
    lat = [o["lat"] for o in ops]
    move = [o["move"] for o in ops]
    succ = [[] for _ in range(n)]
    for i in range(n):
        for j in deps[i]:
            succ[j].append((i, HOP if deps[i][j] else 0.0))
    first = dict((min(u), nm) for nm, u in users.items())
    banks = [sorted(set(x[1] for x in o["rd"] + o["wr"] if x[1][0] == "@")) for o in ops]

    def place(pr, pick, old=None, moved=()):
        if old is None:
            left = dict((nm, len(u)) for nm, u in users.items())
            waiting = sorted(first, reverse=True)
            last, phys, held = {}, {}, {}
            free = dict((b, (0.0, None)) for b in range(8))
            fin, est, since = [0.0] * n, [0.0] * n, [0] * n
            cnt = [len(d) for d in deps]
            efree = dict((e, 0.0) for e in "tvagsrd")
            open_ = [i for i in range(n) if cnt[i] == 0]
            order, marks = [], []
        else:
            k = min(old[6][i] for i in moved) // 50
            marks = old[5][:k]
            left, waiting, last, phys, held, free, fin, est, since, cnt, efree, open_ = [x.copy() for x in old[5][k]]
            order = old[1][:50 * k]
        ready = dict((e, []) for e in "tvagsr")
        place_of = {}
        for i in open_:
            ready[alts[i][pick[i]][0]].append(i)
        for step in range(len(order), n):
            if step % 50 == 0:
                marks.append([x.copy() for x in (left, waiting, last, phys, held, free, fin, est, since, cnt, efree)]
                             + [sorted(i for L in ready.values() for i in L)])
            pairs = sorted((max(free[b][0], free[b + 1][0]), b) for b in free if b % 2 == 0 and b + 1 in free)
            alone = sorted((free[b][0], b) for b in free if b ^ 1 not in free)
            halves = sorted((free[b][0], b) for b in free if b ^ 1 in free)
            while waiting and waiting[-1] in held:
                waiting.pop()
            best = None
            for e, L in ready.items():
                ef = efree[e]
                c = []
                for i in L:
                    s = est[i]
                    if i in first:
                        two = first[i][1] == "D"
                        if i != waiting[-1] and len(free) < RES + two:
                            continue
                        got = pairs if two else alone
                        if not two and halves and not (got and got[0][0] <= max(s, ef, halves[0][0])):
                            got = halves
                        if not got:
                            continue
                        place_of[i] = got[0][1]
                        if got[0][0] > s:
                            s = got[0][0]
                    c.append((s if s > ef else ef, i))
                if c:
                    m = min(c)[0]
                    if best is None or m < best[0]:
                        best = (m, e, c)
            if best is None:
                return None
            m, e, c = best
            s, i = max((x for x in c if x[0] <= m + 0.05), key=lambda x: pr[x[1]])
            if i in first:
                b = phys[first[i]] = place_of[i]
                held[i] = [free.pop(k)[1] for k in range(b, b + 1 + (first[i][1] == "D"))]
            efree[e] = s + alts[i][pick[i]][4]
            f = efree[e]
            if move[i]:
                f = efree["d"] = max(f, efree["d"]) + move[i]
            f = fin[i] = f + lat[i]
            order.append(i)
            ready[e].remove(i)
            for nm in banks[i]:
                left[nm] -= 1
                last[nm] = max(last.get(nm, 0.0), f)
                if left[nm] == 0:
                    for k in range(phys[nm], phys[nm] + 1 + (nm[1] == "D")):
                        free[k] = (last[nm] + HOP, nm)
            for j, h in succ[i]:
                if est[j] < f + h:
                    est[j] = f + h
                cnt[j] -= 1
                if cnt[j] == 0:
                    ready[alts[j][pick[j]][0]].append(j)
                    since[j] = step
        return max(fin), order, phys, fin, held, marks, since

    def chain(cur, pick):
        order, fin = cur[1], cur[3]
        prev, last = {}, {}
        for i in order:
            e = alts[i][pick[i]][0]
            prev[i] = last.get(e)
            last[e] = i
        i = max(order, key=lambda k: fin[k])
        out = []
        while i is not None:
            out.append(i)
            c = [(fin[j], j) for j in deps[i]]
            if prev[i] is not None:
                c.append((fin[prev[i]] - lat[prev[i]] - move[prev[i]], prev[i]))
            i = max(c)[1] if c else None
        return out

    pr = [0.0] * n
    for i in range(n - 1, -1, -1):
        pr[i] = alts[i][0][4] + lat[i] + move[i] + max([pr[j] + h for j, h in succ[i]] + [0.0])
    sends = [i for i in range(n) if alts[i][0][1] == "send" and ops[i]["tag"] != "setup"]
    worth = lambda c: c[0] + MILE * sum(c[3][i] for i in sends)
    pick = [0] * n
    rng = np.random.default_rng(seed)
    cur = place(pr, pick)
    ch = chain(cur, pick)
    best = (cur, pick)
    for it in range(tries):
        q, p = pr, pick
        L = ch if rng.random() < 0.8 else range(n)
        if rng.random() < 0.45:
            L = [i for i in L if len(alts[i]) > 1]
            p = list(pick)
            a = int(rng.integers(0, len(L) + 1))
            moved = L[a:a + int(rng.integers(1, 3))]
            for i in moved:
                p[i] = (p[i] + 1 + int(rng.integers(0, len(alts[i]) - 1))) % len(alts[i])
        else:
            q = list(pr)
            a = L[int(rng.integers(0, len(L)))]
            d = float(rng.normal()) * 3.0
            w = int(rng.integers(0, 10))
            moved = range(max(0, a - w), min(n, a + w + 1))
            for i in moved:
                q[i] += d
        if not moved:
            continue
        new = place(q, p, cur, moved)
        if new is not None and worth(new) <= worth(cur) + HEAT * (1.0 - it / tries) * rng.random():
            cur, pr, pick = new, q, p
            ch = chain(cur, pick)
            if cur[0] < best[0][0]:
                best = (cur, pick)
    cur, pick = best
    order, phys, fin, held = cur[1:5]
    for i, nms in held.items():
        for nm in nms:
            for j in users.get(nm, ()):
                deps[i][j] = True
    order, pick, fin = polish([(ops, HOP, 1.0)], deps, order, pick, rng, POLISH * tries)
    return order, deps, phys, fin, pick


def plan(starts, tries):
    views = [(build(*c), hop, weight) for c, hop, weight in COSTS]
    ops = views[0][0]
    order, deps, phys, fin, pick = min((schedule(ops, tries, seed) for seed in starts), key=lambda c: max(c[3]))
    rng = np.random.default_rng(0)
    base, users = depend(ops)
    first = dict((min(u), nm) for nm, u in users.items())
    for turn in range(TURNS):
        at = dict((i, k) for k, i in enumerate(order))
        owner, where, more = dict((b, None) for b in range(8)), {}, [dict(d) for d in base]
        for i in order:
            if i in first:
                free = [(max([fin[j] for j in users.get(nm, ())] + [0.0]), b) for b, nm in owner.items()
                        if nm is None or max(at[j] for j in users[nm]) < at[i]]
                b = where[first[i]] = min(free)[1]
                more[i].update((j, True) for j in users.get(owner[b], ()))
                owner[b] = first[i]
        new = polish(views[:1], more, order, pick, rng, 2 * tries)
        if max(new[2]) < max(fin):
            (order, pick, fin), deps, phys = new, more, where
    order, pick, fin = polish(views, deps, order, pick, rng, 40 * tries)
    return ops, order, deps, phys, fin, [o["alts"][k] for o, k in zip(ops, pick)]


def polish(views, deps, order, pick, rng, tries):
    n = len(deps)
    alts = [o["alts"] for o in views[0][0]]
    data = [([o["alts"] for o in ops], [(o["lat"], o["move"]) for o in ops],
             [[(j, hop if w else 0.0) for j, w in d.items()] for d in deps], weight) for ops, hop, weight in views]
    succ = [[] for _ in range(n)]
    for i in range(n):
        for j in deps[i]:
            succ[j].append(i)

    def run(order, pick, bound=1e9):
        total, pairs, first = 0.0, [], None
        for k, (alts, tail, pred, weight) in enumerate(data):
            x, fin, p = one(order, pick, alts, tail, pred)
            total += weight * x
            pairs += p
            first = first or (fin, x)
            if k == 0 and x > bound + 1.0:
                return (1e9,)
        return total, first[0], pairs, first[1]

    def one(order, pick, alts, tail, pred):
        fin, why = [0.0] * n, [None] * n
        efree, last = dict((e, 0.0) for e in "tvagsrd"), {}
        for i in order:
            alt = alts[i][pick[i]]
            e = alt[0]
            s, w = efree[e], (last.get(e), True)
            for j, h in pred[i]:
                if fin[j] + h > s:
                    s, w = fin[j] + h, (j, False)
            f = efree[e] = s + alt[4]
            if tail[i][1]:
                f = efree["d"] = max(f, efree["d"]) + tail[i][1]
            fin[i], why[i], last[e] = f + tail[i][0], w, i
        i = fin.index(max(fin))
        pairs = []
        while why[i][0] is not None:
            if why[i][1]:
                pairs.append((why[i][0], i))
            i = why[i][0]
        return max(fin) + MEAN * sum(fin) / n, fin, pairs

    cur = run(order, pick)
    for _ in range(tries):
        a, b = cur[2][int(rng.integers(0, len(cur[2])))]
        o, p = order, pick
        u = rng.random()
        if u < 0.25:
            i = (a, b)[int(rng.integers(0, 2))]
            if len(alts[i]) < 2:
                continue
            p = list(pick)
            p[i] = (p[i] + 1 + int(rng.integers(0, len(alts[i]) - 1))) % len(alts[i])
        else:
            x, y = order.index(a), order.index(b)
            x = max(0, x - int(rng.integers(0, 12))) if u < 0.5 else x
            y = min(n - 1, y + int(rng.integers(0, 12))) if u > 0.75 else y
            part = order[x:y + 1]
            if u < 0.625:
                take = {b}
                for i in part[::-1]:
                    if any(j in take for j in succ[i]):
                        take.add(i)
                part = [i for i in part if i in take] + [i for i in part if i not in take]
            else:
                take = {a}
                for i in part:
                    if any(j in take for j in deps[i]):
                        take.add(i)
                part = [i for i in part if i not in take] + [i for i in part if i in take]
            o = order[:x] + part + order[y + 1:]
        new = run(o, p, cur[3])
        if new[0] <= cur[0]:
            cur, order, pick = new, o, p
    return order, pick, cur[1]


PLAN = []


def rank_program(g, core, T, topo):
    rank = T.rank_of(core)
    if rank is None:
        return
    if not PLAN:
        PLAN.append(plan(STARTS, TRIES))
    ops, order, deps, phys, fin, way = PLAN[0]
    N = len(T.cores)
    peers = [T.cores[(rank + d) % N] for d in range(1, N)]
    eng = [e for e in topo.engines(core, peers[0]) if all(e in topo.engines(core, p) for p in peers)]
    queue = {"t": g.tensor, "v": g.vector, "a": g.scalar, "g": g, "s": g.sync}
    call = {"tensor_tensor": g.vector.tensor_tensor, "tensor_scalar": g.vector.tensor_scalar,
            "tensor_copy": g.vector.tensor_copy, "memset": g.vector.memset, "transpose": g.vector.transpose,
            "activation": g.scalar.activation, "iota": g.iota, "scan": g.vector.tensor_tensor_scan, "affine_select": g.affine_select}

    def ap(x):
        if not is_ap(x):
            return x
        if x[0] == "ind":
            return ap(x[1]).indirect(ap(x[2]))
        nm, o = ("P%d" % (phys[x[1]] // 2), phys[x[1]] % 2 * 512) if x[1][0] == "@" else PLACE[x[1]]
        p = slice(None) if x[5] is None else slice(*x[5])
        return T[nm][p, o + x[2]:o + x[3]] if x[4] == 1 else T[nm][p, o + x[2]:o + x[3]:x[4]]

    def side(x):
        if is_ap(x):
            return ap(x)
        return T[x[0]][:, x[1]:x[2]] if isinstance(x, tuple) else T[x][:]

    mark = {}
    clock = {}
    known = dict((e, {}) for e in queue)
    count = dict((e, 0) for e in "tvag")
    total = {}
    sent = 0
    for i in order:
        e, kind, a, kw, _ = way[i]
        if e == "r":
            mark[i] = (a[0], (N - 1) * a[1])
            clock[i] = {mark[i][0]: mark[i][1]}
            total[mark[i][0]] = mark[i][1]
            continue
        q, kn = queue[e], known[e]
        need = sorted((j for j in deps[i] if deps[i][j] and j in mark), key=lambda j: -fin[j])
        for j in need:
            sem, val = mark[j]
            if kn.get(sem, 0) < val:
                val = max(mark[k][1] for k in need if mark[k][0] == sem)
                q.wait_ge(T.sem[sem], val)
                kn[sem] = val
            for s, v in clock[j].items():
                kn[s] = max(kn.get(s, 0), v)
        if kind == "send":
            trs = []
            used = 0
            for src, nm, c0, w, sem, ne in a[0]:
                ids, dsts = [], []
                for d, p in enumerate(peers):
                    rid, pid = topo.addr(p, core)
                    ids.append(DstId(rid=rid, pnc=pid))
                    dsts.append(ap(S(nm, c0 + d * w, c0 + d * w + width(src))))
                trs.append(RemoteDMATransfer(dst_ids=ids, dma_engine_mask=sum(1 << x for x in eng[used:used + ne]),
                                             remote_sem=T.sem[sem], src=ap(src), dsts=dsts))
                used += ne
            g.remote_dma_fused(trs, local_sem=T.sem.ls)
            sent += used
            continue
        if kind == "dma":
            q.dma_start(side(a[0]), side(a[1]), **({"accum_op": A.add} if a[2] else {})).then_inc(T.sem[a[3]], 16)
            mark[i] = (a[3], 16)
            total[a[3]] = 16
        elif kind == "dmas":
            for out, src in a[0]:
                q.dma_start(side(out), side(src)).then_inc(T.sem[a[1]], 16)
            mark[i] = (a[1], 16 * len(a[0]))
            total[a[1]] = mark[i][1]
        else:
            if kind == "mm":
                for out, terms in a[0]:
                    for m, (l, r) in enumerate(terms):
                        ins = q.matmul(ap(out), ap(l), ap(r), a[1] and m == 0, a[2] and m == len(terms) - 1)
            else:
                ins = call[kind](*[ap(x) for x in a], **dict((k, ap(v)) for k, v in kw.items()))
            count[e] += 1
            ins.then_inc(T.sem["q" + e], 1)
            mark[i] = ("q" + e, count[e])
            total["q" + e] = count[e]
        clock[i] = dict(kn)
        clock[i][mark[i][0]] = mark[i][1]
    g.wait_ge(T.sem.ls, sent)
    for sem, val in total.items():
        if known["s"].get(sem, 0) < val:
            g.sync.wait_ge(T.sem[sem], val)
